import numpy as np, ml_dtypes
CORES = [5,29,101,125,133,157,229,253]
N = 8
BF = ml_dtypes.bfloat16
T, NC, GY, W, H, HW = 384, 3072, 48, 64, 128, 8192
LZ, ZS, UN, P = 4096, 3, 16, 2
def poses(rng, a, b):
    p = np.zeros((N, 8, 6), np.int64); p[..., 0] = a; p[..., 1] = b
    p[..., 2] = rng.integers(-4000, 4001, (N, 8)) - (256 * a + 4 * GY * b)
    p[..., 3] = rng.integers(-4000, 4001, (N, 8)) + 16384 - (4 * GY * a - 256 * b)
    p[..., 4] = rng.integers(-5 * H, 5 * H + 1, (N, 8)); p[..., 5] = rng.integers(LZ // 16, LZ // 3, (N, 8))
    return p.astype(np.int32)
def image(v):
    return v.astype(np.float32).astype(BF)
def setup_inputs(rng):
    w = rng.random((N, 1)) * 2 * np.pi; j = rng.integers(-2, 3, (2, N, 8))
    a = np.clip(np.rint(64 * np.cos(w)).astype(np.int64) + j[0], -64, 64); b = np.clip(np.rint(64 * np.sin(w)).astype(np.int64) + j[1], -64, 64)
    v = rng.integers(-31, 32, (N, 16, HW)); v[:, :2] = rng.integers(-12, 13, (N, 2, HW)); v[:, 15] = rng.integers(0, 256, (N, HW))
    return {"cam": image(v), "lens": rng.integers(0, 1024, (N, 8, LZ)).astype(np.int32), "pose": poses(rng, a, b)}
def setup_inputs_ends(rng):
    d = setup_inputs(rng); p = d["pose"]; e = d["lens"]; top = 32768 - 512 * (GY - 1)
    p[..., 0] = 64; p[..., 1] = 0; p[..., 2] = rng.integers(-2000, 2001, (N, 8)) - 16384; p[..., 5] = LZ
    p[..., 3] = rng.permuted(np.tile(np.array([0, -1, top - 1, top]), (N, 2, 1)), axis=2).reshape(N, 8)
    e[:] = np.where(rng.random(e.shape) < 0.75, e, rng.choice(np.array([0, 1, 4095]), e.shape))
    e[:, :, 0] = rng.integers(1, 256, (N, 8)); e[:, :, LZ - 1] = rng.integers(1, 256, (N, 8)); e[:, 4:] = 1024
    p[:, 4, 4] = -2 * H - 1; p[:, 5, 4] = 2 * H; p[:, 6, 4] = 2 * H - 1; p[:, 7, 4] = -2 * H
    p[:, 6, 2] = 384 - 16384; p[:, 7, 2] = -16384
    return d
def setup_inputs_ties(rng):
    d = setup_inputs(rng); a = 16 * rng.integers(1, 4, (N, 8)) * rng.choice(np.array([-1, 1]), (N, 8)); b = 16 * rng.integers(-2, 3, (N, 8))
    p = poses(rng, a, b); p[..., 3] = p[..., 3] & -128
    p[..., 5] = rng.permuted(np.tile(UN * np.array([0, 1, 32, 64]), (N, 2, 1)), axis=2).reshape(N, 8)
    d["pose"] = p; return d
def setup_inputs_one(rng):
    d = setup_inputs(rng); d["lens"][:, :4] = 0; d["pose"][:, :2, 5] = LZ
    v = d["cam"].astype(np.float32); v[:, :2] = rng.choice(np.array([-31, 31]), (N, 2, HW)); d["cam"] = image(v); return d
def setup_inputs_blind(rng):
    d = setup_inputs(rng); q = rng.permutation(N); p = d["pose"]
    p[q[0], :, 0] = 64; p[q[0], :, 1] = 0; p[q[0], :, 3] = -49152; p[q[1], :, 5] = 0
    v = d["cam"].astype(np.float32); v[q[2], 15] = 0; d["cam"] = image(v); return d
def setup_inputs_spread(rng):
    d = setup_inputs(rng); p = d["pose"]
    v = rng.integers(-31, 32, (N, 16, HW)); v = np.sign(v) * (np.abs(v) >> rng.integers(0, 6, (N, 1, HW))); v[:, 15] = rng.integers(0, 256, (N, HW)) >> rng.integers(0, 3, (N, HW))
    d["cam"] = image(v); d["lens"] = (rng.integers(0, 4096, (N, 8, LZ)) >> rng.integers(0, 8, (N, 8, LZ))).astype(np.int32)
    y = rng.integers(-4095, 4096, (N, 8)); p[..., 4] = np.sign(y) * (np.abs(y) >> rng.integers(0, 8, (N, 8)))
    p[..., 5] = rng.integers(LZ // 4, LZ + 1, (N, 8)) >> rng.integers(0, 6, (N, 8)); return d
def check_inputs(d):
    bad = []; c = d["cam"].astype(np.float32); p = d["pose"].astype(np.int64); e = d["lens"]
    if not (np.isfinite(c).all() and (c == np.floor(c)).all()): bad.append("whole numbers in cam")
    if not (np.abs(c[:, :15]) <= 31).all(): bad.append("features")
    if not ((c[:, 15] >= 0) & (c[:, 15] <= 255)).all(): bad.append("depth")
    if not ((e >= 0) & (e <= 4095)).all(): bad.append("lens")
    if not (np.abs(p[..., 0:2]) <= 64).all(): bad.append("turning numbers")
    if not (np.abs(p[..., 2:4]) <= 49152).all(): bad.append("offsets")
    if not (np.abs(p[..., 4]) <= 4095).all(): bad.append("height")
    if not ((p[..., 5] >= 0) & (p[..., 5] <= LZ)).all(): bad.append("tolerance")
    return bad
def reference(cam, lens, pose):
    c = np.arange(NC); sx = np.zeros(NC, np.int64); sy = np.zeros(NC, np.int64)
    im = np.concatenate([cam.astype(np.float32), np.zeros((N, 16, 1), np.float32)], 2).astype(np.int64)
    for k in range(P):
        gx = 8 * (c & 63) + sx; gy = 8 * (c >> 6) + sy; s = np.zeros((16, NC), np.int64)
        for r in range(N):
            for g in range(8):
                a, b, tx, tz, h, tol = [int(v) for v in pose[r, g]]
                x = (a * gx + b * gy + tx) >> 5; z = (a * gy - b * gx + tz) >> ZS
                near = (z >= 0) & (z < LZ); m = lens[r, g][np.where(near, z, 0)].astype(np.int64)
                u = ((x * m) >> 12) + W // 2; v = ((h * m) >> 12) + H // 2
                seen = near & (u >= 0) & (u < W) & (v >= 0) & (v < H)
                t = im[r][:, np.where(seen, W * v + u, HW)]
                s += t * (np.abs(UN * t[15] - z) <= tol)
        sx = np.minimum(np.maximum(s[0], -31), 31); sy = np.minimum(np.maximum(s[1], -31), 31)
    y = np.ascontiguousarray(s.reshape(16, N, T).transpose(1, 0, 2)).astype(np.float32)
    return {"y": y}

@@ -1,0 +1,588 @@
+import numpy as np
+from concourse.bass import DstId, RemoteDMATransfer
+from concourse.mybir import AluOpType as A, ActivationFunctionType as F
+
+CFG = {"W": [64, 64, 64], "piece": 2, "merge": 2, "delta": 500.0, "early": 3, "lat0": 9000.0, "lat": 5500.0, "gat": 1.62,
+       "pe": 1.04, "bw": 250.0, "tries": 2500}
+CASES = ((1.0, 1.0, 1.0, 1.0, 0.9), (0.7, 0.5, 0.7, 0.7, 0.6), (1.35, 1.0, 1.3, 1.3, 1.5), (1.0, 0.5, 0.8, 1.0, 0.6),
+         (0.85, 1.0, 1.0, 0.7, 1.2))
+FOUND = {}
+SLOT = 32
+B, H, W32, I32 = "bfloat16", "float16", "float32", "int32"
+SCRATCH = {n: ("sbuf", [128, c], d) for n, c, d in (
+    ("img", 8320, B), ("win", 4112, B), ("posei", 8, I32), ("p8", 8, W32), ("pa", 8, W32), ("kc", 24, W32), ("hs", 4, W32),
+    ("lc", 256, I32), ("v0", 256, I32), ("tab", 768, B), ("dj", 32, I32), ("d16f", 16, W32), ("wp", 256, B), ("ones8", 192, W32),
+    ("rep", 128, W32), ("onesb", 128, B), ("ident", 128, B), ("identh", 128, H), ("identg", 128, B), ("diag", 512, B),
+    ("cz", 512, B), ("cx", 512, B), ("pc", 8, I32), ("cf", 16, W32), ("i12", 192, W32), ("s0", 48, B), ("dz", 144, W32),
+    ("zm", 144, W32), ("wl", 144, B), ("wd", 144, B), ("sb1", 16, B), ("sb2", 24, B), ("m8", 192, W32), ("i16b", 192, W32),
+    ("f01", 256, B), ("h01", 384, B), ("h2", 384, W32), ("xb", 192, I32), ("off", 960, "uint16"), ("gb", 15360, B),
+    ("tmp", 192 * 17, W32), ("tmi", 384, I32), ("mt", 384, B), ("ne", 192, B), ("x1", 8 * SLOT * 4, B), ("sh", 48, B),
+    ("sg", 48, H), ("fs", 384, H), ("x2", 384, H), ("rl", 96, H), ("yo", 128, W32))}
+for _b in range(8):
+    SCRATCH["ps%d" % _b] = ("psum", [128, 512], "float32")
+SEMAPHORES = ["cV", "cA", "cP", "cG", "dpose", "dlens", "dimg", "dtab", "dy", "xa0", "xa1", "xa2", "xa3", "fa", "fb", "r0", "r1",
+              "r2", "r3", "s0", "s1", "loc"]
+
+MNEG = -12582912.0
+M32 = 402653184.0
+LAST = 8319.0
+KOFF = -MNEG + 4192.0
+CYC = 1.04
+
+
+def mask_of(engs):
+    m = 0
+    for e in engs:
+        m |= 1 << e
+    return m
+
+
+def helpers(core, T, topo):
+    far = [d for d in T.cores if d != core and not topo.may_write(core, d)]
+    can = [c for c in topo.cores_of(core) if T.rank_of(c) is None and all(topo.may_write(c, d) for d in far)]
+    first = [c for c in can if topo.die(c) == topo.die(core)][0]
+    second = [c for c in can if topo.die(c) != topo.die(core)][0]
+    return far, [first, second]
+
+
+def dst_id(topo, d, s):
+    rid, pid = topo.addr(d, s)
+    return DstId(rid=rid, pnc=pid)
+
+
+def x1_part(T, q, r):
+    c0 = SLOT * (8 * q + r)
+    return T.x1[:, c0:c0 + CFG["W"][q] // 4]
+
+
+def helper_program(g, core, owner, far, i, T, topo):
+    r = T.rank_of(owner)
+    engs = topo.engines(core, far[0])
+    half = len(engs) // 2
+    n_in = len(topo.engines(owner, core)) - len(engs)
+    loc = 0
+    for q in range(len(CFG["W"])):
+        g.wait_ge(T.sem["r%d" % q], n_in)
+        piece = x1_part(T, q, r)
+        g.remote_dma_fused([RemoteDMATransfer(dst_ids=[dst_id(topo, d, core)], dma_engine_mask=mask_of(engs[j * half:(j + 1) * half]),
+                                              remote_sem=T.sem["xa%d" % q], src=piece, dst=piece)
+                            for j, d in enumerate(far[2 * i:2 * i + 2])], local_sem=T.sem.loc)
+        loc += 2 * half
+    for j in range(2):
+        d = far[2 * j + i]
+        g.wait_ge(T.sem["s%d" % j], n_in)
+        rid, pid = topo.addr(d, core)
+        g.remote_dma(T.x2[:, 48 * r:48 * r + 48], T.rl[:, 48 * j:48 * j + 48], T.sem.fb, T.sem.loc, pid, rid, mask_of(engs))
+        loc += len(engs)
+    g.wait_ge(T.sem.loc, loc)
+
+
+def lengths(ops, case):
+    cost = [(o["cost"] - 60) * case[0] + 60 if o["gat"] else o["cost"] * case[1] if o["eng"] == "P" else o["cost"] for o in ops]
+    late = [o["late"] * case[4 if o["bytes"] < 0 else 2] if o["eng"] is None else o["late"] for o in ops]
+    return cost, late, [max(0, o["bytes"]) * case[3] / CFG["bw"] for o in ops]
+
+
+def plan(ops, pre, succ, prio, size):
+    cost, late, load = size
+    n = len(ops)
+    left = [len(p) for p in pre]
+    free, at, eng, order, line = {}, [0.0] * n, [o["eng"] for o in ops], [], 0.0
+    ready = [i for i in range(n) if left[i] == 0]
+    while ready:
+        cand = []
+        for i in ready:
+            for e in (("A", "V") if eng[i] == "VA" else (eng[i],)):
+                cand.append((max(at[i], free.get(e, 0.0)) if e else at[i], -prio[i], e, i))
+        t0, _, e0, i0 = min(cand, key=lambda c: c[:2])
+        if e0 is not None:
+            d = CFG["delta"] if cost[i0] > 400 else 30.0
+            t0, _, e0, i0 = min([c for c in cand if c[2] == e0 and c[0] <= t0 + d], key=lambda c: (c[1], c[0]))
+        eng[i0] = e0
+        t1 = free[e0] = t0 + cost[i0]
+        if load[i0]:
+            line = max(line, t1) + load[i0]
+        fin = (line if load[i0] else t1) + late[i0]
+        order.append(i0)
+        ready.remove(i0)
+        for j, kind in succ[i0]:
+            at[j] = max(at[j], t1 if kind else fin + 60)
+            left[j] -= 1
+            if left[j] == 0:
+                ready.append(j)
+    return order, eng
+
+
+def replay(order, eng, succ, size):
+    cost, late, load = size
+    free, at, line, end = {}, [0.0] * len(eng), 0.0, 0.0
+    for i in order:
+        e = eng[i]
+        t1 = (max(at[i], free.get(e, 0.0)) if e else at[i]) + cost[i]
+        free[e] = t1
+        if load[i]:
+            line = max(line, t1) + load[i]
+        fin = (line if load[i] else t1) + late[i]
+        end = max(end, fin)
+        for j, kind in succ[i]:
+            at[j] = max(at[j], t1 if kind else fin + 60)
+    return end
+
+
+def schedule(ops):
+    n = len(ops)
+    succ = [[] for _ in range(n)]
+    pre = []
+    for i, o in enumerate(ops):
+        pre.append(set(o["deps"]) | set(o["after"]))
+        for j in pre[i]:
+            succ[j].append((i, j not in o["deps"] or (o["eng"] == "P" and ops[j]["eng"] == "P")))
+    sizes = [lengths(ops, c) for c in CASES]
+    base = [0.0] * n
+    for i in range(n - 1, -1, -1):
+        base[i] = sizes[0][0][i] + sizes[0][1][i] + sizes[0][2][i] + 60 + max([base[j] for j, _ in succ[i]] + [0.0])
+
+    def value(bend):
+        order, eng = plan(ops, pre, succ, [b + d for b, d in zip(base, bend)], sizes[0])
+        return sum(replay(order, eng, succ, s) for s in sizes), order, eng
+
+    rng = np.random.RandomState(1)
+    bend = FOUND.get(n, [0.0] * n)
+    best = value(bend)
+    for _ in range(CFG["tries"] if n not in FOUND else 0):
+        other = list(bend)
+        a = int(rng.randint(n))
+        step = float(rng.normal()) * 1500.0
+        for i in range(a, min(n, a + 1 + int(rng.randint(12)))):
+            other[i] += step
+        got = value(other)
+        if got[0] <= best[0]:
+            best, bend = got, other
+    FOUND.setdefault(n, bend)
+    for o, e in zip(ops, best[2]):
+        o["eng"] = e
+    return best[1]
+
+
+def rank_program(g, core, T, topo):
+    rank = T.rank_of(core)
+    if rank is None:
+        for owner in T.cores:
+            if core in topo.cores_of(owner):
+                far, hl = helpers(owner, T, topo)
+                if core in hl:
+                    helper_program(g, core, owner, far, hl.index(core), T, topo)
+        return
+    far, hl = helpers(core, T, topo)
+    near = [d for d in T.cores if d != core and d not in far]
+    out_e = topo.engines(core, near[0])
+    in_e = [e for e in topo.engines(core, hl[0]) if e not in out_e]
+    V, S, P, Y = g.vector, g.scalar, g.tensor, g.sync
+    queue = {"V": V, "A": S, "P": P, "G": g, "Y": Y}
+    ps = [T["ps%d" % b] for b in range(8)]
+    W = CFG["W"]
+    NQ = len(W)
+    C0 = [sum(W[:q]) for q in range(NQ)]
+
+    ops, last_w, readers, last_q = [], {}, {}, {}
+
+    def op(eng, fn, cost, r=(), w=(), bank=None, dma=None, arrive=None, late=0.0, nbytes=0, gat=None):
+        i = len(ops)
+        r, w = list(r), list(w)
+        if bank is not None:
+            (r if eng == "V" else w).append(("bank", bank))
+        deps = set()
+        for x in r:
+            if x in last_w:
+                deps.add(last_w[x])
+        for x in w:
+            if x in last_w:
+                deps.add(last_w[x])
+            deps.update(readers.get(x, []))
+        for x in r:
+            readers.setdefault(x, []).append(i)
+        for x in w:
+            last_w[x] = i
+            readers[x] = []
+        after = []
+        if eng in ("G", "Y"):
+            if eng in last_q:
+                after.append(last_q[eng])
+            last_q[eng] = i
+        ops.append({"eng": eng, "fn": fn, "deps": deps, "dma": dma, "arrive": arrive, "cost": cost, "late": late, "bytes": nbytes,
+                    "after": after, "gat": gat})
+
+    def vc(n):
+        return 60 + max(64, n) * CYC
+
+    def ts(n, out, in0, s1, s2, o0, o1, r, w, bank=None):
+        if o1 is None:
+            op("V", lambda: V.tensor_scalar(out, in0, s1, None, o0), vc(n), r, w, bank)
+        else:
+            op("V", lambda: V.tensor_scalar(out, in0, s1, s2, o0, o1), vc(n), r, w, bank)
+
+    def tt(n, out, a, b, o, r, w, bank=None):
+        op("V", lambda: V.tensor_tensor(out, a, b, o), vc(n if bank is not None else 2 * n), r, w, bank)
+
+    def cp(n, out, a, r, w, bank=None):
+        op("V", lambda: V.tensor_copy(out, a), vc(n), r, w, bank)
+
+    def ms(n, ap, c, w):
+        op("V", lambda: V.memset(ap, c), vc(n // 2), (), w)
+
+    def act(n, out, a, r, w, scale=1.0, bias=0.0, bank=None):
+        op("A", lambda: S.activation(out, a, F.Identity, bias=bias, scale=scale), vc(n), r, w, bank)
+
+    def mms(b, calls, r):
+        op("P", lambda: [P.matmul(*c[1:]) for c in calls][-1], sum(max(64, c[0]) for c in calls) * CFG["pe"], r, (), b)
+
+    def iota(n, out, pat, base, cm, w, fl=True):
+        if fl:
+            op("G", lambda: g.iota(out, pat, base, cm, allow_small_or_imprecise_dtypes=True), 130 + 2 * n * CYC, (), w)
+        else:
+            op("G", lambda: g.iota(out, pat, base, cm), 130 + 2 * n * CYC, (), w)
+
+    def sel(n, out, a, pat, cm, r, w):
+        op("G", lambda: g.affine_select(out, a, pat, A.is_equal, 0.0, 0, cm), 170 + 2 * n * CYC, r, w)
+
+    def dma(eng, nbytes, out, a, sem, r, w):
+        op(eng, lambda: queue[eng].dma_start(out, a), 60, r, w, None, sem, late=1700.0, nbytes=nbytes)
+
+    nt = [0]
+
+    def tmp(n):
+        nt[0] += n
+        return T.tmp[:, nt[0] - n:nt[0]], "t%d" % nt[0]
+
+    IMG = ["img%d" % k for k in range(8)] + ["imgz0", "imgz1"]
+    WIN = ["win0", "win1", "win2"]
+
+    def units(c0, c1):
+        return range(c0 // 8, (c1 + 7) // 8)
+
+    def pieces(u0, u1):
+        return [range(a, min(u1, a + CFG["piece"])) for a in range(u0, u1, CFG["piece"])]
+
+    def offs(st, q):
+        return T.off[:, 192 * st + C0[q]:192 * st + C0[q] + W[q]], [("off", st, u) for u in units(C0[q], C0[q] + W[q])]
+
+    def gb(st, c0, c1, step=1):
+        return T.gb[:, 3072 * st + c0:3072 * st + c1:step] if step > 1 else T.gb[:, 3072 * st + c0:3072 * st + c1]
+
+    def gather_call(eng, st, u0, u1):
+        w = T.win[:, 0:4112] if st in (0, 2) else T.img[:, 0:8320]
+        src = w.indirect(T.off[:, 192 * st + 8 * u0:192 * st + 8 * u1])
+        out = gb(st, 128 * u0, 128 * u1)
+        return V.tensor_copy(out, src) if eng == "V" else S.activation(out, src, F.Identity)
+
+    def gather(st, u0, u1):
+        for us in pieces(u0, u1):
+            op("VA", None, 60 + 128 * len(us) * CFG["gat"], (WIN if st in (0, 2) else IMG) + [("off", st, u) for u in us],
+               [("g", st, u) for u in us], gat=[st, us[0], us[-1] + 1])
+
+    def img_load(k):
+        dma("Y", 262144, T.img[16 * k:16 * k + 16, 64:8256], T.cam[:, :], "dimg", (), ["img%d" % k])
+
+    kc = lambda j: T.kc[:, j:j + 1]
+    loc = [0]
+
+    dma("Y", 192, T.posei[0:8, 0:6], T.pose[:, :], "dpose", (), ["posei"])
+    dma("Y", 131072, T.lc[:, :], T.lens[:, :], "dlens", (), ["lc"])
+    for k in range(CFG["early"]):
+        img_load(k)
+    iota(16, T.dj[:, 0:16], [[1, 16]], 128, -1, ["dj"], False)
+    iota(2, T.pc[:, 0:2], [[16, 2]], 0, 1, ["pc"], False)
+    iota(48, T.i12[:, 0:48], [[0, 12], [16, 4]], 0, 0, ["i1"])
+    iota(192, T.ones8[0:8, :], [[0, 192]], 1, 0, ["ones8"])
+    sel(128, T.rep[0:8, :], T.ones8[0:8, 0:128], [[1, 8], [0, 16]], -1, ["ones8"], ["rep"])
+    for q in range(NQ):
+        iota(W[q] // 4, T.i12[:, 48 + C0[q] // 4:48 + (C0[q] + W[q]) // 4], [[1, W[q] // 16], [0, 4]], C0[q] // 4, 0, [("i2", q)])
+    iota(128, T.onesb[:, :], [[0, 128]], 1, 0, ["onesb"])
+    sel(128, T.ident[:, :], T.onesb[:, :], [[-1, 128]], 1, ["onesb"], ["ident"])
+    iota(144, T.dz[:, :], [[1, 144]], 0, -1, ["dz"])
+    sel(192, T.m8[0:8, :], T.ones8[0:8, :], [[0, 24], [1, 8]], -1, ["ones8"], ["m8"])
+    iota(192, T.i16b[0:8, :], [[16, 24], [0, 8]], 0, 0, ["i16b"])
+    iota(128, T.f01[0:8, 0:128], [[0, 2], [8, 64]], 0, 0, ["f0"])
+    iota(128, T.f01[0:8, 128:256], [[8, 2], [0, 64]], 0, 0, ["f1"])
+
+    ms(256, T.wp[:, :], 0.0, ["wp"])
+    ms(1024, T.win[:, 0:1024], 64.0, ["wina"])
+    ms(1040, T.win[:, 3072:4112], 64.0, ["wind"])
+    act(1024, T.win[:, 1024:2048], T.win[:, 0:1024], ["wina"], ["winb"])
+    act(1024, T.win[:, 2048:3072], T.win[:, 0:1024], ["wina"], ["winc"])
+    ts(16, T.dj[:, 16:32], T.dj[:, 0:16], 15, None, A.bitwise_and, None, ["dj"], ["dj2"])
+    ts(6, T.p8[0:8, 0:6], T.posei[0:8, 0:6], 1.0 / 32, None, A.mult, None, ["posei"], ["p8"])
+    mms(7, [(256, ps[7][:, 0:6], T.rep[0:8, :], T.p8[0:8, 0:6], True, True)], ["rep", "p8"])
+    ts(16, T.wp[:, 112:128], T.dj[:, 16:32], 0.0, None, A.is_equal, None, ["dj2"], ["wp"])
+    ts(256, T.tab[:, 0:256], T.lc[:, :], M32, M32 + 32.0, A.add, A.subtract, ["lc"], ["tab0"])
+    ts(1, T.hs[:, 0:1], ps[7][:, 4:5], 1.0 / 128, None, A.mult, None, (), ["hs"], 7)
+    tt(256, T.tab[:, 256:512], T.lc[:, :], T.tab[:, 0:256], A.subtract, ["lc", "tab0"], ["tab1"])
+    ts(256, T.v0[:, :], T.lc[:, :], T.hs[:, 0:1], -0.5 + 1.0 / 8192, A.mult, A.add, ["lc", "hs"], ["v0"])
+    ts(256, T.tab[:, 512:768], T.v0[:, :], -65.0, 64.0, A.max, A.min, ["v0"], ["tab2"])
+    for t in range(3):
+        dma("Y", 65536, T.win[t:128:16, 1:4097], T.tab[:, 256 * t:256 * t + 256], "dtab",
+            ["tab%d" % t, "wina", "winb", "winc", "wind"], ["win%d" % t])
+    for k in range(CFG["early"], 8):
+        img_load(k)
+
+    act(6, T.pa[:, 0:6], ps[7][:, 0:6], (), ["pa"], bank=7)
+    act(1, kc(0), T.pa[:, 1:2], ["pa"], ["k0"], scale=-4.0)
+    act(1, kc(1), T.pa[:, 0:1], ["pa"], ["k1"], scale=4.0)
+    act(128, T.diag[:, 0:128], T.ident[:, :], ["ident", "k0"], ["dg0"], scale=kc(0))
+    act(128, T.diag[:, 128:256], T.ident[:, :], ["ident", "k1"], ["dg1"], scale=kc(1))
+    act(128, T.diag[:, 256:384], T.ident[:, :], ["ident", "pa"], ["dg2"], scale=T.pa[:, 0:1])
+    act(128, T.diag[:, 384:512], T.ident[:, :], ["ident", "pa"], ["dg3"], scale=T.pa[:, 1:2])
+    wpv = lambda s: T.wp[:, 112 - 16 * s:240 - 16 * s]
+    for b, d0, c, cn in ((6, 0, T.cz, "cz"), (1, 2, T.cx, "cx")):
+        mms(b, [(128, ps[b][:, 128 * h:128 * h + 128], wpv(2 * h + ch), T.diag[:, 128 * (d0 + ch):128 * (d0 + ch + 1)], ch == 0, ch == 1)
+                for h in range(4) for ch in range(2)], ["wp", "dg%d" % d0, "dg%d" % (d0 + 1)])
+        act(512, c[:, :], ps[b][:, :], (), [cn], bank=b)
+    act(1, kc(3), T.pa[:, 3:4], ["pa"], ["k3"], scale=4.0, bias=1.0 - 3.5 / 8)
+    act(192, T.h01[0:8, 0:192], T.m8[0:8, :], ["m8", "p8"], ["h0"], scale=T.p8[0:8, 0:1])
+    act(192, T.h01[0:8, 192:384], T.m8[0:8, :], ["m8", "p8"], ["h1"], scale=T.p8[0:8, 1:2])
+    act(192, T.h2[0:8, 0:192], T.i16b[0:8, :], ["i16b", "p8"], ["h2a"], scale=T.p8[0:8, 1:2], bias=T.p8[0:8, 2:3])
+
+    ts(1, T.pc[:, 2:3], T.pc[:, 0:1], 15, None, A.bitwise_and, None, ["pc"], ["pc2"])
+    ts(2, T.pc[:, 3:5], T.pc[:, 0:2], 1, 8, A.arith_shift_right, A.bitwise_and, ["pc"], ["pc3"])
+    ts(1, T.pc[:, 5:6], T.pc[:, 0:1], 5, None, A.arith_shift_right, None, ["pc"], ["pc5"])
+    ts(16, T.d16f[:, :], T.dj[:, 16:32], 0.0, None, A.is_equal, None, ["dj2"], ["d16f"])
+    cp(4, T.cf[:, 0:4], T.pc[:, 2:6], ["pc2", "pc3", "pc5"], ["cf"])
+    ts(48, T.i12[:, 96:144], T.i12[:, 0:48], T.cf[:, 0:1], T.cf[:, 2:3], A.add, A.mult, ["i1", "cf"], ["i3"])
+    for q in range(NQ):
+        a, b = C0[q] // 4, (C0[q] + W[q]) // 4
+        if W[q] not in W[:q]:
+            ts(1, T.cf[:, 4 + q:5 + q], T.cf[:, 3:4], float(W[q] // 16), None, A.mult, None, ["cf"], [("hn", W[q])])
+        j = 4 + W.index(W[q])
+        ts(b - a, T.i12[:, 144 + a:144 + b], T.i12[:, 48 + a:48 + b], T.cf[:, j:j + 1], T.cf[:, 1:2], A.add, A.mult,
+           [("i2", q), "cf", ("hn", W[q])], [("i4", q)])
+    ts(144, T.zm[:, :], T.dz[:, :], T.cf[:, 0:1], 15.0, A.add, A.is_equal, ["dz", "cf"], ["zm"])
+    tt(48, T.s0[:, :], T.i12[:, 96:144], T.i12[:, 144:192], A.add, ["i3"] + [("i4", q) for q in range(NQ)], ["s0"])
+    part = lambda buf, q: buf[:, C0[q] // 4:(C0[q] + W[q]) // 4]
+    for q in range(NQ):
+        n = W[q] // 4
+        b = 0 if q == 0 else 3
+        mms(b, [(n, ps[b][:, C0[q] + n * h:C0[q] + n * h + n], T.cz[:, 128 * h:128 * h + 128], part(T.s0, q), True, True) for h in range(4)],
+            ["cz", "s0"])
+    for b, a, e in ((0, 0, W[0]), (3, W[0], 192)):
+        ts(e - a, T.off[:, a:e], ps[b][:, a:e], kc(3), 4097.0, A.add, A.min, ["k3"], [("off", 0, u) for u in units(a, e)], b)
+    ts(1, kc(8), T.cf[:, 0:1], 2.0, 1.0 / 4096, A.is_lt, A.mult, ["cf"], ["k8"])
+    ts(1, kc(9), T.cf[:, 0:1], 2.0, 64.0, A.is_equal, A.mult, ["cf"], ["k9"])
+    tt(192, T.h2[0:8, 192:384], T.h2[0:8, 0:192], T.m8[0:8, :], A.mult, ["h2a", "m8"], ["h2"])
+    mms(5, [(192, ps[5][:, 0:192], T.f01[0:8, 0:128], T.h01[0:8, 0:192], True, False),
+            (192, ps[5][:, 0:192], T.f01[0:8, 128:256], T.h01[0:8, 192:384], False, False),
+            (768, ps[5][:, 0:192], T.ones8[0:8, 0:128], T.h2[0:8, 192:384], False, True)], ["f0", "h0", "f1", "h1", "ones8", "h2"])
+    g8 = T.zm[:, 15:143:16]
+    act(8, T.sb1[:, 0:16:2], g8, ["zm", "k8"], ["sb1a"], scale=kc(8))
+    act(8, T.sb1[:, 1:16:2], g8, ["zm", "k9"], ["sb1b"], scale=kc(9))
+    ms(64, T.img[:, 0:64], 0.0, ["imgz0"])
+    ms(64, T.img[:, 8256:8320], 0.0, ["imgz1"])
+    ts(192, T.xb[:, :], ps[5][:, 0:192], -15.5 / 32, None, A.add, None, (), ["xb"], 5)
+    act(1, kc(10), T.d16f[:, 15:16], ["d16f"], ["k10"], scale=-16.0)
+    act(1, kc(4), T.pa[:, 3:4], ["pa"], ["k4"], scale=-4.0)
+    act(1, kc(5), T.pa[:, 3:4], ["pa"], ["k5"], scale=-4.0, bias=0.875)
+    act(8, T.sb2[:, 0:24:3], g8, ["zm", "d16f"], ["sb2a"], scale=T.d16f[:, 0:1])
+    act(8, T.sb2[:, 1:24:3], g8, ["zm", "d16f"], ["sb2b"], scale=T.d16f[:, 1:2])
+    act(8, T.sb2[:, 2:24:3], g8, ["zm", "k10"], ["sb2c"], scale=kc(10))
+    act(1, kc(6), T.pa[:, 5:6], ["pa", "k4"], ["k6"], scale=-32.0, bias=kc(4))
+    act(1, kc(7), T.pa[:, 5:6], ["pa", "k5"], ["k7"], scale=32.0, bias=kc(5))
+    act(1, kc(11), kc(8), ["k8", "k9"], ["k11"], bias=kc(9))
+    act(1, kc(2), T.pa[:, 2:3], ["pa"], ["k2"], bias=-15.5 / 32)
+    act(144, T.wd[:, :], T.zm[:, :], ["zm", "k10"], ["wd"], scale=kc(10))
+    act(144, T.wl[:, :], T.zm[:, :], ["zm", "k11"], ["wl"], scale=kc(11))
+    act(128, T.identg[:, :], T.ident[:, :], ["ident"], ["identg"], scale=32768.0)
+    cp(64, T.identh[:, :], T.ident[:, :], ["ident"], ["identh"])
+    zero = T.wp[:, 128:256]
+
+    for q in range(NQ):
+        w, c0, n = W[q], C0[q], W[q] // 4
+        u0, u1 = c0 // 8, (c0 + w) // 8
+        bl, be, bp = 2 + q % 2, 4 + q % 2, 6 + q % 2
+        gather(0, u0, u1)
+        for us in pieces(u0, u1):
+            mms(bl, [(16, ps[bl][:, 16 * (u - u0):16 * (u - u0 + 1)], gb(0, 128 * u, 128 * u + 128), T.sb1[:, :], True, True) for u in us],
+                [("g", 0, u) for u in us] + ["sb1a", "sb1b"])
+        (p, pn), (x, xn), (c, cn), (e, en), (s, sn), (t, tn), (d, dn), (m, mn) = [tmp(w) for _ in range(8)]
+        tt(w, p, ps[bl][:, 0:2 * w:2], T.xb[:, c0:c0 + w], A.mult, ["xb"], [pn], bl)
+        ts(w, x, p, -0.5 + 1.0 / 8192, MNEG, A.add, A.add, [pn], [xn])
+        ts(w, c, p, -32.0, 32.0 - 1.0 / 4096, A.max, A.min, [pn], [cn])
+        tt(w, s, ps[bl][:, 1:2 * w:2], x, A.add, [xn], [sn], bl)
+        tt(w, e, p, c, A.is_equal, [pn, cn], [en])
+        tt(w, t, s, e, A.mult, [sn, en], [tn])
+        o, on = offs(1, q)
+        ts(w, o, t, KOFF, LAST, A.add, A.min, [tn], on)
+        mms(be, [(3 * w, ps[be][:, 0:3 * w], zero, T.cz[:, 0:3 * w], True, False)]
+            + [(n, ps[be][:, 3 * n * h + 2:3 * n * (h + 1):3], T.cz[:, 128 * h:128 * h + 128], part(T.s0, q), False, False) for h in range(4)],
+            ["wp", "cz", "s0"])
+        gather(1, u0, u1)
+        for us in pieces(u0, u1):
+            mms(be, [(24, ps[be][:, 24 * (u - u0):24 * (u - u0 + 1)], gb(1, 128 * u, 128 * u + 128), T.sb2[:, :], False, u == u1 - 1)
+                     for u in us], [("g", 1, u) for u in us] + ["sb2a", "sb2b", "sb2c"])
+        ts(w, d, ps[be][:, 2:3 * w:3], kc(6), kc(7), A.max, A.min, ["k6", "k7"], [dn], be)
+        tt(w, m, ps[be][:, 2:3 * w:3], d, A.is_equal, [dn], [mn], be)
+        for ch in range(2):
+            tt(w, T.mt[:, 192 * ch + c0:192 * ch + c0 + w], ps[be][:, ch:3 * w:3], m, A.mult, [mn], [("mt", q, ch)], be)
+        for ch in range(2):
+            a = 192 * ch + c0
+            mms(bp, [(n, ps[bp][:, 0:n], wpv(2 * h + ch), T.mt[:, a + n * h:a + n * h + n], ch == 0 and h == 0, ch == 1 and h == 3)
+                     for h in range(4)], ["wp", ("mt", q, ch)])
+        piece = x1_part(T, q, rank)
+        cp(n, piece, ps[bp][:, 0:n], (), [("x1own", q)], bp)
+        trs = [RemoteDMATransfer(dst_ids=[dst_id(topo, d, core) for d in ds], dma_engine_mask=mask_of(es), remote_sem=sm,
+                                 srcs=[piece], dsts=[piece] * len(ds))
+               for ds, es, sm in ((hl, in_e, T.sem["r%d" % q]), (near, out_e, T.sem["xa%d" % q]))]
+        for some in ([trs[:1], trs[1:]] if q == 0 else [trs]):
+            op("G", lambda some=some: g.remote_dma_fused(some, local_sem=T.sem.loc), 800, [("x1own", q)], [("sent", q)], None, "remote")
+        loc[0] += len(in_e) + len(out_e)
+        op(None, None, 0, [("sent", q)], [("way", q)], late=CFG["lat0"] if q == 0 else CFG["lat"], nbytes=-1 if q == 0 else 0)
+        op(None, None, 0, [("way", q), ("x1in", q - 1)], [("x1in", q)], late=600.0,
+           arrive=("xa%d" % q, len(near) * len(out_e) + len(far) * (len(out_e) // 2)))
+
+    def turn(b, a, c, q, closed):
+        n = W[q] // 4
+        return [(n, ps[b][:, a + n * h:a + n * h + n], c[:, 128 * h:128 * h + 128], part(T.sg, q), closed, closed) for h in range(4)]
+
+    def keep_mm(b, wm, wn, st, q, start):
+        mms(b, [(W[q], ps[b][:, 0:W[q]], wm[:, 15 - k:143 - k], gb(st, 16 * C0[q] + k, 16 * (C0[q] + W[q]), 16), start and k == 0, k == 15)
+                for k in range(16)], [wn] + [("g", st, u) for u in units(C0[q], C0[q] + W[q])])
+
+    def final(k):
+        ds = sorted(T.cores[2 * k:2 * k + 2], key=lambda d: d not in far)
+        trs, rs = [], []
+        for i, d in enumerate(ds):
+            rd = T.rank_of(d)
+            b = 6 + i
+            gather(4, 3 * rd, 3 * rd + 3)
+            mms(b, [(16, ps[b][:, 256 + j:304:3], gb(4, 128 * (3 * rd + j), 128 * (3 * rd + j + 1)), T.wp[:, 112:128], True, True)
+                    for j in range(3)], ["wp"] + [("g", 4, 3 * rd + j) for j in range(3)])
+            buf = T.x2 if d == core else T.fs
+            cp(48, buf[:, 48 * rd:48 * rd + 48], ps[b][:, 256:304], (), [("fs", rd)], b)
+            src = T.fs[:, 48 * rd:48 * rd + 48]
+            if d in far:
+                j = far.index(d)
+                trs.append(RemoteDMATransfer(dst_ids=[dst_id(topo, hl[j % 2], core)], dma_engine_mask=mask_of(in_e),
+                                             remote_sem=T.sem["s%d" % (j // 2)], src=src, dst=T.rl[:, 48 * (j // 2):48 * (j // 2) + 48]))
+            elif d in near:
+                trs.append(RemoteDMATransfer(dst_ids=[dst_id(topo, d, core)], dma_engine_mask=mask_of(out_e), remote_sem=T.sem.fa,
+                                             src=src, dst=T.x2[:, 48 * rank:48 * rank + 48]))
+            if d != core:
+                rs.append(("fs", rd))
+                loc[0] += len(out_e)
+        op("G", lambda: g.remote_dma_fused(trs, local_sem=T.sem.loc), 800, rs, [("fsent", k)], None, "remote")
+
+    done = 0
+    for q in range(NQ):
+        w, c0, n = W[q], C0[q], W[q] // 4
+        u0, u1 = c0 // 8, (c0 + w) // 8
+        bs, bl, be = q % 2, 2 + (NQ + q) % 2, (4 + (NQ + q) % 2 if q < 2 else (q + 1) % 2)
+        mms(bs, [(n, ps[bs][:, 256:256 + n], T.ident[:, :], x1_part(T, q, r), r == 0, r == 7) for r in range(8)],
+            ["ident", ("x1in", q), ("x1own", q)])
+        ts(n, part(T.sh, q), ps[bs][:, 256:256 + n], -31.0, 31.0, A.max, A.min, (), [("sh", q)], bs)
+        tt(n, part(T.sg, q), part(T.sh, q), part(T.s0, q), A.add, [("sh", q), "s0"], [("sg", q)])
+        mms(bs, turn(bs, 0, T.cz, q, True), ["cz", ("sg", q)])
+        o, on = offs(2, q)
+        ts(w, o, ps[bs][:, 0:w], kc(3), 4097.0, A.add, A.min, ["k3"], on, bs)
+        mms(be, [(w, ps[be][:, 0:w], zero, T.cz[:, 0:w], True, False)] + turn(be, 0, T.cz, q, False), ["wp", "cz", ("sg", q)])
+        mms(bl, turn(bl, 256, T.cx, q, True), ["cx", ("sg", q)])
+        xi, vi = T.tmi[:, c0:c0 + w], T.tmi[:, 192 + c0:192 + c0 + w]
+        ts(w, xi, ps[bl][:, 256:256 + w], kc(2), None, A.add, None, ["k2"], [("x", q)], bl)
+        gather(2, u0, u1)
+        keep_mm(bl, T.wl, "wl", 2, q, True)
+        (m, mn), (p, pn), (x, xn), (s, sn), (c, cn), (d, dn), (e, en), (t, tn) = [tmp(w) for _ in range(8)]
+        ts(w, vi, ps[bl][:, 0:w], -0.5, None, A.add, None, (), [("vi", q)], bl)
+        tt(w, m, ps[bl][:, 0:w], vi, A.subtract, [("vi", q)], [mn], bl)
+        tt(w, p, m, xi, A.mult, [mn, ("x", q)], [pn])
+        ts(w, x, p, -0.5 + 1.0 / 8192, MNEG, A.add, A.add, [pn], [xn])
+        tt(w, s, x, vi, A.add, [xn, ("vi", q)], [sn])
+        o, on = offs(3, q)
+        ts(w, o, s, KOFF, LAST, A.add, A.min, [sn], on)
+        ts(w, c, p, -32.0, 32.0 - 1.0 / 4096, A.max, A.min, [pn], [cn])
+        tt(w, T.ne[:, c0:c0 + w], p, c, A.not_equal, [pn, cn], [("ne", q)])
+        mms(be, [(w, ps[be][:, 0:w], T.identg[:, :], T.ne[:, c0:c0 + w], False, False)], ["identg", ("ne", q)])
+        gather(3, u0, u1)
+        keep_mm(be, T.wd, "wd", 3, q, False)
+        ts(w, d, ps[be][:, 0:w], kc(6), kc(7), A.max, A.min, ["k6", "k7"], [dn], be)
+        tt(w, e, ps[be][:, 0:w], d, A.is_equal, [dn], [en], be)
+        tt(w, t, s, e, A.mult, [sn, en], [tn])
+        o, on = offs(4, q)
+        ts(w, o, t, KOFF, LAST, A.add, A.min, [tn], on)
+        while 48 * (done + 1) <= c0 + w:
+            final(done)
+            done += 1
+
+    sent = [("fsent", k) for k in range(4)]
+    op(None, None, 0, sent, ["fa"], late=CFG["lat"] / 2, arrive=("fa", len(near) * len(out_e)))
+    op(None, None, 0, sent, ["fb"], late=CFG["lat"], arrive=("fb", len(far) * len(out_e)))
+    for ds, res in (([core], ("fs", rank)), (near, "fa"), (far, "fb")):
+        mms(1, [(128, ps[1][0:48, 384:512], T.x2[:, 48 * T.rank_of(d):48 * T.rank_of(d) + 48], T.identh[:, :], d == core, d == far[-1])
+                for d in ds], ["identh", res])
+    act(128, T.yo[0:48, :], ps[1][0:48, 384:512], (), ["yo"], bank=1)
+    dma("Y", 24576, T.y[:, :], T.yo[0:48, :], "dy", ["yo"], ["y"])
+    op("Y", None, 0, ["y"], ())
+
+    order = schedule(ops)
+    first = {i: k for k, i in enumerate(order)}
+    into, prev = {}, {}
+    for i in order:
+        o, j = ops[i], prev.get(ops[i]["eng"])
+        a = ops[j]["gat"] if j is not None else None
+        b = o["gat"]
+        if a and b and a[0] == b[0] and a[2] == b[1] and b[2] - a[1] <= CFG["merge"] and b[0] != 4 and \
+                all(first[d] < first[j] for d in o["deps"]):
+            a[2] = b[2]
+            ops[j]["deps"] = ops[j]["deps"] | o["deps"]
+            into[i] = j
+        else:
+            prev[o["eng"]] = i
+    order = [i for i in order if i not in into]
+    pos = {i: k for k, i in enumerate(order)}
+
+    def live(o):
+        ds = set(into.get(j, j) for j in o["deps"])
+        return [j for j in ds if not (o["eng"] == "P" and ops[j]["eng"] == "P") and ops[j]["dma"] != "remote"]
+
+    needed = set()
+    for i in order:
+        best = {}
+        for j in (live(ops[i]) if ops[i]["eng"] else []):
+            e = ops[j]["eng"]
+            if ops[j]["dma"] is None and ops[j]["arrive"] is None and (e not in best or pos[j] > pos[best[e]]):
+                best[e] = j
+        needed.update(best.values())
+    total, token, count = {}, {}, {}
+    for o in ops:
+        if o["dma"] not in (None, "remote"):
+            total[o["dma"]] = total.get(o["dma"], 0) + 16
+    for i in order:
+        o = ops[i]
+        if o["arrive"] is not None:
+            token[i] = o["arrive"]
+        elif o["dma"] is not None:
+            token[i] = (o["dma"], total.get(o["dma"], 0))
+        elif i in needed:
+            count[o["eng"]] = count.get(o["eng"], 0) + 1
+            token[i] = ("c" + o["eng"], count[o["eng"]])
+    waited = {}
+    for i in order:
+        o = ops[i]
+        if o["eng"] is None:
+            continue
+        want = {}
+        for j in live(o):
+            if j in token:
+                sm, v = token[j]
+                want[sm] = max(want.get(sm, 0), v)
+        for sm, v in sorted(want.items()):
+            if waited.get((o["eng"], sm), 0) < v:
+                queue[o["eng"]].wait_ge(T.sem[sm], v)
+                waited[(o["eng"], sm)] = v
+        if o["gat"]:
+            ins = gather_call(o["eng"], o["gat"][0], o["gat"][1], o["gat"][2])
+        elif o["fn"] is None:
+            continue
+        else:
+            ins = o["fn"]()
+        if o["dma"] not in (None, "remote"):
+            ins.then_inc(T.sem[o["dma"]], 16)
+        elif i in needed:
+            ins.then_inc(T.sem["c" + o["eng"]], 1)
+    g.wait_ge(T.sem.loc, loc[0])

@@ -2,10 +2,10 @@ import numpy as np
 from concourse.bass import DstId, RemoteDMATransfer
 from concourse.mybir import AluOpType as A, ActivationFunctionType as F
 
-CFG = {"W": [64, 64, 64], "piece": 2, "merge": 2, "delta": 500.0, "early": 3, "lat0": 9000.0, "lat": 5500.0, "gat": 1.62,
-       "pe": 1.04, "bw": 250.0, "tries": 2500}
-CASES = ((1.0, 1.0, 1.0, 1.0, 0.9), (0.7, 0.5, 0.7, 0.7, 0.6), (1.35, 1.0, 1.3, 1.3, 1.5), (1.0, 0.5, 0.8, 1.0, 0.6),
-         (0.85, 1.0, 1.0, 0.7, 1.2))
+CFG = {"W": [48, 64, 80], "piece": 3, "merge": 4, "delta": 300.0, "early": 4, "lat0": 6500.0, "lat": 4300.0, "gat": 1.62,
+       "pe": 1.04, "bw": 250.0, "tries": 3500}
+CASES = ((0.8, 0.8, 1.0, 0.85, 1.0, 0.8), (0.6, 0.4, 0.9, 0.7, 0.85, 0.8), (1.3, 1.1, 1.4, 1.3, 1.6, 1.15),
+         (1.0, 0.5, 1.2, 1.0, 1.4, 1.0), (0.8, 0.8, 1.3, 0.85, 1.5, 0.8))
 FOUND = {}
 SLOT = 32
 B, H, W32, I32 = "bfloat16", "float16", "float32", "int32"
@@ -20,8 +20,8 @@ SCRATCH = {n: ("sbuf", [128, c], d) for n, c, d in (
     ("sg", 48, H), ("fs", 384, H), ("x2", 384, H), ("rl", 96, H), ("yo", 128, W32))}
 for _b in range(8):
     SCRATCH["ps%d" % _b] = ("psum", [128, 512], "float32")
-SEMAPHORES = ["cV", "cA", "cP", "cG", "dpose", "dlens", "dimg", "dtab", "dy", "xa0", "xa1", "xa2", "xa3", "fa", "fb", "r0", "r1",
-              "r2", "r3", "s0", "s1", "loc"]
+SEMAPHORES = ["cV", "cA", "cP", "cG", "dpose", "dlens", "dimg", "dtab", "dy", "xa0", "xa1", "xa2", "xb0", "xb1", "xb2", "fa", "fb",
+              "r0", "r1", "r2", "s0", "s1", "loc"]
 
 MNEG = -12582912.0
 M32 = 402653184.0
@@ -65,7 +65,7 @@ def helper_program(g, core, owner, far, i, T, topo):
         g.wait_ge(T.sem["r%d" % q], n_in)
         piece = x1_part(T, q, r)
         g.remote_dma_fused([RemoteDMATransfer(dst_ids=[dst_id(topo, d, core)], dma_engine_mask=mask_of(engs[j * half:(j + 1) * half]),
-                                              remote_sem=T.sem["xa%d" % q], src=piece, dst=piece)
+                                              remote_sem=T.sem["xb%d" % q], src=piece, dst=piece)
                             for j, d in enumerate(far[2 * i:2 * i + 2])], local_sem=T.sem.loc)
         loc += 2 * half
     for j in range(2):
@@ -78,7 +78,8 @@ def helper_program(g, core, owner, far, i, T, topo):
 
 
 def lengths(ops, case):
-    cost = [(o["cost"] - 60) * case[0] + 60 if o["gat"] else o["cost"] * case[1] if o["eng"] == "P" else o["cost"] for o in ops]
+    cost = [(o["cost"] - 60) * case[0] + 60 if o["gat"] else o["cost"] * case[1] if o["eng"] == "P" else
+            (o["cost"] - 60) * case[5] + 60 if o["eng"] in ("V", "A") else o["cost"] for o in ops]
     late = [o["late"] * case[4 if o["bytes"] < 0 else 2] if o["eng"] is None else o["late"] for o in ops]
     return cost, late, [max(0, o["bytes"]) * case[3] / CFG["bw"] for o in ops]
 
@@ -434,8 +435,8 @@ def rank_program(g, core, T, topo):
             op("G", lambda some=some: g.remote_dma_fused(some, local_sem=T.sem.loc), 800, [("x1own", q)], [("sent", q)], None, "remote")
         loc[0] += len(in_e) + len(out_e)
         op(None, None, 0, [("sent", q)], [("way", q)], late=CFG["lat0"] if q == 0 else CFG["lat"], nbytes=-1 if q == 0 else 0)
-        op(None, None, 0, [("way", q), ("x1in", q - 1)], [("x1in", q)], late=600.0,
-           arrive=("xa%d" % q, len(near) * len(out_e) + len(far) * (len(out_e) // 2)))
+        op(None, None, 0, [("way", q), ("x1in", q - 1)], [("x1in", q)], late=600.0, arrive=("xb%d" % q, len(far) * (len(out_e) // 2)))
+        op(None, None, 0, [("sent", q)], [("x1near", q)], late=CFG["lat"] / 2, arrive=("xa%d" % q, len(near) * len(out_e)))
 
     def turn(b, a, c, q, closed):
         n = W[q] // 4
@@ -445,10 +446,18 @@ def rank_program(g, core, T, topo):
         mms(b, [(W[q], ps[b][:, 0:W[q]], wm[:, 15 - k:143 - k], gb(st, 16 * C0[q] + k, 16 * (C0[q] + W[q]), 16), start and k == 0, k == 15)
                 for k in range(16)], [wn] + [("g", st, u) for u in units(C0[q], C0[q] + W[q])])
 
+    def groups(src):
+        late = sorted(T.cores[4:], key=lambda d: d == src or topo.may_write(src, d))
+        return [sorted(T.cores[a:a + 2], key=lambda d: d == src or topo.may_write(src, d)) for a in (0, 2)] + [late[:2], late[2:]]
+
+    def direct(src, dst):
+        return [[d for d in ds if d != src and topo.may_write(src, d)] for ds in groups(src) if dst in ds][0]
+
+    ways = {"fa": [], "fb": []}
+
     def final(k):
-        ds = sorted(T.cores[2 * k:2 * k + 2], key=lambda d: d not in far)
         trs, rs = [], []
-        for i, d in enumerate(ds):
+        for i, d in enumerate(groups(core)[k]):
             rd = T.rank_of(d)
             b = 6 + i
             gather(4, 3 * rd, 3 * rd + 3)
@@ -459,14 +468,19 @@ def rank_program(g, core, T, topo):
             src = T.fs[:, 48 * rd:48 * rd + 48]
             if d in far:
                 j = far.index(d)
-                trs.append(RemoteDMATransfer(dst_ids=[dst_id(topo, hl[j % 2], core)], dma_engine_mask=mask_of(in_e),
+                es = (in_e, out_e)[i]
+                trs.append(RemoteDMATransfer(dst_ids=[dst_id(topo, hl[j % 2], core)], dma_engine_mask=mask_of(es),
                                              remote_sem=T.sem["s%d" % (j // 2)], src=src, dst=T.rl[:, 48 * (j // 2):48 * (j // 2) + 48]))
             elif d in near:
-                trs.append(RemoteDMATransfer(dst_ids=[dst_id(topo, d, core)], dma_engine_mask=mask_of(out_e), remote_sem=T.sem.fa,
+                m = len(out_e) // len(direct(core, d))
+                j = direct(core, d).index(d)
+                es = out_e[m * j:m * j + m]
+                trs.append(RemoteDMATransfer(dst_ids=[dst_id(topo, d, core)], dma_engine_mask=mask_of(es), remote_sem=T.sem.fa,
                                              src=src, dst=T.x2[:, 48 * rank:48 * rank + 48]))
             if d != core:
                 rs.append(("fs", rd))
-                loc[0] += len(out_e)
+                loc[0] += len(es)
+                ways["fb" if d in far else "fa"].append(("fsent", k))
         op("G", lambda: g.remote_dma_fused(trs, local_sem=T.sem.loc), 800, rs, [("fsent", k)], None, "remote")
 
     done = 0
@@ -474,8 +488,9 @@ def rank_program(g, core, T, topo):
         w, c0, n = W[q], C0[q], W[q] // 4
         u0, u1 = c0 // 8, (c0 + w) // 8
         bs, bl, be = q % 2, 2 + (NQ + q) % 2, (4 + (NQ + q) % 2 if q < 2 else (q + 1) % 2)
-        mms(bs, [(n, ps[bs][:, 256:256 + n], T.ident[:, :], x1_part(T, q, r), r == 0, r == 7) for r in range(8)],
-            ["ident", ("x1in", q), ("x1own", q)])
+        for ds, res in (([core] + near, [("x1near", q), ("x1own", q)]), (far, [("x1in", q)])):
+            mms(bs, [(n, ps[bs][:, 256:256 + n], T.ident[:, :], x1_part(T, q, T.rank_of(d)), d == core, d == far[-1]) for d in ds],
+                ["ident"] + res)
         ts(n, part(T.sh, q), ps[bs][:, 256:256 + n], -31.0, 31.0, A.max, A.min, (), [("sh", q)], bs)
         tt(n, part(T.sg, q), part(T.sh, q), part(T.s0, q), A.add, [("sh", q), "s0"], [("sg", q)])
         mms(bs, turn(bs, 0, T.cz, q, True), ["cz", ("sg", q)])
@@ -505,13 +520,12 @@ def rank_program(g, core, T, topo):
         tt(w, t, s, e, A.mult, [sn, en], [tn])
         o, on = offs(4, q)
         ts(w, o, t, KOFF, LAST, A.add, A.min, [tn], on)
-        while 48 * (done + 1) <= c0 + w:
+        while done < 4 and (48, 96, 192, 192)[done] <= c0 + w:
             final(done)
             done += 1
 
-    sent = [("fsent", k) for k in range(4)]
-    op(None, None, 0, sent, ["fa"], late=CFG["lat"] / 2, arrive=("fa", len(near) * len(out_e)))
-    op(None, None, 0, sent, ["fb"], late=CFG["lat"], arrive=("fb", len(far) * len(out_e)))
+    op(None, None, 0, ways["fa"], ["fa"], late=CFG["lat"] / 2, arrive=("fa", sum(len(out_e) // len(direct(d, core)) for d in near)))
+    op(None, None, 0, ways["fb"], ["fb"], late=CFG["lat"], arrive=("fb", len(far) * len(out_e)))
     for ds, res in (([core], ("fs", rank)), (near, "fa"), (far, "fb")):
         mms(1, [(128, ps[1][0:48, 384:512], T.x2[:, 48 * T.rank_of(d):48 * T.rank_of(d) + 48], T.identh[:, :], d == core, d == far[-1])
                 for d in ds], ["identh", res])

@@ -1,32 +1,35 @@
+import math
 import numpy as np
 from concourse.bass import DstId, RemoteDMATransfer
 from concourse.mybir import AluOpType as A, ActivationFunctionType as F
 
-CFG = {"W": [48, 64, 80], "piece": 3, "merge": 4, "delta": 300.0, "early": 4, "lat0": 6500.0, "lat": 4300.0, "gat": 1.62,
-       "pe": 1.04, "bw": 250.0, "tries": 3500}
-CASES = ((0.8, 0.8, 1.0, 0.85, 1.0, 0.8), (0.6, 0.4, 0.9, 0.7, 0.85, 0.8), (1.3, 1.1, 1.4, 1.3, 1.6, 1.15),
-         (1.0, 0.5, 1.2, 1.0, 1.4, 1.0), (0.8, 0.8, 1.3, 0.85, 1.5, 0.8))
+CFG = {"piece": 2, "merge": {"V": 4, "A": 6}, "delta": 300.0, "early": 3, "lat0": 3600.0, "lat": 3100.0, "gap": 1000.0, "latn": 2600.0,
+       "latf": 3600.0, "gat": 1.62, "pe": 0.7, "bw": 350.0, "tries": 60000, "heat": 120.0, "seed": 1, "dma": 1100.0, "call": 350.0,
+       "call0": 1650.0, "mean": 0.1, "when": 2, "d2": 60.0, "rep": 4}
+G1 = [[0], [1, 2]]
+ROWS = 98000
+CASES = ((0.7, 1.0, 1.0, 1.0, 1.0, 0.83), (0.57, 0.8, 0.85, 0.85, 0.85, 0.8), (1.2, 1.4, 1.4, 1.3, 1.5, 1.1))
+WEIGHTS = (0.5, 0.3, 0.2)
+WAKE, FIX = 90.0, 42.0
 FOUND = {}
-SLOT = 32
+NQ = 3
 B, H, W32, I32 = "bfloat16", "float16", "float32", "int32"
 SCRATCH = {n: ("sbuf", [128, c], d) for n, c, d in (
-    ("img", 8320, B), ("win", 4112, B), ("posei", 8, I32), ("p8", 8, W32), ("pa", 8, W32), ("kc", 24, W32), ("hs", 4, W32),
-    ("lc", 256, I32), ("v0", 256, I32), ("tab", 768, B), ("dj", 32, I32), ("d16f", 16, W32), ("wp", 256, B), ("ones8", 192, W32),
-    ("rep", 128, W32), ("onesb", 128, B), ("ident", 128, B), ("identh", 128, H), ("identg", 128, B), ("diag", 512, B),
-    ("cz", 512, B), ("cx", 512, B), ("pc", 8, I32), ("cf", 16, W32), ("i12", 192, W32), ("s0", 48, B), ("dz", 144, W32),
-    ("zm", 144, W32), ("wl", 144, B), ("wd", 144, B), ("sb1", 16, B), ("sb2", 24, B), ("m8", 192, W32), ("i16b", 192, W32),
-    ("f01", 256, B), ("h01", 384, B), ("h2", 384, W32), ("xb", 192, I32), ("off", 960, "uint16"), ("gb", 15360, B),
-    ("tmp", 192 * 17, W32), ("tmi", 384, I32), ("mt", 384, B), ("ne", 192, B), ("x1", 8 * SLOT * 4, B), ("sh", 48, B),
-    ("sg", 48, H), ("fs", 384, H), ("x2", 384, H), ("rl", 96, H), ("yo", 128, W32))}
+    ("img", 8320, B), ("win", 4112, B), ("posei", 8, I32), ("p8", 8, W32), ("pa", 8, W32), ("kc", 16, W32), ("hs", 4, W32),
+    ("lc", 256, I32), ("v0", 256, I32), ("tab", 768, B), ("dj", 32, I32), ("d16", 16, W32), ("d4", 32, B), ("wp", 208, B),
+    ("ones", 128, W32), ("rep", 128, W32), ("onesb", 128, B), ("ident", 128, B), ("ig0", 128, B), ("ig1", 128, B), ("ig2", 128, B),
+    ("sel", 192, B), ("lt", 48, B), ("lm", 256, B), ("cm", 192, B), ("s0", 384, B), ("ru", 384, B), ("wd", 144, B),
+    ("sb1", 16, B), ("sb2", 24, B), ("sb3", 16, B), ("cr", 448, W32), ("ct", 384, W32), ("xi", 384, I32),
+    ("off", 960, "uint16"), ("gb", 15360, B), ("tf", 576, W32), ("tb", 768, B), ("tz", 1440, B), ("mt", 384, B), ("x1", 384, B),
+    ("raw", 4096, B), ("r16", 128, B), ("xc", 48, B), ("sh", 384, H), ("fs", 384, H), ("x2", 384, H), ("rl", 96, H), ("yo", 128, W32))}
 for _b in range(8):
     SCRATCH["ps%d" % _b] = ("psum", [128, 512], "float32")
-SEMAPHORES = ["cV", "cA", "cP", "cG", "dpose", "dlens", "dimg", "dtab", "dy", "xa0", "xa1", "xa2", "xb0", "xb1", "xb2", "fa", "fb",
-              "r0", "r1", "r2", "s0", "s1", "loc"]
+SEMAPHORES = ["cV", "cA", "cP", "cG", "dpose", "dlens", "dimg", "dtab", "draw", "dy", "loc", "s", "fa", "fb"] + \
+    [n + str(q) for n in ("xa", "xb", "r") for q in range(NQ)]
 
-MNEG = -12582912.0
-M32 = 402653184.0
 LAST = 8319.0
-KOFF = -MNEG + 4192.0
+ROUND = 191.5 + 1.0 / 8192
+BASE = 64.0 * 65 - 160
 CYC = 1.04
 
 
@@ -50,36 +53,32 @@ def dst_id(topo, d, s):
     return DstId(rid=rid, pnc=pid)
 
 
-def x1_part(T, q, r):
-    c0 = SLOT * (8 * q + r)
-    return T.x1[:, c0:c0 + CFG["W"][q] // 4]
+def part(buf, qs, r):
+    return buf[:, 16 * (NQ * r + qs[0]):16 * (NQ * r + qs[-1] + 1)]
+
+
+def group(groups, q):
+    return [x for x in groups if q in x][0]
 
 
 def helper_program(g, core, owner, far, i, T, topo):
     r = T.rank_of(owner)
     engs = topo.engines(core, far[0])
     half = len(engs) // 2
-    n_in = len(topo.engines(owner, core)) - len(engs)
-    loc = 0
-    for q in range(len(CFG["W"])):
-        g.wait_ge(T.sem["r%d" % q], n_in)
-        piece = x1_part(T, q, r)
+    n_in = len(topo.engines(owner, core)) // 2
+    steps = [("r%d" % qs[-1], "xb%d" % qs[-1], [part(T.x1, qs, r)] * 2, part(T.x1, qs, r)) for qs in G1]
+    steps.append(("s", "fb", [T.rl[:, 0:48], T.rl[:, 48:96]], part(T.x2, range(NQ), r)))
+    for came, sem, src, dst in steps:
+        g.wait_ge(T.sem[came], n_in)
         g.remote_dma_fused([RemoteDMATransfer(dst_ids=[dst_id(topo, d, core)], dma_engine_mask=mask_of(engs[j * half:(j + 1) * half]),
-                                              remote_sem=T.sem["xb%d" % q], src=piece, dst=piece)
+                                              remote_sem=T.sem[sem], src=src[j], dst=dst)
                             for j, d in enumerate(far[2 * i:2 * i + 2])], local_sem=T.sem.loc)
-        loc += 2 * half
-    for j in range(2):
-        d = far[2 * j + i]
-        g.wait_ge(T.sem["s%d" % j], n_in)
-        rid, pid = topo.addr(d, core)
-        g.remote_dma(T.x2[:, 48 * r:48 * r + 48], T.rl[:, 48 * j:48 * j + 48], T.sem.fb, T.sem.loc, pid, rid, mask_of(engs))
-        loc += len(engs)
-    g.wait_ge(T.sem.loc, loc)
+    g.wait_ge(T.sem.loc, len(steps) * len(engs))
 
 
 def lengths(ops, case):
-    cost = [(o["cost"] - 60) * case[0] + 60 if o["gat"] else o["cost"] * case[1] if o["eng"] == "P" else
-            (o["cost"] - 60) * case[5] + 60 if o["eng"] in ("V", "A") else o["cost"] for o in ops]
+    cost = [(o["cost"] - 60) * case[0] + FIX if o["gat"] else o["cost"] * case[1] if o["eng"] == "P" else
+            (o["cost"] - 60) * case[5] + FIX if o["eng"] in ("V", "A", "VA") else o["cost"] for o in ops]
     late = [o["late"] * case[4 if o["bytes"] < 0 else 2] if o["eng"] is None else o["late"] for o in ops]
     return cost, late, [max(0, o["bytes"]) * case[3] / CFG["bw"] for o in ops]
 
@@ -97,13 +96,13 @@ def plan(ops, pre, succ, prio, size):
                 cand.append((max(at[i], free.get(e, 0.0)) if e else at[i], -prio[i], e, i))
         t0, _, e0, i0 = min(cand, key=lambda c: c[:2])
         if e0 is not None:
-            d = CFG["delta"] if cost[i0] > 400 else 30.0
+            d = CFG["delta"] if cost[i0] > 300 else CFG["d2"]
             t0, _, e0, i0 = min([c for c in cand if c[2] == e0 and c[0] <= t0 + d], key=lambda c: (c[1], c[0]))
         eng[i0] = e0
         t1 = free[e0] = t0 + cost[i0]
         if load[i0]:
-            line = max(line, t1) + load[i0]
-        fin = (line if load[i0] else t1) + late[i0]
+            line = max(line, t1 + late[i0] * 0.6) + load[i0]
+        fin = line + late[i0] * 0.4 if load[i0] else t1 + late[i0]
         order.append(i0)
         ready.remove(i0)
         for j, kind in succ[i0]:
@@ -114,20 +113,55 @@ def plan(ops, pre, succ, prio, size):
     return order, eng
 
 
-def replay(order, eng, succ, size):
+def replay(order, eng, succ, size, gat, trace=None):
     cost, late, load = size
-    free, at, line, end = {}, [0.0] * len(eng), 0.0, 0.0
+    n = len(eng)
+    free, last, at, line, end = {e: 0.0 for e in "VAPGY"}, {"V": None, "A": None}, [0.0] * n, 0.0, 0.0
+    why, before, start, final, lineby = [None] * n, {}, [0.0] * n, None, None
     for i in order:
-        e = eng[i]
-        t1 = (max(at[i], free.get(e, 0.0)) if e else at[i]) + cost[i]
-        free[e] = t1
+        e, t1 = eng[i], at[i]
+        if e:
+            f = free[e]
+            if e in last:
+                a, b = last[e], gat[i]
+                if a and b and a[0] == b[0] and a[2] == b[1] and t1 < f - cost[i]:
+                    f -= FIX
+                last[e] = b
+            if f > t1:
+                t1 = f
+                if trace is not None:
+                    why[i] = (before[e], True)
+            if trace is not None:
+                before[e], start[i] = i, max(t1, free[e])
+            t1 += cost[i] + 15.0 if e == "A" else cost[i]
+            free[e] = t1
+        elif trace is not None:
+            start[i] = t1
         if load[i]:
-            line = max(line, t1) + load[i]
-        fin = (line if load[i] else t1) + late[i]
-        end = max(end, fin)
+            if trace is not None:
+                if line > t1 + late[i] * 0.6:
+                    why[i] = (lineby, False)
+                lineby = i
+            line = max(line, t1 + late[i] * 0.6) + load[i]
+            fin = line + late[i] * 0.4
+        else:
+            fin = t1 + late[i]
+        if fin > end:
+            end, final = fin, i
+        fin += WAKE
         for j, kind in succ[i]:
-            at[j] = max(at[j], t1 if kind else fin + 60)
-    return end
+            t = t1 if kind else fin
+            if t > at[j]:
+                at[j] = t
+                if trace is not None:
+                    why[j] = (i, False)
+    if trace is not None:
+        trace["start"], trace["held"] = start, []
+        while why[final]:
+            if why[final][1]:
+                trace["held"].append((why[final][0], final))
+            final = why[final][0]
+    return end + CFG["mean"] * sum(at) / n
 
 
 def schedule(ops):
@@ -143,26 +177,67 @@ def schedule(ops):
     for i in range(n - 1, -1, -1):
         base[i] = sizes[0][0][i] + sizes[0][1][i] + sizes[0][2][i] + 60 + max([base[j] for j, _ in succ[i]] + [0.0])
 
-    def value(bend):
-        order, eng = plan(ops, pre, succ, [b + d for b, d in zip(base, bend)], sizes[0])
-        return sum(replay(order, eng, succ, s) for s in sizes), order, eng
-
-    rng = np.random.RandomState(1)
-    bend = FOUND.get(n, [0.0] * n)
-    best = value(bend)
-    for _ in range(CFG["tries"] if n not in FOUND else 0):
-        other = list(bend)
-        a = int(rng.randint(n))
-        step = float(rng.normal()) * 1500.0
-        for i in range(a, min(n, a + 1 + int(rng.randint(12)))):
-            other[i] += step
-        got = value(other)
-        if got[0] <= best[0]:
-            best, bend = got, other
-    FOUND.setdefault(n, bend)
-    for o, e in zip(ops, best[2]):
+    if n not in FOUND:
+        order, eng = plan(ops, pre, succ, base, sizes[0])
+        gat = [o["gat"] for o in ops]
+        value = lambda order, eng: sum(w * replay(order, eng, succ, s, gat) for w, s in zip(WEIGHTS, sizes))
+        free = [i for i, o in enumerate(ops) if o["eng"] in ("V", "A", "VA", "P")]
+        now = value(order, eng)
+        best = (now, order, eng)
+        rng = np.random.RandomState(CFG["seed"])
+        rand = rng.rand(CFG["tries"], 8).tolist()
+        held = None
+        for k, r in enumerate(rand):
+            if held is None:
+                trace = {}
+                replay(order, eng, succ, sizes[0 if r[7] < 0.6 else 1 if r[7] < 0.8 else 2], gat, trace)
+                order = sorted(order, key=lambda i: trace["start"][i])
+                held = [(j, i) for j, i in trace["held"] if ops[i]["eng"] not in ("G", "Y")]
+            other, e2 = list(order), list(eng)
+            if held and r[0] < 0.5:
+                j, i = held[int(r[1] * len(held))]
+                a = (i, j)[r[2] < 0.5]
+                if ops[a]["eng"] == "VA" and r[3] < 0.5:
+                    e2[a] = "V" if eng[a] == "A" else "A"
+                elif a == i:
+                    pj, pi = other.index(j), other.index(i)
+                    need = {i}
+                    for x in other[pi - 1:pj - 1 if pj else None:-1]:
+                        if any(y in need for y, _ in succ[x]):
+                            need.add(x)
+                    if j in need:
+                        continue
+                    mid = other[pj:pi + 1]
+                    other[pj:pi + 1] = [x for x in mid if x in need] + [x for x in mid if x not in need]
+                else:
+                    pj, pi = other.index(j), min(n - 1, other.index(i) + int(r[4] * r[4] * 12))
+                    need = {j}
+                    for x in other[pj + 1:pi + 1]:
+                        if pre[x] & need:
+                            need.add(x)
+                    mid = other[pj:pi + 1]
+                    other[pj:pi + 1] = [x for x in mid if x not in need] + [x for x in mid if x in need]
+            else:
+                i = free[int(r[1] * len(free))]
+                if ops[i]["eng"] == "VA" and r[2] < 0.4:
+                    e2[i] = "V" if eng[i] == "A" else "A"
+                p = other.index(i)
+                lo, hi, reach = p, p, 1 + int(r[3] * 30)
+                while lo > max(0, p - reach) and other[lo - 1] not in pre[i]:
+                    lo -= 1
+                while hi < min(n - 1, p + reach) and i not in pre[other[hi + 1]]:
+                    hi += 1
+                other.pop(p)
+                other.insert(lo if r[4] < 0.2 else hi if r[4] > 0.8 else lo + int(r[5] * (hi + 1 - lo)), i)
+            got = value(other, e2)
+            if got <= now - CFG["heat"] * (1 - k / CFG["tries"]) * math.log(r[6] + 1e-12):
+                now, order, eng, held = got, other, e2, None
+                if got < best[0]:
+                    best = (got, other, e2)
+        FOUND[n] = best
+    for o, e in zip(ops, FOUND[n][2]):
         o["eng"] = e
-    return best[1]
+    return list(FOUND[n][1])
 
 
 def rank_program(g, core, T, topo):
@@ -178,12 +253,14 @@ def rank_program(g, core, T, topo):
     near = [d for d in T.cores if d != core and d not in far]
     out_e = topo.engines(core, near[0])
     in_e = [e for e in topo.engines(core, hl[0]) if e not in out_e]
+    other = helpers(T.cores[0], T, topo)[0]
+    half = [[r for r, d in enumerate(T.cores) if (d in other) == h] for h in (False, True)]
+    dk, dh = half[0][1] - half[0][0], half[1][0] - half[0][0]
+    assert half == [[h * dh + k * dk for k in range(4)] for h in range(2)]
+    hfar = 1 if rank in half[0] else 0
     V, S, P, Y = g.vector, g.scalar, g.tensor, g.sync
     queue = {"V": V, "A": S, "P": P, "G": g, "Y": Y}
     ps = [T["ps%d" % b] for b in range(8)]
-    W = CFG["W"]
-    NQ = len(W)
-    C0 = [sum(W[:q]) for q in range(NQ)]
 
     ops, last_w, readers, last_q = [], {}, {}, {}
 
@@ -218,62 +295,71 @@ def rank_program(g, core, T, topo):
 
     def ts(n, out, in0, s1, s2, o0, o1, r, w, bank=None):
         if o1 is None:
-            op("V", lambda: V.tensor_scalar(out, in0, s1, None, o0), vc(n), r, w, bank)
+            op("V", lambda e: V.tensor_scalar(out, in0, s1, None, o0), vc(n), r, w, bank)
         else:
-            op("V", lambda: V.tensor_scalar(out, in0, s1, s2, o0, o1), vc(n), r, w, bank)
+            op("V", lambda e: V.tensor_scalar(out, in0, s1, s2, o0, o1), vc(n), r, w, bank)
 
     def tt(n, out, a, b, o, r, w, bank=None):
-        op("V", lambda: V.tensor_tensor(out, a, b, o), vc(n if bank is not None else 2 * n), r, w, bank)
+        op("V", lambda e: V.tensor_tensor(out, a, b, o), vc(n if bank is not None else 2 * n), r, w, bank)
 
-    def cp(n, out, a, r, w, bank=None):
-        op("V", lambda: V.tensor_copy(out, a), vc(n), r, w, bank)
+    def ms(n, ap, c, r, w):
+        op("V", lambda e: V.memset(ap, c), vc(n // 2), r, w)
 
-    def ms(n, ap, c, w):
-        op("V", lambda: V.memset(ap, c), vc(n // 2), (), w)
+    def lin(n, out, a, r, w, scale=1.0, bias=0.0, bank=None, eng="VA"):
+        op(eng, lambda e: S.activation(out, a, F.Identity, bias=bias, scale=scale) if e == "A" else
+           V.tensor_scalar(out, a, scale, bias, A.mult, A.add), vc(n), r, w, bank)
 
-    def act(n, out, a, r, w, scale=1.0, bias=0.0, bank=None):
-        op("A", lambda: S.activation(out, a, F.Identity, bias=bias, scale=scale), vc(n), r, w, bank)
-
-    def mms(b, calls, r):
-        op("P", lambda: [P.matmul(*c[1:]) for c in calls][-1], sum(max(64, c[0]) for c in calls) * CFG["pe"], r, (), b)
+    def mms(b, calls, r, four=False, least=64):
+        op("P", lambda e: [P.matmul(*c[1:]) for c in calls][-1], sum(max(least, c[0]) for c in calls) * CFG["pe"] * (4 if four else 1),
+           r, (), b)
 
     def iota(n, out, pat, base, cm, w, fl=True):
         if fl:
-            op("G", lambda: g.iota(out, pat, base, cm, allow_small_or_imprecise_dtypes=True), 130 + 2 * n * CYC, (), w)
+            op("G", lambda e: g.iota(out, pat, base, cm, allow_small_or_imprecise_dtypes=True), 130 + 2 * n * 0.87, (), w)
         else:
-            op("G", lambda: g.iota(out, pat, base, cm), 130 + 2 * n * CYC, (), w)
+            op("G", lambda e: g.iota(out, pat, base, cm), 130 + 2 * n * 0.87, (), w)
 
     def sel(n, out, a, pat, cm, r, w):
-        op("G", lambda: g.affine_select(out, a, pat, A.is_equal, 0.0, 0, cm), 170 + 2 * n * CYC, r, w)
+        op("G", lambda e: g.affine_select(out, a, pat, A.is_equal, 0.0, 0, cm), 170 + 2 * n * 0.87, r, w)
 
-    def dma(eng, nbytes, out, a, sem, r, w):
-        op(eng, lambda: queue[eng].dma_start(out, a), 60, r, w, None, sem, late=1700.0, nbytes=nbytes)
+    def dma(nbytes, out, a, sem, r, w):
+        op("Y", lambda e: Y.dma_start(out, a), 60, r, w, None, sem, late=CFG["dma"], nbytes=nbytes)
 
-    nt = [0]
+    loc = [0]
 
-    def tmp(n):
-        nt[0] += n
-        return T.tmp[:, nt[0] - n:nt[0]], "t%d" % nt[0]
+    def send(trs, r, w):
+        cost = CFG["call"] if loc[0] else CFG["call0"]
+        loc[0] += sum(len(t[1]) for t in trs)
+        calls = [RemoteDMATransfer(dst_ids=[dst_id(topo, d, core) for d in ds], dma_engine_mask=mask_of(es), remote_sem=T.sem[sm],
+                                   srcs=[src], dsts=[dst] * len(ds)) for ds, es, sm, src, dst in trs]
+        op("G", lambda e: g.remote_dma_fused(calls, local_sem=T.sem.loc), cost, r, w, None, "remote")
 
-    IMG = ["img%d" % k for k in range(8)] + ["imgz0", "imgz1"]
+    nt = {"tf": 0, "tb": 0}
+
+    def tmp(buf):
+        nt[buf] += 64
+        return T[buf][:, nt[buf] - 64:nt[buf]], buf + str(nt[buf])
+
+    IMG = ["img%d" % k for k in range(8)] + ["imgz0", "imgz1"] + [("imgr", j) for j in range(CFG["rep"])]
     WIN = ["win0", "win1", "win2"]
-
-    def units(c0, c1):
-        return range(c0 // 8, (c1 + 7) // 8)
 
     def pieces(u0, u1):
         return [range(a, min(u1, a + CFG["piece"])) for a in range(u0, u1, CFG["piece"])]
 
     def offs(st, q):
-        return T.off[:, 192 * st + C0[q]:192 * st + C0[q] + W[q]], [("off", st, u) for u in units(C0[q], C0[q] + W[q])]
+        return T.off[:, 192 * st + 64 * q:192 * st + 64 * q + 64], [("off", st, u) for u in range(8 * q, 8 * q + 8)]
 
-    def gb(st, c0, c1, step=1):
-        return T.gb[:, 3072 * st + c0:3072 * st + c1:step] if step > 1 else T.gb[:, 3072 * st + c0:3072 * st + c1]
+    def gb(st, q, c0, c1, step=1):
+        a = 3072 * st + 1024 * q
+        return T.gb[:, a + c0:a + c1:step] if step > 1 else T.gb[:, a + c0:a + c1]
+
+    def got(st, q):
+        return [("g", st, u) for u in range(8 * q, 8 * q + 8)]
 
     def gather_call(eng, st, u0, u1):
         w = T.win[:, 0:4112] if st in (0, 2) else T.img[:, 0:8320]
         src = w.indirect(T.off[:, 192 * st + 8 * u0:192 * st + 8 * u1])
-        out = gb(st, 128 * u0, 128 * u1)
+        out = gb(st, 0, 128 * u0, 128 * u1)
         return V.tensor_copy(out, src) if eng == "V" else S.activation(out, src, F.Identity)
 
     def gather(st, u0, u1):
@@ -281,256 +367,281 @@ def rank_program(g, core, T, topo):
             op("VA", None, 60 + 128 * len(us) * CFG["gat"], (WIN if st in (0, 2) else IMG) + [("off", st, u) for u in us],
                [("g", st, u) for u in us], gat=[st, us[0], us[-1] + 1])
 
+    NP = 8192 - 512 * CFG["rep"]
+
     def img_load(k):
-        dma("Y", 262144, T.img[16 * k:16 * k + 16, 64:8256], T.cam[:, :], "dimg", (), ["img%d" % k])
+        dma(32 * NP, T.img[16 * k:16 * k + 16, 64:64 + NP], T.cam[:, 0:NP], "dimg", (), ["img%d" % k])
 
     kc = lambda j: T.kc[:, j:j + 1]
-    loc = [0]
+    pa = lambda j: T.pa[:, j:j + 1]
+    s0 = lambda q, e=None: T.s0[0:16, 128 * q:128 * q + 128] if e is None else T.s0[0:16, 128 * q + e:128 * q + 128:2]
+    sh = lambda q, e=None: T.sh[0:16, 128 * q:128 * q + 128] if e is None else T.sh[0:16, 128 * q + e:128 * q + 128:2]
+    lm = lambda e: T.lm[0:16, 128 * e:128 * e + 128]
+    zero = T.wp[:, 16:144]
 
-    dma("Y", 192, T.posei[0:8, 0:6], T.pose[:, :], "dpose", (), ["posei"])
-    dma("Y", 131072, T.lc[:, :], T.lens[:, :], "dlens", (), ["lc"])
+    dma(192, T.posei[0:8, 0:6], T.pose[:, :], "dpose", (), ["posei"])
+    dma(131072 + ROWS, T.lc[:, :], T.lens[:, :], "dlens", (), ["lc"])
+    if CFG["rep"]:
+        dma(32 * (8192 - NP), T.raw[0:16, 0:8192 - NP], T.cam[:, NP:8192], "draw", (), ["raw"])
     for k in range(CFG["early"]):
         img_load(k)
     iota(16, T.dj[:, 0:16], [[1, 16]], 128, -1, ["dj"], False)
-    iota(2, T.pc[:, 0:2], [[16, 2]], 0, 1, ["pc"], False)
-    iota(48, T.i12[:, 0:48], [[0, 12], [16, 4]], 0, 0, ["i1"])
-    iota(192, T.ones8[0:8, :], [[0, 192]], 1, 0, ["ones8"])
-    sel(128, T.rep[0:8, :], T.ones8[0:8, 0:128], [[1, 8], [0, 16]], -1, ["ones8"], ["rep"])
-    for q in range(NQ):
-        iota(W[q] // 4, T.i12[:, 48 + C0[q] // 4:48 + (C0[q] + W[q]) // 4], [[1, W[q] // 16], [0, 4]], C0[q] // 4, 0, [("i2", q)])
+    iota(128, T.ones[:, :], [[0, 128]], 1, 0, ["ones"])
+    sel(128, T.rep[0:8, :], T.ones[0:8, :], [[1, 8], [0, 16]], -1, ["ones"], ["rep"])
     iota(128, T.onesb[:, :], [[0, 128]], 1, 0, ["onesb"])
     sel(128, T.ident[:, :], T.onesb[:, :], [[-1, 128]], 1, ["onesb"], ["ident"])
-    iota(144, T.dz[:, :], [[1, 144]], 0, -1, ["dz"])
-    sel(192, T.m8[0:8, :], T.ones8[0:8, :], [[0, 24], [1, 8]], -1, ["ones8"], ["m8"])
-    iota(192, T.i16b[0:8, :], [[16, 24], [0, 8]], 0, 0, ["i16b"])
-    iota(128, T.f01[0:8, 0:128], [[0, 2], [8, 64]], 0, 0, ["f0"])
-    iota(128, T.f01[0:8, 128:256], [[8, 2], [0, 64]], 0, 0, ["f1"])
+    s0n = lambda q: "s0a" if q == 0 else "s0b"
+    for qs in ([0], [1, 2]):
+        for q in qs:
+            for h in range(2):
+                iota(64, T.s0[0:16, 128 * q + 64 * h:128 * q + 64 * h + 64], [[48 * dk, 4], [8, 2], [0, 8]], 16 * q + 48 * dh * h, 0, [s0n(q)])
+        iota(128 * len(qs), T.s0[0:8, 128 * qs[0]:128 * (qs[-1] + 1)], [[0, 16 * len(qs)], [64, 8]], 0, 8, [s0n(qs[0])])
+        if qs[0] == 0:
+            if CFG["rep"]:
+                sel(128, T.r16[0:16, :], T.onesb[0:16, :], [[0, 8], [1, 16]], -1, ["onesb"], ["r16"])
+            sel(64, T.sel[:, 0:64], T.onesb[:, 0:64], [[-1, 8], [-16, 8]], 1, ["onesb"], ["sel1"])
+    iota(192, T.wp[:, 16:208], [[0, 192]], 0, 0, ["wp"])
+    iota(64, T.img[:, 0:64], [[0, 64]], 0, 0, ["imgz0"])
+    iota(64, T.img[:, 8256:8320], [[0, 64]], 0, 0, ["imgz1"])
+    for q in range(NQ):
+        for e in range(2):
+            iota(64, T.ru[0:16, 128 * q + 64 * e:128 * q + 64 * e + 64], [[0, 8], [48 * dh, 2], [48 * dk, 4]], 16 * q + 8 * e, 0, [("ru", q)])
+        iota(128, T.ru[0:8, 128 * q:128 * q + 128], [[0, 2], [8, 8], [0, 8]], 0, 64, [("ru", q)])
+    sel(128, T.sel[:, 64:192], T.onesb[:, :], [[-16, 8], [-1, 8], [0, 2]], 1, ["onesb"], ["sel2"])
+    iota(16, T.wd[:, 128:144], [[0, 16]], 0, 0, ["wd0"])
 
-    ms(256, T.wp[:, :], 0.0, ["wp"])
-    ms(1024, T.win[:, 0:1024], 64.0, ["wina"])
-    ms(1040, T.win[:, 3072:4112], 64.0, ["wind"])
-    act(1024, T.win[:, 1024:2048], T.win[:, 0:1024], ["wina"], ["winb"])
-    act(1024, T.win[:, 2048:3072], T.win[:, 0:1024], ["wina"], ["winc"])
-    ts(16, T.dj[:, 16:32], T.dj[:, 0:16], 15, None, A.bitwise_and, None, ["dj"], ["dj2"])
+    ms(1040, T.win[:, 0:1040], 64.0, (), ["wina"])
+    ms(1008, T.win[:, 1040:2048], 64.0, (), ["winb"])
+    ms(1024, T.win[:, 2048:3072], 64.0, (), ["winc"])
+    lin(1040, T.win[:, 3072:4112], T.win[:, 0:1040], ["wina"], ["wind"], eng="A")
     ts(6, T.p8[0:8, 0:6], T.posei[0:8, 0:6], 1.0 / 32, None, A.mult, None, ["posei"], ["p8"])
-    mms(7, [(256, ps[7][:, 0:6], T.rep[0:8, :], T.p8[0:8, 0:6], True, True)], ["rep", "p8"])
-    ts(16, T.wp[:, 112:128], T.dj[:, 16:32], 0.0, None, A.is_equal, None, ["dj2"], ["wp"])
-    ts(256, T.tab[:, 0:256], T.lc[:, :], M32, M32 + 32.0, A.add, A.subtract, ["lc"], ["tab0"])
-    ts(1, T.hs[:, 0:1], ps[7][:, 4:5], 1.0 / 128, None, A.mult, None, (), ["hs"], 7)
+    mms(7, [(6, ps[7][:, 0:6], T.rep[0:8, :], T.p8[0:8, 0:6], True, True)], ["rep", "p8"], True)
+    lin(6, T.pa[:, 0:6], ps[7][:, 0:6], (), ["pa"], bank=7)
+    lin(1, T.hs[:, 0:1], pa(4), ["pa"], ["hs"], scale=1.0 / 128)
+    ts(256, T.tab[:, 0:256], T.lc[:, :], 1.0, None, A.mult, None, ["lc"], ["tab0"])
     tt(256, T.tab[:, 256:512], T.lc[:, :], T.tab[:, 0:256], A.subtract, ["lc", "tab0"], ["tab1"])
     ts(256, T.v0[:, :], T.lc[:, :], T.hs[:, 0:1], -0.5 + 1.0 / 8192, A.mult, A.add, ["lc", "hs"], ["v0"])
     ts(256, T.tab[:, 512:768], T.v0[:, :], -65.0, 64.0, A.max, A.min, ["v0"], ["tab2"])
     for t in range(3):
-        dma("Y", 65536, T.win[t:128:16, 1:4097], T.tab[:, 256 * t:256 * t + 256], "dtab",
+        dma(65536 + ROWS, T.win[t:128:16, 1:4097], T.tab[:, 256 * t:256 * t + 256], "dtab",
             ["tab%d" % t, "wina", "winb", "winc", "wind"], ["win%d" % t])
     for k in range(CFG["early"], 8):
         img_load(k)
 
-    act(6, T.pa[:, 0:6], ps[7][:, 0:6], (), ["pa"], bank=7)
-    act(1, kc(0), T.pa[:, 1:2], ["pa"], ["k0"], scale=-4.0)
-    act(1, kc(1), T.pa[:, 0:1], ["pa"], ["k1"], scale=4.0)
-    act(128, T.diag[:, 0:128], T.ident[:, :], ["ident", "k0"], ["dg0"], scale=kc(0))
-    act(128, T.diag[:, 128:256], T.ident[:, :], ["ident", "k1"], ["dg1"], scale=kc(1))
-    act(128, T.diag[:, 256:384], T.ident[:, :], ["ident", "pa"], ["dg2"], scale=T.pa[:, 0:1])
-    act(128, T.diag[:, 384:512], T.ident[:, :], ["ident", "pa"], ["dg3"], scale=T.pa[:, 1:2])
-    wpv = lambda s: T.wp[:, 112 - 16 * s:240 - 16 * s]
-    for b, d0, c, cn in ((6, 0, T.cz, "cz"), (1, 2, T.cx, "cx")):
-        mms(b, [(128, ps[b][:, 128 * h:128 * h + 128], wpv(2 * h + ch), T.diag[:, 128 * (d0 + ch):128 * (d0 + ch + 1)], ch == 0, ch == 1)
-                for h in range(4) for ch in range(2)], ["wp", "dg%d" % d0, "dg%d" % (d0 + 1)])
-        act(512, c[:, :], ps[b][:, :], (), [cn], bank=b)
-    act(1, kc(3), T.pa[:, 3:4], ["pa"], ["k3"], scale=4.0, bias=1.0 - 3.5 / 8)
-    act(192, T.h01[0:8, 0:192], T.m8[0:8, :], ["m8", "p8"], ["h0"], scale=T.p8[0:8, 0:1])
-    act(192, T.h01[0:8, 192:384], T.m8[0:8, :], ["m8", "p8"], ["h1"], scale=T.p8[0:8, 1:2])
-    act(192, T.h2[0:8, 0:192], T.i16b[0:8, :], ["i16b", "p8"], ["h2a"], scale=T.p8[0:8, 1:2], bias=T.p8[0:8, 2:3])
+    ts(16, T.dj[:, 16:32], T.dj[:, 0:16], 15, None, A.bitwise_and, None, ["dj"], ["dj2"])
+    for ch in range(2):
+        ts(16, T.d4[:, 16 * ch:16 * ch + 16], T.dj[:, 16:32], 0.0, 8.0 * ch - 4.0, A.is_equal, A.mult, ["dj2"], [("d4", ch)])
+    for e in range(2):
+        for ch in range(2):
+            a = 16 * e + 8 * ch
+            lin(8, T.lt[:, a:a + 8], T.d4[:, 16 * ch + 8 * e:16 * ch + 8 * e + 8], [("d4", ch), "pa"], [("lt", e, ch)], scale=pa(1 - ch))
+    mms(6, [(128, ps[6][0:16, 128 * e:128 * e + 128], T.lt[:, 16 * e:16 * e + 16], T.ident[:, :], True, True) for e in range(2)],
+        ["ident"] + [("lt", e, ch) for e in range(2) for ch in range(2)])
+    lin(256, T.lm[0:16, :], ps[6][0:16, 0:256], (), ["lm"], bank=6)
+    lin(1, kc(3), pa(3), ["pa"], ["k3"], scale=4.0, bias=1.0 - 3.5 / 8)
+    for b, qs in ((3, [0]), (6, [1, 2])):
+        mms(b, [(64, ps[b][:, 256 + 64 * q:320 + 64 * q], lm(e), s0(q, e), e == 0, e == 1) for q in qs for e in range(2)],
+            ["lm", s0n(qs[0])])
+        a, n = 64 * qs[0], 64 * len(qs)
+        ts(n, T.off[:, a:a + n], ps[b][:, 256 + a:256 + a + n], kc(3), 4097.0, A.add, A.min, ["k3"],
+           [x for q in qs for x in offs(0, q)[1]], b)
 
-    ts(1, T.pc[:, 2:3], T.pc[:, 0:1], 15, None, A.bitwise_and, None, ["pc"], ["pc2"])
-    ts(2, T.pc[:, 3:5], T.pc[:, 0:2], 1, 8, A.arith_shift_right, A.bitwise_and, ["pc"], ["pc3"])
-    ts(1, T.pc[:, 5:6], T.pc[:, 0:1], 5, None, A.arith_shift_right, None, ["pc"], ["pc5"])
-    ts(16, T.d16f[:, :], T.dj[:, 16:32], 0.0, None, A.is_equal, None, ["dj2"], ["d16f"])
-    cp(4, T.cf[:, 0:4], T.pc[:, 2:6], ["pc2", "pc3", "pc5"], ["cf"])
-    ts(48, T.i12[:, 96:144], T.i12[:, 0:48], T.cf[:, 0:1], T.cf[:, 2:3], A.add, A.mult, ["i1", "cf"], ["i3"])
-    for q in range(NQ):
-        a, b = C0[q] // 4, (C0[q] + W[q]) // 4
-        if W[q] not in W[:q]:
-            ts(1, T.cf[:, 4 + q:5 + q], T.cf[:, 3:4], float(W[q] // 16), None, A.mult, None, ["cf"], [("hn", W[q])])
-        j = 4 + W.index(W[q])
-        ts(b - a, T.i12[:, 144 + a:144 + b], T.i12[:, 48 + a:48 + b], T.cf[:, j:j + 1], T.cf[:, 1:2], A.add, A.mult,
-           [("i2", q), "cf", ("hn", W[q])], [("i4", q)])
-    ts(144, T.zm[:, :], T.dz[:, :], T.cf[:, 0:1], 15.0, A.add, A.is_equal, ["dz", "cf"], ["zm"])
-    tt(48, T.s0[:, :], T.i12[:, 96:144], T.i12[:, 144:192], A.add, ["i3"] + [("i4", q) for q in range(NQ)], ["s0"])
-    part = lambda buf, q: buf[:, C0[q] // 4:(C0[q] + W[q]) // 4]
-    for q in range(NQ):
-        n = W[q] // 4
-        b = 0 if q == 0 else 3
-        mms(b, [(n, ps[b][:, C0[q] + n * h:C0[q] + n * h + n], T.cz[:, 128 * h:128 * h + 128], part(T.s0, q), True, True) for h in range(4)],
-            ["cz", "s0"])
-    for b, a, e in ((0, 0, W[0]), (3, W[0], 192)):
-        ts(e - a, T.off[:, a:e], ps[b][:, a:e], kc(3), 4097.0, A.add, A.min, ["k3"], [("off", 0, u) for u in units(a, e)], b)
-    ts(1, kc(8), T.cf[:, 0:1], 2.0, 1.0 / 4096, A.is_lt, A.mult, ["cf"], ["k8"])
-    ts(1, kc(9), T.cf[:, 0:1], 2.0, 64.0, A.is_equal, A.mult, ["cf"], ["k9"])
-    tt(192, T.h2[0:8, 192:384], T.h2[0:8, 0:192], T.m8[0:8, :], A.mult, ["h2a", "m8"], ["h2"])
-    mms(5, [(192, ps[5][:, 0:192], T.f01[0:8, 0:128], T.h01[0:8, 0:192], True, False),
-            (192, ps[5][:, 0:192], T.f01[0:8, 128:256], T.h01[0:8, 192:384], False, False),
-            (768, ps[5][:, 0:192], T.ones8[0:8, 0:128], T.h2[0:8, 192:384], False, True)], ["f0", "h0", "f1", "h1", "ones8", "h2"])
-    g8 = T.zm[:, 15:143:16]
-    act(8, T.sb1[:, 0:16:2], g8, ["zm", "k8"], ["sb1a"], scale=kc(8))
-    act(8, T.sb1[:, 1:16:2], g8, ["zm", "k9"], ["sb1b"], scale=kc(9))
-    ms(64, T.img[:, 0:64], 0.0, ["imgz0"])
-    ms(64, T.img[:, 8256:8320], 0.0, ["imgz1"])
-    ts(192, T.xb[:, :], ps[5][:, 0:192], -15.5 / 32, None, A.add, None, (), ["xb"], 5)
-    act(1, kc(10), T.d16f[:, 15:16], ["d16f"], ["k10"], scale=-16.0)
-    act(1, kc(4), T.pa[:, 3:4], ["pa"], ["k4"], scale=-4.0)
-    act(1, kc(5), T.pa[:, 3:4], ["pa"], ["k5"], scale=-4.0, bias=0.875)
-    act(8, T.sb2[:, 0:24:3], g8, ["zm", "d16f"], ["sb2a"], scale=T.d16f[:, 0:1])
-    act(8, T.sb2[:, 1:24:3], g8, ["zm", "d16f"], ["sb2b"], scale=T.d16f[:, 1:2])
-    act(8, T.sb2[:, 2:24:3], g8, ["zm", "k10"], ["sb2c"], scale=kc(10))
-    act(1, kc(6), T.pa[:, 5:6], ["pa", "k4"], ["k6"], scale=-32.0, bias=kc(4))
-    act(1, kc(7), T.pa[:, 5:6], ["pa", "k5"], ["k7"], scale=32.0, bias=kc(5))
-    act(1, kc(11), kc(8), ["k8", "k9"], ["k11"], bias=kc(9))
-    act(1, kc(2), T.pa[:, 2:3], ["pa"], ["k2"], bias=-15.5 / 32)
-    act(144, T.wd[:, :], T.zm[:, :], ["zm", "k10"], ["wd"], scale=kc(10))
-    act(144, T.wl[:, :], T.zm[:, :], ["zm", "k11"], ["wl"], scale=kc(11))
-    act(128, T.identg[:, :], T.ident[:, :], ["ident"], ["identg"], scale=32768.0)
-    cp(64, T.identh[:, :], T.ident[:, :], ["ident"], ["identh"])
-    zero = T.wp[:, 128:256]
+    for j in range(CFG["rep"]):
+        mms(j % 2, [(512, ps[j % 2][:, :], T.r16[0:16, :], T.raw[0:16, 512 * j:512 * j + 512], True, True)], ["r16", "raw"])
+        lin(512, T.img[:, 64 + NP + 512 * j:576 + NP + 512 * j], ps[j % 2][:, :], (), [("imgr", j)], bank=j % 2)
+    ts(16, T.d16[:, :], T.dj[:, 16:32], 0.0, None, A.is_equal, None, ["dj2"], ["d16"])
+    lin(16, T.wp[:, 0:16], T.d16[:, :], ["d16"], ["d16b"])
+    for ch in range(2):
+        lin(8, T.lt[:, 32 + 8 * ch:40 + 8 * ch], T.d16[:, 0:8], ["d16", "pa"], [("lx", ch)], scale=pa(ch))
+    mms(4, [(64, ps[4][0:16, 0:64], T.lt[:, 32:48], T.sel[:, 0:64], True, True)], ["sel1", ("lx", 0), ("lx", 1)])
+    lin(64, T.cm[0:16, 0:64], ps[4][0:16, 0:64], (), ["cm1"], bank=4)
+    lin(1, kc(2), pa(2), ["pa"], ["k2"], bias=-15.5 / 32)
+    lin(64, T.cr[:, 0:64], T.sel[:, 0:64], ["sel1", "k2"], ["cr0"], scale=kc(2))
+    mms(5, [c for q in range(NQ) for c in ((256, ps[5][:, 64 * q:64 * q + 64], T.ones[:, :], T.cr[:, 0:64], True, False),
+                                           (64, ps[5][:, 64 * q:64 * q + 64], s0(q), T.cm[0:16, 0:64], False, True))],
+        ["ones", "cr0", "cm1", "s0a", "s0b"])
+    ts(192, T.xi[:, 0:192], ps[5][:, 0:192], 1.0, None, A.mult, None, (), ["xi"], 5)
+    mms(2, [(8, ps[2][:, 0:8], T.rep[0:8, :], T.rep[0:8, 0:128:16], True, True)], ["rep"], True)
+    g8 = ps[2][:, 0:8]
+    ts(1, kc(8), T.dj[:, 31:32], 13.0, 1.0 / 4096, A.is_gt, A.mult, ["dj2"], ["k8"])
+    lin(1, kc(9), T.d16[:, 2:3], ["d16"], ["k9"], scale=64.0)
+    lin(1, kc(10), T.d16[:, 15:16], ["d16"], ["k10"], scale=-16.0)
+    for t in range(2):
+        lin(8, T.sb1[:, t:16:2], g8, ["k%d" % (8 + t)], [("sb1", t)], scale=kc(8 + t), bank=2)
+    for t, col, nm in ((0, T.d16[:, 0:1], "d16"), (1, T.d16[:, 1:2], "d16"), (2, kc(10), "k10")):
+        lin(8, T.sb2[:, t:24:3], g8, [nm], [("sb2", t)], scale=col, bank=2)
+    lin(128, T.ig0[:, :], T.ident[:, :], ["ident"], ["idg0"], scale=16384.0)
+    lin(128, T.ig1[:, :], T.ident[:, :], ["ident"], ["idg1"], scale=-16384.0)
+    lin(1, kc(4), pa(3), ["pa"], ["k4"], scale=-4.0)
+    lin(1, kc(5), pa(3), ["pa"], ["k5"], scale=-4.0, bias=0.875)
+    lin(1, kc(6), pa(5), ["pa", "k4"], ["k6"], scale=-32.0, bias=kc(4))
+    lin(1, kc(7), pa(5), ["pa", "k5"], ["k7"], scale=32.0, bias=kc(5))
+
+    def second_constants(when):
+        mms(6, [(64, ps[6][0:16, 64 * j:64 * j + 64], T.lt[:, 32 - 32 * j:48 - 32 * j], T.sel[:, 64:192:2], True, True) for j in range(2)],
+            ["sel2", ("lx", 0), ("lx", 1), ("lt", 0, 0), ("lt", 0, 1)])
+        lin(128, T.cm[0:16, 64:192], ps[6][0:16, 0:128], [when], ["cm"], bank=6)
+        for j, k in enumerate((2, 6, 7)):
+            lin(128, T.cr[:, 64 + 128 * j:192 + 128 * j], T.sel[:, 64:192], ["sel2", "k%d" % k, when], [("cr", j)], scale=kc(k))
+        mms(7, [(384, ps[7][:, 0:384], T.ones[:, :], T.cr[:, 64:448], True, True)], ["ones"] + [("cr", j) for j in range(3)], True)
+        lin(384, T.ct[:, :], ps[7][:, 0:384], (), ["ct"], bank=7)
+        for t in range(2):
+            lin(8, T.sb3[:, 8 * t:8 * t + 8], T.sb1[:, t:16:2], [("sb1", t), when], [("sb3", t)])
+        lin(128, T.wd[:, 0:128], T.ident[:, :], ["ident", "k10", when], ["wd"], scale=kc(10))
+        lin(128, T.ig2[:, :], T.ident[:, :], ["ident", when], ["idg2"], scale=2.0 ** 27)
+        ms(720, T.tz[:, 0:720], 0.0, [when], ["tz"])
 
     for q in range(NQ):
-        w, c0, n = W[q], C0[q], W[q] // 4
-        u0, u1 = c0 // 8, (c0 + w) // 8
-        bl, be, bp = 2 + q % 2, 4 + q % 2, 6 + q % 2
-        gather(0, u0, u1)
-        for us in pieces(u0, u1):
-            mms(bl, [(16, ps[bl][:, 16 * (u - u0):16 * (u - u0 + 1)], gb(0, 128 * u, 128 * u + 128), T.sb1[:, :], True, True) for u in us],
-                [("g", 0, u) for u in us] + ["sb1a", "sb1b"])
-        (p, pn), (x, xn), (c, cn), (e, en), (s, sn), (t, tn), (d, dn), (m, mn) = [tmp(w) for _ in range(8)]
-        tt(w, p, ps[bl][:, 0:2 * w:2], T.xb[:, c0:c0 + w], A.mult, ["xb"], [pn], bl)
-        ts(w, x, p, -0.5 + 1.0 / 8192, MNEG, A.add, A.add, [pn], [xn])
-        ts(w, c, p, -32.0, 32.0 - 1.0 / 4096, A.max, A.min, [pn], [cn])
-        tt(w, s, ps[bl][:, 1:2 * w:2], x, A.add, [xn], [sn], bl)
-        tt(w, e, p, c, A.is_equal, [pn, cn], [en])
-        tt(w, t, s, e, A.mult, [sn, en], [tn])
+        bm, bu = q, 3 + q
+        (p, pn), (v, vn), (u, un), (c, cn), (d, dn), (m, mn) = [tmp(b) for b in ("tf", "tb", "tb", "tb", "tf", "tb")]
+        gather(0, 8 * q, 8 * q + 8)
+        mms(bm, [(16, ps[bm][:, 16 * r:16 * r + 16], gb(0, q, r, 1024, 8), T.sb1[:, :], True, True) for r in range(8)],
+            got(0, q) + [("sb1", 0), ("sb1", 1)])
+        tt(64, p, ps[bm][:, 0:128:2], T.xi[:, 64 * q:64 * q + 64], A.mult, ["xi"], [pn], bm)
+        lin(64, v, ps[bm][:, 1:128:2], [pn], [vn], bank=bm)
+        ts(64, u, p, ROUND, None, A.add, None, [pn], [un])
+        ts(32, c, u, 160.0, 223.0, A.max, A.min, [un], [cn])
+        s = ps[bu][:, 0:64]
+        mms(bu, [(64, s, T.ident[:, :], v, True, False)], ["ident", vn])
+        mms(bu, [(64, s, T.ig0[:, :], u, False, False)], ["idg0", un])
+        mms(bu, [(64, s, T.ig1[:, :], c, False, False), (64, s, T.ident[:, :], c, False, True)], ["idg1", "ident", cn])
         o, on = offs(1, q)
-        ts(w, o, t, KOFF, LAST, A.add, A.min, [tn], on)
-        mms(be, [(3 * w, ps[be][:, 0:3 * w], zero, T.cz[:, 0:3 * w], True, False)]
-            + [(n, ps[be][:, 3 * n * h + 2:3 * n * (h + 1):3], T.cz[:, 128 * h:128 * h + 128], part(T.s0, q), False, False) for h in range(4)],
-            ["wp", "cz", "s0"])
-        gather(1, u0, u1)
-        for us in pieces(u0, u1):
-            mms(be, [(24, ps[be][:, 24 * (u - u0):24 * (u - u0 + 1)], gb(1, 128 * u, 128 * u + 128), T.sb2[:, :], False, u == u1 - 1)
-                     for u in us], [("g", 1, u) for u in us] + ["sb2a", "sb2b", "sb2c"])
-        ts(w, d, ps[be][:, 2:3 * w:3], kc(6), kc(7), A.max, A.min, ["k6", "k7"], [dn], be)
-        tt(w, m, ps[be][:, 2:3 * w:3], d, A.is_equal, [dn], [mn], be)
+        ts(64, o, s, BASE, LAST, A.add, A.min, (), on, bu)
+        z = ps[bu][:, 2:192:3]
+        mms(bu, [(192, ps[bu][:, 0:192], zero, T.wp[:, 16:208], True, False)]
+            + [(64, z, lm(e), T.ru[0:16, 128 * q + 64 * e:128 * q + 64 * e + 64], False, False) for e in range(2)], ["wp", "lm", ("ru", q)])
+        gather(1, 8 * q, 8 * q + 8)
+        for us in pieces(0, 8):
+            mms(bu, [(24, ps[bu][:, 24 * r:24 * r + 24], gb(1, q, 128 * r, 128 * r + 128), T.sb2[:, :], False, r == 7) for r in us],
+                [("g", 1, 8 * q + r) for r in us] + [("sb2", t) for t in range(3)])
+        ts(64, d, z, kc(6), kc(7), A.max, A.min, ["k6", "k7"], [dn], bu)
+        tt(64, m, z, d, A.is_equal, [dn], [mn], bu)
         for ch in range(2):
-            tt(w, T.mt[:, 192 * ch + c0:192 * ch + c0 + w], ps[be][:, ch:3 * w:3], m, A.mult, [mn], [("mt", q, ch)], be)
-        for ch in range(2):
-            a = 192 * ch + c0
-            mms(bp, [(n, ps[bp][:, 0:n], wpv(2 * h + ch), T.mt[:, a + n * h:a + n * h + n], ch == 0 and h == 0, ch == 1 and h == 3)
-                     for h in range(4)], ["wp", ("mt", q, ch)])
-        piece = x1_part(T, q, rank)
-        cp(n, piece, ps[bp][:, 0:n], (), [("x1own", q)], bp)
-        trs = [RemoteDMATransfer(dst_ids=[dst_id(topo, d, core) for d in ds], dma_engine_mask=mask_of(es), remote_sem=sm,
-                                 srcs=[piece], dsts=[piece] * len(ds))
-               for ds, es, sm in ((hl, in_e, T.sem["r%d" % q]), (near, out_e, T.sem["xa%d" % q]))]
-        for some in ([trs[:1], trs[1:]] if q == 0 else [trs]):
-            op("G", lambda some=some: g.remote_dma_fused(some, local_sem=T.sem.loc), 800, [("x1own", q)], [("sent", q)], None, "remote")
-        loc[0] += len(in_e) + len(out_e)
-        op(None, None, 0, [("sent", q)], [("way", q)], late=CFG["lat0"] if q == 0 else CFG["lat"], nbytes=-1 if q == 0 else 0)
-        op(None, None, 0, [("way", q), ("x1in", q - 1)], [("x1in", q)], late=600.0, arrive=("xb%d" % q, len(far) * (len(out_e) // 2)))
-        op(None, None, 0, [("sent", q)], [("x1near", q)], late=CFG["lat"] / 2, arrive=("xa%d" % q, len(near) * len(out_e)))
+            a = 128 * q + 64 * ch
+            tt(64, T.mt[:, a:a + 64], ps[bu][:, ch:192:3], m, A.mult, [mn], [("mt", q, ch)], bu)
+        mms(bu, [(16, ps[bu][:, 256:272], T.mt[:, 128 * q:128 * q + 128], T.wp[:, 0:16], True, True)], ["d16b", ("mt", q, 0), ("mt", q, 1)])
+        lin(16, part(T.x1, [q], rank), ps[bu][:, 256:272], (), [("x1own", q)], bank=bu)
+        if q == CFG["when"]:
+            second_constants(("x1own", q))
+        qs = group(G1, q)
+        if q != qs[-1]:
+            continue
+        piece, own = part(T.x1, qs, rank), [("x1own", x) for x in qs]
+        direct = (near, out_e, "xa%d" % q, piece, piece)
+        if qs[0] == 0:
+            send([([hl[0]], in_e, "r%d" % q, piece, piece), ([hl[1]], out_e, "r%d" % q, piece, piece)], own, [("sent", q)])
+            send([direct], own, [("sentn", q)])
+        else:
+            send([(hl, in_e, "r%d" % q, piece, piece), direct], own, [("sent", q), ("sentn", q)])
+        op(None, None, 0, [("sent", q)], [("way", q)], late=CFG["lat0"] if qs[0] == 0 else CFG["lat"], nbytes=-1 if qs[0] == 0 else 0)
+        op(None, None, 0, [("way", q), ("x1in", qs[0] - 1)], [("x1in", q)], late=CFG["gap"], arrive=("xb%d" % q, len(far) * (len(out_e) // 2)))
+        op(None, None, 0, [("sentn", q)], [("x1near", q)], late=CFG["latn"], arrive=("xa%d" % q, len(near) * len(out_e)))
 
-    def turn(b, a, c, q, closed):
-        n = W[q] // 4
-        return [(n, ps[b][:, a + n * h:a + n * h + n], c[:, 128 * h:128 * h + 128], part(T.sg, q), closed, closed) for h in range(4)]
+    def share(src, dst):
+        ds = [d for d in T.cores if d != src and topo.may_write(src, d)]
+        n = len(out_e) // 2
+        return [out_e, out_e[:n], out_e[n:]][ds.index(dst)]
 
-    def keep_mm(b, wm, wn, st, q, start):
-        mms(b, [(W[q], ps[b][:, 0:W[q]], wm[:, 15 - k:143 - k], gb(st, 16 * C0[q] + k, 16 * (C0[q] + W[q]), 16), start and k == 0, k == 15)
-                for k in range(16)], [wn] + [("g", st, u) for u in units(C0[q], C0[q] + W[q])])
+    bank_of = lambda h: 5 if h == hfar else 6
 
-    def groups(src):
-        late = sorted(T.cores[4:], key=lambda d: d == src or topo.may_write(src, d))
-        return [sorted(T.cores[a:a + 2], key=lambda d: d == src or topo.may_write(src, d)) for a in (0, 2)] + [late[:2], late[2:]]
+    def heights(h, k, q, a):
+        b = bank_of(h)
+        return (16, ps[b][:, 48 * k + q:48 * k + 48:3], gb(4, 0, a, a - a % 2 + 256, 2), T.wp[:, 0:16], True, True)
 
-    def direct(src, dst):
-        return [[d for d in ds if d != src and topo.may_write(src, d)] for ds in groups(src) if dst in ds][0]
-
-    ways = {"fa": [], "fb": []}
-
-    def final(k):
-        trs, rs = [], []
-        for i, d in enumerate(groups(core)[k]):
-            rd = T.rank_of(d)
-            b = 6 + i
-            gather(4, 3 * rd, 3 * rd + 3)
-            mms(b, [(16, ps[b][:, 256 + j:304:3], gb(4, 128 * (3 * rd + j), 128 * (3 * rd + j + 1)), T.wp[:, 112:128], True, True)
-                    for j in range(3)], ["wp"] + [("g", 4, 3 * rd + j) for j in range(3)])
-            buf = T.x2 if d == core else T.fs
-            cp(48, buf[:, 48 * rd:48 * rd + 48], ps[b][:, 256:304], (), [("fs", rd)], b)
-            src = T.fs[:, 48 * rd:48 * rd + 48]
-            if d in far:
-                j = far.index(d)
-                es = (in_e, out_e)[i]
-                trs.append(RemoteDMATransfer(dst_ids=[dst_id(topo, hl[j % 2], core)], dma_engine_mask=mask_of(es),
-                                             remote_sem=T.sem["s%d" % (j // 2)], src=src, dst=T.rl[:, 48 * (j // 2):48 * (j // 2) + 48]))
-            elif d in near:
-                m = len(out_e) // len(direct(core, d))
-                j = direct(core, d).index(d)
-                es = out_e[m * j:m * j + m]
-                trs.append(RemoteDMATransfer(dst_ids=[dst_id(topo, d, core)], dma_engine_mask=mask_of(es), remote_sem=T.sem.fa,
-                                             src=src, dst=T.x2[:, 48 * rank:48 * rank + 48]))
-            if d != core:
-                rs.append(("fs", rd))
-                loc[0] += len(es)
-                ways["fb" if d in far else "fa"].append(("fsent", k))
-        op("G", lambda: g.remote_dma_fused(trs, local_sem=T.sem.loc), 800, rs, [("fsent", k)], None, "remote")
-
-    done = 0
-    for q in range(NQ):
-        w, c0, n = W[q], C0[q], W[q] // 4
-        u0, u1 = c0 // 8, (c0 + w) // 8
-        bs, bl, be = q % 2, 2 + (NQ + q) % 2, (4 + (NQ + q) % 2 if q < 2 else (q + 1) % 2)
-        for ds, res in (([core] + near, [("x1near", q), ("x1own", q)]), (far, [("x1in", q)])):
-            mms(bs, [(n, ps[bs][:, 256:256 + n], T.ident[:, :], x1_part(T, q, T.rank_of(d)), d == core, d == far[-1]) for d in ds],
+    for qs, bb, bs, bz in (([0], 7, 0, 0), ([1, 2], 1, 3, 4)):
+        n, q0 = len(qs), qs[0]
+        w, ba = 64 * n, 3 * q0
+        for ds, res in (([core] + near, [("x1near", qs[-1])] + [("x1own", x) for x in qs]), (far, [("x1in", qs[-1])])):
+            mms(ba, [(16 * n, ps[ba][:, 128:128 + 16 * n], T.ident[:, :], part(T.x1, qs, T.rank_of(d)), d == core, d == far[-1]) for d in ds],
                 ["ident"] + res)
-        ts(n, part(T.sh, q), ps[bs][:, 256:256 + n], -31.0, 31.0, A.max, A.min, (), [("sh", q)], bs)
-        tt(n, part(T.sg, q), part(T.sh, q), part(T.s0, q), A.add, [("sh", q), "s0"], [("sg", q)])
-        mms(bs, turn(bs, 0, T.cz, q, True), ["cz", ("sg", q)])
-        o, on = offs(2, q)
-        ts(w, o, ps[bs][:, 0:w], kc(3), 4097.0, A.add, A.min, ["k3"], on, bs)
-        mms(be, [(w, ps[be][:, 0:w], zero, T.cz[:, 0:w], True, False)] + turn(be, 0, T.cz, q, False), ["wp", "cz", ("sg", q)])
-        mms(bl, turn(bl, 256, T.cx, q, True), ["cx", ("sg", q)])
-        xi, vi = T.tmi[:, c0:c0 + w], T.tmi[:, 192 + c0:192 + c0 + w]
-        ts(w, xi, ps[bl][:, 256:256 + w], kc(2), None, A.add, None, ["k2"], [("x", q)], bl)
-        gather(2, u0, u1)
-        keep_mm(bl, T.wl, "wl", 2, q, True)
-        (m, mn), (p, pn), (x, xn), (s, sn), (c, cn), (d, dn), (e, en), (t, tn) = [tmp(w) for _ in range(8)]
-        ts(w, vi, ps[bl][:, 0:w], -0.5, None, A.add, None, (), [("vi", q)], bl)
-        tt(w, m, ps[bl][:, 0:w], vi, A.subtract, [("vi", q)], [mn], bl)
-        tt(w, p, m, xi, A.mult, [mn, ("x", q)], [pn])
-        ts(w, x, p, -0.5 + 1.0 / 8192, MNEG, A.add, A.add, [pn], [xn])
-        tt(w, s, x, vi, A.add, [xn, ("vi", q)], [sn])
-        o, on = offs(3, q)
-        ts(w, o, s, KOFF, LAST, A.add, A.min, [sn], on)
-        ts(w, c, p, -32.0, 32.0 - 1.0 / 4096, A.max, A.min, [pn], [cn])
-        tt(w, T.ne[:, c0:c0 + w], p, c, A.not_equal, [pn, cn], [("ne", q)])
-        mms(be, [(w, ps[be][:, 0:w], T.identg[:, :], T.ne[:, c0:c0 + w], False, False)], ["identg", ("ne", q)])
-        gather(3, u0, u1)
-        keep_mm(be, T.wd, "wd", 3, q, False)
-        ts(w, d, ps[be][:, 0:w], kc(6), kc(7), A.max, A.min, ["k6", "k7"], [dn], be)
-        tt(w, e, ps[be][:, 0:w], d, A.is_equal, [dn], [en], be)
-        tt(w, t, s, e, A.mult, [sn, en], [tn])
-        o, on = offs(4, q)
-        ts(w, o, t, KOFF, LAST, A.add, A.min, [tn], on)
-        while done < 4 and (48, 96, 192, 192)[done] <= c0 + w:
-            final(done)
-            done += 1
+        ts(16 * n, T.xc[:, 16 * q0:16 * (q0 + n)], ps[ba][:, 128:128 + 16 * n], -31.0, 31.0, A.max, A.min, (), [("xc", q0)], ba)
+        for q in qs:
+            b = ba + q - q0
+            mms(b, [(16, ps[b][0:16, 16 * c:16 * c + 16], T.ident[:, c:128:8], T.xc[:, 16 * q:16 * q + 16], True, True) for c in range(8)],
+                ["ident", ("xc", q0)], least=20)
+            tt(128, sh(q), ps[b][0:16, 0:128], s0(q), A.add, [s0n(q)], [("sh", q)], b)
+            mms(b, [(64, ps[b][:, 256:320], lm(e), sh(q, e), e == 0, e == 1) for e in range(2)], ["lm", ("sh", q)])
+            o, on = offs(2, q)
+            ts(64, o, ps[b][:, 256:320], kc(3), 4097.0, A.add, A.min, ["k3"], on, b)
+            gather(2, 8 * q, 8 * q + 8)
+        shn = [("sh", q) for q in qs]
+        ct = lambda j: T.ct[:, 128 * j:128 * j + 128:2 // n]
+        mms(bb, [(64, ps[bb][:, 256 + q - q0:256 + w:n], sh(q), T.cm[0:16, 64:128], True, True) for q in qs], ["cm"] + shn)
+        x = T.xi[:, 192 + 64 * q0:192 + 64 * q0 + w]
+        tt(w, x, ps[bb][:, 256:256 + w], ct(0), A.add, ["ct"], [("x", q0)], bb)
+        for q in qs:
+            mms(bb, [(16, ps[bb][:, n * r + q - q0:2 * w:8 * n], gb(2, q, r, 1024, 8), T.sb3[:, :], True, True) for r in range(8)],
+                got(2, q) + [("sb3", 0), ("sb3", 1)])
+        c0 = lambda j: 144 * j + 720 * q0
+        tile = lambda j: T.tz[:, c0(j) + 2 - n:c0(j) + 130 - n:2 // n]
+        tn = lambda j: ("tz", q0, j)
+        p, pn = T.tf[:, 384 + 64 * q0:384 + 64 * q0 + w], ("p", q0)
+        tt(w, p, ps[bb][:, 0:w], x, A.mult, [("x", q0)], [pn], bb)
+        lin(w, tile(0), ps[bb][:, w:2 * w], [pn, "tz"], [tn(0)], bank=bb)
+        ts(w, tile(1), p, ROUND, None, A.add, None, [pn, "tz"], [tn(1)])
+        ts(w // 2, tile(2), tile(1), 160.0, 223.0, A.max, A.min, [tn(1), "tz"], [tn(2)])
 
-    op(None, None, 0, ways["fa"], ["fa"], late=CFG["lat"] / 2, arrive=("fa", sum(len(out_e) // len(direct(d, core)) for d in near)))
-    op(None, None, 0, ways["fb"], ["fb"], late=CFG["lat"], arrive=("fb", len(far) * len(out_e)))
-    for ds, res in (([core], ("fs", rank)), (near, "fa"), (far, "fb")):
-        mms(1, [(128, ps[1][0:48, 384:512], T.x2[:, 48 * T.rank_of(d):48 * T.rank_of(d) + 48], T.identh[:, :], d == core, d == far[-1])
-                for d in ds], ["identh", res])
-    act(128, T.yo[0:48, :], ps[1][0:48, 384:512], (), ["yo"], bank=1)
-    dma("Y", 24576, T.y[:, :], T.yo[0:48, :], "dy", ["yo"], ["y"])
+        def turned(b, terms, start, stop):
+            calls = []
+            for j, m, mn in terms:
+                for e in range(2 // n):
+                    calls.append((w, ps[b][:, 0:w], T.tz[:, c0(j) + 2 - n - e:c0(j) + 130 - n - e], m[:, w * e:w * e + w],
+                                  start and not calls, False))
+            calls[-1] = calls[-1][:5] + (stop,)
+            mms(b, calls, [x for j, m, mn in terms for x in (tn(j), mn)])
+
+        if n == 1:
+            mms(bs, [(w, ps[bs][:, 0:w], T.ident[:, :], tile(j), j == 0, j == 1) for j in range(2)], ["ident", tn(0), tn(1)])
+        else:
+            turned(bs, [(0, T.ident, "ident")], True, False)
+            turned(bs, [(1, T.ident, "ident")], False, True)
+        on = lambda st: [x for q in qs for x in offs(st, q)[1]]
+        ts(w, T.off[:, 576 + 64 * q0:576 + 64 * q0 + w], ps[bs][:, 0:w], BASE, LAST, A.add, A.min, (), on(3), bs)
+        z = ps[bz][:, 0:w]
+        mms(bz, ([(w, z, zero, T.ident[:, :], True, False)] if n == 2 else [])
+            + [(64, ps[bz][:, q - q0:w:n], sh(q), T.cm[0:16, 128:192], n == 1, False) for q in qs], ["cm", "wp", "ident"] + shn)
+        turned(bb, [(0, T.ident, "ident")], True, False)
+        turned(bb, [(1, T.ig0, "idg0")], False, False)
+        turned(bb, [(2, T.ig1, "idg1"), (2, T.ident, "ident")], False, False)
+        gather(3, 8 * q0, 8 * (q0 + n))
+        if n == 1:
+            mms(bz, [(64, z, T.wd[:, 15 - k:143 - k], gb(3, 0, k, 1024, 16), False, k == 15) for k in range(16)], ["wd", "wd0"] + got(3, 0))
+        else:
+            mms(bz, [(8, ps[bz][:, k:w:16], gb(3, q0, k, 2048, 16), T.sb2[:, 2:24:3], False, k == 15) for k in range(16)],
+                [("sb2", 2)] + got(3, 1) + got(3, 2))
+        for j, cmp in ((1, A.is_lt), (2, A.is_gt)):
+            tt(w, tile(2 + j), z, ct(j), cmp, ["ct", "tz"], [tn(2 + j)], bz)
+            turned(bb, [(2 + j, T.ig2, "idg2")], False, j == 2)
+        ts(w, T.off[:, 768 + 64 * q0:768 + 64 * q0 + w], ps[bb][:, 0:w], BASE, LAST, A.add, A.min, (), on(4), bb)
+        if n == 1:
+            gather(4, 0, 8)
+            for k in range(4):
+                for h in (hfar, 1 - hfar):
+                    mms(bank_of(h), [heights(h, k, 0, 256 * k + h)], ["d16b", ("g", 4, 2 * k), ("g", 4, 2 * k + 1)])
+            continue
+        for h in (hfar, 1 - hfar):
+            b, a = bank_of(h), 0 if h == hfar else 192
+            gather(4, 8 + 8 * h, 16 + 8 * h)
+            for k in range(4):
+                mms(b, [heights(h, k, 1 + j, 1024 + 1024 * h + 256 * k + j) for j in range(2)],
+                    ["d16b", ("g", 4, 8 + 8 * h + 2 * k), ("g", 4, 9 + 8 * h + 2 * k)])
+            ts(192, T.fs[:, a:a + 192], ps[b][:, 0:192], 1.0, None, A.mult, None, (), [("fs", a)], b)
+            if h == hfar:
+                send([([hl[i]], es, "s", T.fs[:, 96 * i:96 * i + 96], T.rl[:, :]) for i, es in enumerate((in_e, out_e))], [("fs", a)], ["fsent"])
+                op(None, None, 0, ["fsent"], ["fb"], late=CFG["latf"], arrive=("fb", len(far) * (len(out_e) // 2)))
+            else:
+                trs = [([T.cores[r]], share(core, T.cores[r]), "fa", T.fs[:, a + 48 * k:a + 48 * k + 48], part(T.x2, range(NQ), rank))
+                       for k, r in enumerate(half[h]) if r != rank]
+                send(trs[:1], [("fs", a)], ["nsent1"])
+                send(trs[1:], [("fs", a)], ["nsent"])
+                op(None, None, 0, ["nsent"], ["fa"], late=CFG["latn"], arrive=("fa", sum(len(share(d, core)) for d in near)))
+
+    a = 192 + 48 * half[1 - hfar].index(rank)
+    for ds, res in (([core], ("fs", 192)), (far, "fb"), (near, "fa")):
+        mms(7, [(128, ps[7][0:48, 0:128], T.fs[:, a:a + 48] if d == core else part(T.x2, range(NQ), T.rank_of(d)), T.ident[:, :],
+                 d == core, d == near[-1]) for d in ds], ["ident", res])
+    lin(128, T.yo[0:48, :], ps[7][0:48, 0:128], (), ["yo"], bank=7)
+    dma(24576 + ROWS * 3 // 8, T.y[:, :], T.yo[0:48, :], "dy", ["yo"], ["y"])
     op("Y", None, 0, ["y"], ())
 
     order = schedule(ops)
@@ -540,7 +651,7 @@ def rank_program(g, core, T, topo):
         o, j = ops[i], prev.get(ops[i]["eng"])
         a = ops[j]["gat"] if j is not None else None
         b = o["gat"]
-        if a and b and a[0] == b[0] and a[2] == b[1] and b[2] - a[1] <= CFG["merge"] and b[0] != 4 and \
+        if a and b and a[0] == b[0] and a[2] == b[1] and b[2] - a[1] <= CFG["merge"][o["eng"]] and \
                 all(first[d] < first[j] for d in o["deps"]):
             a[2] = b[2]
             ops[j]["deps"] = ops[j]["deps"] | o["deps"]
@@ -594,7 +705,7 @@ def rank_program(g, core, T, topo):
         elif o["fn"] is None:
             continue
         else:
-            ins = o["fn"]()
+            ins = o["fn"](o["eng"])
         if o["dma"] not in (None, "remote"):
             ins.then_inc(T.sem[o["dma"]], 16)
         elif i in needed:

@@ -5,21 +5,21 @@ from concourse.mybir import AluOpType as A, ActivationFunctionType as F
 
 CFG = {"piece": 2, "merge": {"V": 4, "A": 6}, "delta": 300.0, "early": 3, "lat0": 3600.0, "lat": 3100.0, "gap": 1000.0, "latn": 2600.0,
        "latf": 3600.0, "gat": 1.62, "pe": 0.7, "bw": 350.0, "tries": 60000, "heat": 120.0, "seed": 1, "dma": 1100.0, "call": 350.0,
-       "call0": 1650.0, "mean": 0.1, "when": 2, "d2": 60.0, "rep": 4}
+       "call0": 1650.0, "mean": 0.1, "when": 2, "d2": 60.0, "rep": 4, "p1a": [[0], [1], [2]], "p1": [[0], [1], [2]], "split": 1, "stagger": 1, "pq": "A", "hi": "V"}
 G1 = [[0], [1, 2]]
 ROWS = 98000
 CASES = ((0.7, 1.0, 1.0, 1.0, 1.0, 0.83), (0.57, 0.8, 0.85, 0.85, 0.85, 0.8), (1.2, 1.4, 1.4, 1.3, 1.5, 1.1))
 WEIGHTS = (0.5, 0.3, 0.2)
-WAKE, FIX = 90.0, 42.0
+WAKE, FIX = 100.0, 42.0
 FOUND = {}
 NQ = 3
 B, H, W32, I32 = "bfloat16", "float16", "float32", "int32"
 SCRATCH = {n: ("sbuf", [128, c], d) for n, c, d in (
     ("img", 8320, B), ("win", 4112, B), ("posei", 8, I32), ("p8", 8, W32), ("pa", 8, W32), ("kc", 16, W32), ("hs", 4, W32),
-    ("lc", 256, I32), ("v0", 256, I32), ("tab", 768, B), ("dj", 32, I32), ("d16", 16, W32), ("d4", 32, B), ("wp", 208, B),
+    ("lc", 256, I32), ("v0", 256, I32), ("tab", 768, B), ("dj", 32, I32), ("wp", 144, B),
     ("ones", 128, W32), ("rep", 128, W32), ("onesb", 128, B), ("ident", 128, B), ("ig0", 128, B), ("ig1", 128, B), ("ig2", 128, B),
     ("sel", 192, B), ("lt", 48, B), ("lm", 256, B), ("cm", 192, B), ("s0", 384, B), ("ru", 384, B), ("wd", 144, B),
-    ("sb1", 16, B), ("sb2", 24, B), ("sb3", 16, B), ("cr", 448, W32), ("ct", 384, W32), ("xi", 384, I32),
+    ("sb1", 16, B), ("sb2", 32, B), ("sb3", 16, B), ("cr", 448, W32), ("ct", 384, W32), ("xi", 384, I32),
     ("off", 960, "uint16"), ("gb", 15360, B), ("tf", 576, W32), ("tb", 768, B), ("tz", 1440, B), ("mt", 384, B), ("x1", 384, B),
     ("raw", 4096, B), ("r16", 128, B), ("xc", 48, B), ("sh", 384, H), ("fs", 384, H), ("x2", 384, H), ("rl", 96, H), ("yo", 128, W32))}
 for _b in range(8):
@@ -69,7 +69,7 @@ def helper_program(g, core, owner, far, i, T, topo):
     steps = [("r%d" % qs[-1], "xb%d" % qs[-1], [part(T.x1, qs, r)] * 2, part(T.x1, qs, r)) for qs in G1]
     steps.append(("s", "fb", [T.rl[:, 0:48], T.rl[:, 48:96]], part(T.x2, range(NQ), r)))
     for came, sem, src, dst in steps:
-        g.wait_ge(T.sem[came], n_in)
+        g.wait_ge(T.sem[came], 2 * n_in if came == "s" and CFG["stagger"] else n_in)
         g.remote_dma_fused([RemoteDMATransfer(dst_ids=[dst_id(topo, d, core)], dma_engine_mask=mask_of(engs[j * half:(j + 1) * half]),
                                               remote_sem=T.sem[sem], src=src[j], dst=dst)
                             for j, d in enumerate(far[2 * i:2 * i + 2])], local_sem=T.sem.loc)
@@ -86,7 +86,10 @@ def lengths(ops, case):
 def plan(ops, pre, succ, prio, size):
     cost, late, load = size
     n = len(ops)
-    left = [len(p) for p in pre]
+    left = [0] * n
+    for s in succ:
+        for j, _ in s:
+            left[j] += 1
     free, at, eng, order, line = {}, [0.0] * n, [o["eng"] for o in ops], [], 0.0
     ready = [i for i in range(n) if left[i] == 0]
     while ready:
@@ -111,6 +114,37 @@ def plan(ops, pre, succ, prio, size):
             if left[j] == 0:
                 ready.append(j)
     return order, eng
+
+
+def quick(order, eng, succ, size, gat):
+    cost, late, load = size
+    n = len(eng)
+    free, last, at, line, end = {"V": 0.0, "A": 0.0, "P": 0.0, "G": 0.0, "Y": 0.0}, {"V": None, "A": None}, [0.0] * n, 0.0, 0.0
+    for i in order:
+        e, t1 = eng[i], at[i]
+        if e:
+            f, c = free[e], cost[i]
+            if e == "V" or e == "A":
+                a, b = last[e], gat[i]
+                if b and a and a[0] == b[0] and a[2] == b[1] and t1 < f - c:
+                    f -= FIX
+                last[e] = b
+                if e == "A":
+                    c += 15.0
+            t1 = free[e] = (f if f > t1 else t1) + c
+        if load[i]:
+            line = max(line, t1 + late[i] * 0.6) + load[i]
+            fin = line + late[i] * 0.4
+        else:
+            fin = t1 + late[i]
+        if fin > end:
+            end = fin
+        fin += WAKE
+        for j, kind in succ[i]:
+            t = t1 if kind else fin
+            if t > at[j]:
+                at[j] = t
+    return end + CFG["mean"] * sum(at) / n
 
 
 def replay(order, eng, succ, size, gat, trace=None):
@@ -172,6 +206,12 @@ def schedule(ops):
         pre.append(set(o["deps"]) | set(o["after"]))
         for j in pre[i]:
             succ[j].append((i, j not in o["deps"] or (o["eng"] == "P" and ops[j]["eng"] == "P")))
+    below = [set() for _ in range(n)]
+    for i in range(n - 1, -1, -1):
+        for j, _ in succ[i]:
+            below[i] |= below[j] | {j}
+        far = set().union(*[below[j] for j, _ in succ[i]])
+        succ[i] = [(j, kind) for j, kind in succ[i] if j not in far or ops[i]["late"]]
     sizes = [lengths(ops, c) for c in CASES]
     base = [0.0] * n
     for i in range(n - 1, -1, -1):
@@ -180,8 +220,8 @@ def schedule(ops):
     if n not in FOUND:
         order, eng = plan(ops, pre, succ, base, sizes[0])
         gat = [o["gat"] for o in ops]
-        value = lambda order, eng: sum(w * replay(order, eng, succ, s, gat) for w, s in zip(WEIGHTS, sizes))
-        free = [i for i, o in enumerate(ops) if o["eng"] in ("V", "A", "VA", "P")]
+        value = lambda order, eng: sum(w * quick(order, eng, succ, s, gat) for w, s in zip(WEIGHTS, sizes))
+        free = [i for i, o in enumerate(ops) if o["eng"] in ("V", "A", "VA", "P", "G")]
         now = value(order, eng)
         best = (now, order, eng)
         rng = np.random.RandomState(CFG["seed"])
@@ -192,11 +232,13 @@ def schedule(ops):
                 trace = {}
                 replay(order, eng, succ, sizes[0 if r[7] < 0.6 else 1 if r[7] < 0.8 else 2], gat, trace)
                 order = sorted(order, key=lambda i: trace["start"][i])
-                held = [(j, i) for j, i in trace["held"] if ops[i]["eng"] not in ("G", "Y")]
+                held = [(j, i) for j, i in trace["held"] if ops[i]["eng"] != "Y"]
             other, e2 = list(order), list(eng)
             if held and r[0] < 0.5:
                 j, i = held[int(r[1] * len(held))]
                 a = (i, j)[r[2] < 0.5]
+                if order.index(j) > order.index(i):
+                    continue
                 if ops[a]["eng"] == "VA" and r[3] < 0.5:
                     e2[a] = "V" if eng[a] == "A" else "A"
                 elif a == i:
@@ -231,7 +273,9 @@ def schedule(ops):
                 other.insert(lo if r[4] < 0.2 else hi if r[4] > 0.8 else lo + int(r[5] * (hi + 1 - lo)), i)
             got = value(other, e2)
             if got <= now - CFG["heat"] * (1 - k / CFG["tries"]) * math.log(r[6] + 1e-12):
-                now, order, eng, held = got, other, e2, None
+                now, order, eng = got, other, e2
+                if r[5] < 0.25:
+                    held = None
                 if got < best[0]:
                     best = (got, other, e2)
         FOUND[n] = best
@@ -283,7 +327,7 @@ def rank_program(g, core, T, topo):
             last_w[x] = i
             readers[x] = []
         after = []
-        if eng in ("G", "Y"):
+        if eng == "Y" or dma == "remote":
             if eng in last_q:
                 after.append(last_q[eng])
             last_q[eng] = i
@@ -319,11 +363,11 @@ def rank_program(g, core, T, topo):
         else:
             op("G", lambda e: g.iota(out, pat, base, cm), 130 + 2 * n * 0.87, (), w)
 
-    def sel(n, out, a, pat, cm, r, w):
-        op("G", lambda e: g.affine_select(out, a, pat, A.is_equal, 0.0, 0, cm), 170 + 2 * n * 0.87, r, w)
+    def sel(n, out, a, pat, cm, r, w, base=0, cmp=A.is_equal):
+        op("G", lambda e: g.affine_select(out, a, pat, cmp, 0.0, base, cm), 170 + 2 * n * 0.87, r, w)
 
-    def dma(nbytes, out, a, sem, r, w):
-        op("Y", lambda e: Y.dma_start(out, a), 60, r, w, None, sem, late=CFG["dma"], nbytes=nbytes)
+    def dma(nbytes, out, a, sem, r, w, eng="Y"):
+        op(eng, lambda e: queue[e].dma_start(out, a), 60, r, w, None, sem, late=CFG["dma"], nbytes=nbytes)
 
     loc = [0]
 
@@ -336,9 +380,9 @@ def rank_program(g, core, T, topo):
 
     nt = {"tf": 0, "tb": 0}
 
-    def tmp(buf):
-        nt[buf] += 64
-        return T[buf][:, nt[buf] - 64:nt[buf]], buf + str(nt[buf])
+    def tmp(buf, w):
+        nt[buf] += w
+        return T[buf][:, nt[buf] - w:nt[buf]], buf + str(nt[buf])
 
     IMG = ["img%d" % k for k in range(8)] + ["imgz0", "imgz1"] + [("imgr", j) for j in range(CFG["rep"])]
     WIN = ["win0", "win1", "win2"]
@@ -377,9 +421,9 @@ def rank_program(g, core, T, topo):
     s0 = lambda q, e=None: T.s0[0:16, 128 * q:128 * q + 128] if e is None else T.s0[0:16, 128 * q + e:128 * q + 128:2]
     sh = lambda q, e=None: T.sh[0:16, 128 * q:128 * q + 128] if e is None else T.sh[0:16, 128 * q + e:128 * q + 128:2]
     lm = lambda e: T.lm[0:16, 128 * e:128 * e + 128]
-    zero = T.wp[:, 16:144]
+    zero = T.wp[0:16, 16:144]
 
-    dma(192, T.posei[0:8, 0:6], T.pose[:, :], "dpose", (), ["posei"])
+    dma(192, T.posei[0:8, 0:6], T.pose[:, :], "dpose", (), ["posei"], CFG["pq"])
     dma(131072 + ROWS, T.lc[:, :], T.lens[:, :], "dlens", (), ["lc"])
     if CFG["rep"]:
         dma(32 * (8192 - NP), T.raw[0:16, 0:8192 - NP], T.cam[:, NP:8192], "draw", (), ["raw"])
@@ -394,19 +438,27 @@ def rank_program(g, core, T, topo):
     for qs in ([0], [1, 2]):
         for q in qs:
             for h in range(2):
-                iota(64, T.s0[0:16, 128 * q + 64 * h:128 * q + 64 * h + 64], [[48 * dk, 4], [8, 2], [0, 8]], 16 * q + 48 * dh * h, 0, [s0n(q)])
-        iota(128 * len(qs), T.s0[0:8, 128 * qs[0]:128 * (qs[-1] + 1)], [[0, 16 * len(qs)], [64, 8]], 0, 8, [s0n(qs[0])])
+                iota(64, T.s0[0:16, 128 * q + 64 * h:128 * q + 64 * h + 64], [[48 * dk, 4], [8, 2], [0, 8]], 16 * q + 48 * dh * h, 0, [("s0y", q, h)])
+        iota(128 * len(qs), T.s0[0:8, 128 * qs[0]:128 * (qs[-1] + 1)], [[0, 16 * len(qs)], [64, 8]], 0, 8,
+             [s0n(qs[0])] + [("s0y", q, h) for q in qs for h in range(2)])
         if qs[0] == 0:
             if CFG["rep"]:
                 sel(128, T.r16[0:16, :], T.onesb[0:16, :], [[0, 8], [1, 16]], -1, ["onesb"], ["r16"])
             sel(64, T.sel[:, 0:64], T.onesb[:, 0:64], [[-1, 8], [-16, 8]], 1, ["onesb"], ["sel1"])
-    iota(192, T.wp[:, 16:208], [[0, 192]], 0, 0, ["wp"])
+    sel(8, T.sb1[:, 0:16:2], T.onesb[:, 0:8], [[-16, 8]], 1, ["onesb"], [("sb1", 0)], cmp=A.is_ge)
+    iota(8, T.sb1[:, 1:16:2], [[0, 8]], 64, 0, [("sb1", 1)])
+    sel(8, T.sb1[:, 0:16:2], T.sb1[:, 0:16:2], [[16, 8]], -1, (), [("sb1", 0)], base=1, cmp=A.is_ge)
+    sel(8, T.sb1[:, 1:16:2], T.sb1[:, 1:16:2], [[-16, 8]], 1, (), [("sb1", 1)], base=-2)
+    iota(27, T.sb2[:, 0:27], [[0, 27]], 1, 0, ["sb2"])
+    iota(128, zero, [[0, 128]], 0, 0, ["wp"])
+    iota(9, T.sb2[:, 0:27:3], [[0, 9]], -16, 0, ["sb2"])
+    sel(27, T.sb2[:, 0:27], T.sb2[:, 0:27], [[-16, 9], [-1, 3]], 1, (), ["sb2"], base=1)
     iota(64, T.img[:, 0:64], [[0, 64]], 0, 0, ["imgz0"])
     iota(64, T.img[:, 8256:8320], [[0, 64]], 0, 0, ["imgz1"])
     for q in range(NQ):
         for e in range(2):
-            iota(64, T.ru[0:16, 128 * q + 64 * e:128 * q + 64 * e + 64], [[0, 8], [48 * dh, 2], [48 * dk, 4]], 16 * q + 8 * e, 0, [("ru", q)])
-        iota(128, T.ru[0:8, 128 * q:128 * q + 128], [[0, 2], [8, 8], [0, 8]], 0, 64, [("ru", q)])
+            iota(64, T.ru[0:16, 128 * q + 64 * e:128 * q + 64 * e + 64], [[0, 8], [48 * dh, 2], [48 * dk, 4]], 16 * q + 8 * e, 0, [("ruy", q, e)])
+        iota(128, T.ru[0:8, 128 * q:128 * q + 128], [[0, 2], [8, 8], [0, 8]], 0, 64, [("ru", q), ("ruy", q, 0), ("ruy", q, 1)])
     sel(128, T.sel[:, 64:192], T.onesb[:, :], [[-16, 8], [-1, 8], [0, 2]], 1, ["onesb"], ["sel2"])
     iota(16, T.wd[:, 128:144], [[0, 16]], 0, 0, ["wd0"])
 
@@ -418,23 +470,24 @@ def rank_program(g, core, T, topo):
     mms(7, [(6, ps[7][:, 0:6], T.rep[0:8, :], T.p8[0:8, 0:6], True, True)], ["rep", "p8"], True)
     lin(6, T.pa[:, 0:6], ps[7][:, 0:6], (), ["pa"], bank=7)
     lin(1, T.hs[:, 0:1], pa(4), ["pa"], ["hs"], scale=1.0 / 128)
-    ts(256, T.tab[:, 0:256], T.lc[:, :], 1.0, None, A.mult, None, ["lc"], ["tab0"])
+    lin(256, T.tab[:, 0:256], T.lc[:, :], ["lc"], ["tab0"], eng=CFG["hi"])
     tt(256, T.tab[:, 256:512], T.lc[:, :], T.tab[:, 0:256], A.subtract, ["lc", "tab0"], ["tab1"])
     ts(256, T.v0[:, :], T.lc[:, :], T.hs[:, 0:1], -0.5 + 1.0 / 8192, A.mult, A.add, ["lc", "hs"], ["v0"])
     ts(256, T.tab[:, 512:768], T.v0[:, :], -65.0, 64.0, A.max, A.min, ["v0"], ["tab2"])
-    for t in range(3):
+    for t in ((0, 1, 2) if CFG["hi"] == "V" else (0, 2, 1)):
         dma(65536 + ROWS, T.win[t:128:16, 1:4097], T.tab[:, 256 * t:256 * t + 256], "dtab",
             ["tab%d" % t, "wina", "winb", "winc", "wind"], ["win%d" % t])
     for k in range(CFG["early"], 8):
         img_load(k)
 
     ts(16, T.dj[:, 16:32], T.dj[:, 0:16], 15, None, A.bitwise_and, None, ["dj"], ["dj2"])
+    ts(16, T.wp[:, 0:16], T.dj[:, 16:32], 0.0, None, A.is_equal, None, ["dj2"], ["d16b"])
     for ch in range(2):
-        ts(16, T.d4[:, 16 * ch:16 * ch + 16], T.dj[:, 16:32], 0.0, 8.0 * ch - 4.0, A.is_equal, A.mult, ["dj2"], [("d4", ch)])
+        lin(1, kc(ch), pa(1 - ch), ["pa"], ["k%d" % ch], scale=8.0 * ch - 4.0)
     for e in range(2):
         for ch in range(2):
             a = 16 * e + 8 * ch
-            lin(8, T.lt[:, a:a + 8], T.d4[:, 16 * ch + 8 * e:16 * ch + 8 * e + 8], [("d4", ch), "pa"], [("lt", e, ch)], scale=pa(1 - ch))
+            lin(8, T.lt[:, a:a + 8], T.wp[:, 8 * e:8 * e + 8], ["d16b", "k%d" % ch], [("lt", e, ch)], scale=kc(ch))
     mms(6, [(128, ps[6][0:16, 128 * e:128 * e + 128], T.lt[:, 16 * e:16 * e + 16], T.ident[:, :], True, True) for e in range(2)],
         ["ident"] + [("lt", e, ch) for e in range(2) for ch in range(2)])
     lin(256, T.lm[0:16, :], ps[6][0:16, 0:256], (), ["lm"], bank=6)
@@ -449,27 +502,15 @@ def rank_program(g, core, T, topo):
     for j in range(CFG["rep"]):
         mms(j % 2, [(512, ps[j % 2][:, :], T.r16[0:16, :], T.raw[0:16, 512 * j:512 * j + 512], True, True)], ["r16", "raw"])
         lin(512, T.img[:, 64 + NP + 512 * j:576 + NP + 512 * j], ps[j % 2][:, :], (), [("imgr", j)], bank=j % 2)
-    ts(16, T.d16[:, :], T.dj[:, 16:32], 0.0, None, A.is_equal, None, ["dj2"], ["d16"])
-    lin(16, T.wp[:, 0:16], T.d16[:, :], ["d16"], ["d16b"])
     for ch in range(2):
-        lin(8, T.lt[:, 32 + 8 * ch:40 + 8 * ch], T.d16[:, 0:8], ["d16", "pa"], [("lx", ch)], scale=pa(ch))
+        lin(8, T.lt[:, 32 + 8 * ch:40 + 8 * ch], T.wp[:, 0:8], ["d16b", "pa"], [("lx", ch)], scale=pa(ch))
     mms(4, [(64, ps[4][0:16, 0:64], T.lt[:, 32:48], T.sel[:, 0:64], True, True)], ["sel1", ("lx", 0), ("lx", 1)])
     lin(64, T.cm[0:16, 0:64], ps[4][0:16, 0:64], (), ["cm1"], bank=4)
-    lin(1, kc(2), pa(2), ["pa"], ["k2"], bias=-15.5 / 32)
-    lin(64, T.cr[:, 0:64], T.sel[:, 0:64], ["sel1", "k2"], ["cr0"], scale=kc(2))
+    lin(64, T.cr[:, 0:64], T.sel[:, 0:64], ["sel1", "pa"], ["cr0"], scale=pa(2))
     mms(5, [c for q in range(NQ) for c in ((256, ps[5][:, 64 * q:64 * q + 64], T.ones[:, :], T.cr[:, 0:64], True, False),
                                            (64, ps[5][:, 64 * q:64 * q + 64], s0(q), T.cm[0:16, 0:64], False, True))],
         ["ones", "cr0", "cm1", "s0a", "s0b"])
-    ts(192, T.xi[:, 0:192], ps[5][:, 0:192], 1.0, None, A.mult, None, (), ["xi"], 5)
-    mms(2, [(8, ps[2][:, 0:8], T.rep[0:8, :], T.rep[0:8, 0:128:16], True, True)], ["rep"], True)
-    g8 = ps[2][:, 0:8]
-    ts(1, kc(8), T.dj[:, 31:32], 13.0, 1.0 / 4096, A.is_gt, A.mult, ["dj2"], ["k8"])
-    lin(1, kc(9), T.d16[:, 2:3], ["d16"], ["k9"], scale=64.0)
-    lin(1, kc(10), T.d16[:, 15:16], ["d16"], ["k10"], scale=-16.0)
-    for t in range(2):
-        lin(8, T.sb1[:, t:16:2], g8, ["k%d" % (8 + t)], [("sb1", t)], scale=kc(8 + t), bank=2)
-    for t, col, nm in ((0, T.d16[:, 0:1], "d16"), (1, T.d16[:, 1:2], "d16"), (2, kc(10), "k10")):
-        lin(8, T.sb2[:, t:24:3], g8, [nm], [("sb2", t)], scale=col, bank=2)
+    ts(192, T.xi[:, 0:192], ps[5][:, 0:192], -15.5 / 32, None, A.add, None, (), ["xi"], 5)
     lin(128, T.ig0[:, :], T.ident[:, :], ["ident"], ["idg0"], scale=16384.0)
     lin(128, T.ig1[:, :], T.ident[:, :], ["ident"], ["idg1"], scale=-16384.0)
     lin(1, kc(4), pa(3), ["pa"], ["k4"], scale=-4.0)
@@ -481,6 +522,8 @@ def rank_program(g, core, T, topo):
         mms(6, [(64, ps[6][0:16, 64 * j:64 * j + 64], T.lt[:, 32 - 32 * j:48 - 32 * j], T.sel[:, 64:192:2], True, True) for j in range(2)],
             ["sel2", ("lx", 0), ("lx", 1), ("lt", 0, 0), ("lt", 0, 1)])
         lin(128, T.cm[0:16, 64:192], ps[6][0:16, 0:128], [when], ["cm"], bank=6)
+        lin(1, kc(2), pa(2), ["pa", when], ["k2"], bias=-15.5 / 32)
+        ts(1, kc(10), T.dj[:, 31:32], 0.0, -16.0, A.is_equal, A.mult, ["dj2", when], ["k10"])
         for j, k in enumerate((2, 6, 7)):
             lin(128, T.cr[:, 64 + 128 * j:192 + 128 * j], T.sel[:, 64:192], ["sel2", "k%d" % k, when], [("cr", j)], scale=kc(k))
         mms(7, [(384, ps[7][:, 0:384], T.ones[:, :], T.cr[:, 64:448], True, True)], ["ones"] + [("cr", j) for j in range(3)], True)
@@ -491,37 +534,47 @@ def rank_program(g, core, T, topo):
         lin(128, T.ig2[:, :], T.ident[:, :], ["ident", when], ["idg2"], scale=2.0 ** 27)
         ms(720, T.tz[:, 0:720], 0.0, [when], ["tz"])
 
-    for q in range(NQ):
-        bm, bu = q, 3 + q
-        (p, pn), (v, vn), (u, un), (c, cn), (d, dn), (m, mn) = [tmp(b) for b in ("tf", "tb", "tb", "tb", "tf", "tb")]
-        gather(0, 8 * q, 8 * q + 8)
-        mms(bm, [(16, ps[bm][:, 16 * r:16 * r + 16], gb(0, q, r, 1024, 8), T.sb1[:, :], True, True) for r in range(8)],
-            got(0, q) + [("sb1", 0), ("sb1", 1)])
-        tt(64, p, ps[bm][:, 0:128:2], T.xi[:, 64 * q:64 * q + 64], A.mult, ["xi"], [pn], bm)
-        lin(64, v, ps[bm][:, 1:128:2], [pn], [vn], bank=bm)
-        ts(64, u, p, ROUND, None, A.add, None, [pn], [un])
-        ts(32, c, u, 160.0, 223.0, A.max, A.min, [un], [cn])
-        s = ps[bu][:, 0:64]
-        mms(bu, [(64, s, T.ident[:, :], v, True, False)], ["ident", vn])
-        mms(bu, [(64, s, T.ig0[:, :], u, False, False)], ["idg0", un])
-        mms(bu, [(64, s, T.ig1[:, :], c, False, False), (64, s, T.ident[:, :], c, False, True)], ["idg1", "ident", cn])
-        o, on = offs(1, q)
-        ts(64, o, s, BASE, LAST, A.add, A.min, (), on, bu)
-        z = ps[bu][:, 2:192:3]
-        mms(bu, [(192, ps[bu][:, 0:192], zero, T.wp[:, 16:208], True, False)]
-            + [(64, z, lm(e), T.ru[0:16, 128 * q + 64 * e:128 * q + 64 * e + 64], False, False) for e in range(2)], ["wp", "lm", ("ru", q)])
-        gather(1, 8 * q, 8 * q + 8)
-        for us in pieces(0, 8):
-            mms(bu, [(24, ps[bu][:, 24 * r:24 * r + 24], gb(1, q, 128 * r, 128 * r + 128), T.sb2[:, :], False, r == 7) for r in us],
-                [("g", 1, 8 * q + r) for r in us] + [("sb2", t) for t in range(3)])
-        ts(64, d, z, kc(6), kc(7), A.max, A.min, ["k6", "k7"], [dn], bu)
-        tt(64, m, z, d, A.is_equal, [dn], [mn], bu)
-        for ch in range(2):
-            a = 128 * q + 64 * ch
-            tt(64, T.mt[:, a:a + 64], ps[bu][:, ch:192:3], m, A.mult, [mn], [("mt", q, ch)], bu)
-        mms(bu, [(16, ps[bu][:, 256:272], T.mt[:, 128 * q:128 * q + 128], T.wp[:, 0:16], True, True)], ["d16b", ("mt", q, 0), ("mt", q, 1)])
-        lin(16, part(T.x1, [q], rank), ps[bu][:, 256:272], (), [("x1own", q)], bank=bu)
-        if q == CFG["when"]:
+    for qs in CFG["p1a"]:
+        n, q0, q = len(qs), qs[0], qs[-1]
+        w, bm, bu = 64 * n, q0, 3 + q0
+        (p, pn), (v, vn), (u, un), (c, cn) = [tmp(b, w) for b in ("tf", "tb", "tb", "tb")]
+        for x in qs:
+            gather(0, 8 * x, 8 * x + 8)
+            a = 128 * (x - q0)
+            mms(bm, [(16, ps[bm][:, a + 16 * r:a + 16 * r + 16], gb(0, x, r, 1024, 8), T.sb1[:, :], True, True) for r in range(8)],
+                got(0, x) + [("sb1", 0), ("sb1", 1)])
+        tt(w, p, ps[bm][:, 0:2 * w:2], T.xi[:, 64 * q0:64 * q0 + w], A.mult, ["xi"], [pn], bm)
+        lin(w, v, ps[bm][:, 1:2 * w:2], [pn], [vn], bank=bm)
+        ts(w, u, p, 1.0 / 4096, ROUND, A.mult, A.add, [pn], [un])
+        ts(w // 2, c, u, 160.0, 223.0, A.max, A.min, [un], [cn])
+        s = ps[bu][:, 0:w]
+        mms(bu, [(w, s, T.ident[:, :], v, True, False)], ["ident", vn])
+        mms(bu, [(w, s, T.ig0[:, :], u, False, False)], ["idg0", un])
+        mms(bu, [(w, s, T.ig1[:, :], c, False, False), (w, s, T.ident[:, :], c, False, True)], ["idg1", "ident", cn])
+        ts(w, T.off[:, 192 + 64 * q0:192 + 64 * q0 + w], s, BASE, LAST, A.add, A.min, (), [y for x in qs for y in offs(1, x)[1]], bu)
+    for qs in CFG["p1"]:
+        n, q0, q = len(qs), qs[0], qs[-1]
+        w, bu = 64 * n, 3 + q0
+        (d, dn), (m, mn) = tmp("tf", w), tmp("tb", w)
+        z = ps[bu][:, 2:3 * w:3]
+        mms(bu, [(3 * w, ps[bu][:, 0:3 * w], zero, T.s0[0:16, 0:3 * w], True, False)]
+            + [(64, ps[bu][:, 192 * (x - q0) + 2:192 * (x - q0 + 1):3], lm(e), T.ru[0:16, 128 * x + 64 * e:128 * x + 64 * e + 64], False, False)
+               for x in qs for e in range(2)], ["wp", "lm", "s0a", "s0b"] + [("ru", x) for x in qs])
+        gather(1, 8 * q0, 8 * q + 8)
+        for us in pieces(0, 8 * n):
+            mms(bu, [(24, ps[bu][:, 24 * r:24 * r + 24], gb(1, q0, 128 * r, 128 * r + 128), T.sb2[:, 1:25], False, r == 8 * n - 1) for r in us],
+                [("g", 1, 8 * q0 + r) for r in us] + ["sb2"])
+        ts(w, d, z, kc(6), kc(7), A.max, A.min, ["k6", "k7"], [dn], bu)
+        tt(w, m, z, d, A.is_equal, [dn], [mn], bu)
+        for x in qs:
+            a = nt["tb"] - w + 64 * (x - q0)
+            for ch in range(2):
+                tt(64, T.mt[:, 128 * x + 64 * ch:128 * x + 64 * ch + 64], ps[bu][:, 192 * (x - q0) + ch:192 * (x - q0 + 1):3], T.tb[:, a:a + 64],
+                   A.mult, [mn], [("mt", x, ch)], bu)
+        mms(bu, [(16, ps[bu][:, 384 + 16 * (x - q0):400 + 16 * (x - q0)], T.mt[:, 128 * x:128 * x + 128], T.wp[:, 0:16], True, True) for x in qs],
+            ["d16b"] + [("mt", x, ch) for x in qs for ch in range(2)])
+        lin(16 * n, part(T.x1, qs, rank), ps[bu][:, 384:384 + 16 * n], (), [("x1own", x) for x in qs], bank=bu)
+        if CFG["when"] in qs:
             second_constants(("x1own", q))
         qs = group(G1, q)
         if q != qs[-1]:
@@ -542,10 +595,10 @@ def rank_program(g, core, T, topo):
         n = len(out_e) // 2
         return [out_e, out_e[:n], out_e[n:]][ds.index(dst)]
 
-    bank_of = lambda h: 5 if h == hfar else 6
+    bank_of = lambda h, k: 6 if h != hfar else 0 if k > 1 and CFG["stagger"] else 5
 
     def heights(h, k, q, a):
-        b = bank_of(h)
+        b = bank_of(h, k)
         return (16, ps[b][:, 48 * k + q:48 * k + 48:3], gb(4, 0, a, a - a % 2 + 256, 2), T.wp[:, 0:16], True, True)
 
     for qs, bb, bs, bz in (([0], 7, 0, 0), ([1, 2], 1, 3, 4)):
@@ -578,7 +631,7 @@ def rank_program(g, core, T, topo):
         p, pn = T.tf[:, 384 + 64 * q0:384 + 64 * q0 + w], ("p", q0)
         tt(w, p, ps[bb][:, 0:w], x, A.mult, [("x", q0)], [pn], bb)
         lin(w, tile(0), ps[bb][:, w:2 * w], [pn, "tz"], [tn(0)], bank=bb)
-        ts(w, tile(1), p, ROUND, None, A.add, None, [pn, "tz"], [tn(1)])
+        ts(w, tile(1), p, 1.0 / 4096, ROUND, A.mult, A.add, [pn, "tz"], [tn(1)])
         ts(w // 2, tile(2), tile(1), 160.0, 223.0, A.max, A.min, [tn(1), "tz"], [tn(2)])
 
         def turned(b, terms, start, stop):
@@ -597,34 +650,58 @@ def rank_program(g, core, T, topo):
             turned(bs, [(1, T.ident, "ident")], False, True)
         on = lambda st: [x for q in qs for x in offs(st, q)[1]]
         ts(w, T.off[:, 576 + 64 * q0:576 + 64 * q0 + w], ps[bs][:, 0:w], BASE, LAST, A.add, A.min, (), on(3), bs)
-        z = ps[bz][:, 0:w]
-        mms(bz, ([(w, z, zero, T.ident[:, :], True, False)] if n == 2 else [])
-            + [(64, ps[bz][:, q - q0:w:n], sh(q), T.cm[0:16, 128:192], n == 1, False) for q in qs], ["cm", "wp", "ident"] + shn)
-        turned(bb, [(0, T.ident, "ident")], True, False)
-        turned(bb, [(1, T.ig0, "idg0")], False, False)
-        turned(bb, [(2, T.ig1, "idg1"), (2, T.ident, "ident")], False, False)
-        gather(3, 8 * q0, 8 * (q0 + n))
         if n == 1:
+            z = ps[bz][:, 0:w]
+            mms(bz, [(64, z, sh(0), T.cm[0:16, 128:192], True, False)], ["cm"] + shn)
+            turned(bb, [(0, T.ident, "ident")], True, False)
+            turned(bb, [(1, T.ig0, "idg0")], False, False)
+            turned(bb, [(2, T.ig1, "idg1"), (2, T.ident, "ident")], False, False)
+            gather(3, 0, 8)
             mms(bz, [(64, z, T.wd[:, 15 - k:143 - k], gb(3, 0, k, 1024, 16), False, k == 15) for k in range(16)], ["wd", "wd0"] + got(3, 0))
-        else:
-            mms(bz, [(8, ps[bz][:, k:w:16], gb(3, q0, k, 2048, 16), T.sb2[:, 2:24:3], False, k == 15) for k in range(16)],
-                [("sb2", 2)] + got(3, 1) + got(3, 2))
-        for j, cmp in ((1, A.is_lt), (2, A.is_gt)):
-            tt(w, tile(2 + j), z, ct(j), cmp, ["ct", "tz"], [tn(2 + j)], bz)
-            turned(bb, [(2 + j, T.ig2, "idg2")], False, j == 2)
-        ts(w, T.off[:, 768 + 64 * q0:768 + 64 * q0 + w], ps[bb][:, 0:w], BASE, LAST, A.add, A.min, (), on(4), bb)
-        if n == 1:
+            for j, cmp in ((1, A.is_lt), (2, A.is_gt)):
+                tt(w, tile(2 + j), z, ct(j), cmp, ["ct", "tz"], [tn(2 + j)], bz)
+                turned(bb, [(2 + j, T.ig2, "idg2")], False, j == 2)
+            ts(w, T.off[:, 768:832], ps[bb][:, 0:w], BASE, LAST, A.add, A.min, (), on(4), bb)
             gather(4, 0, 8)
             for k in range(4):
                 for h in (hfar, 1 - hfar):
-                    mms(bank_of(h), [heights(h, k, 0, 256 * k + h)], ["d16b", ("g", 4, 2 * k), ("g", 4, 2 * k + 1)])
+                    mms(bank_of(h, k), [heights(h, k, 0, 256 * k + h)], ["d16b", ("g", 4, 2 * k), ("g", 4, 2 * k + 1)])
             continue
+        cuts = [(64 * h, 64 * h + 64) for h in (hfar, 1 - hfar)] if CFG["split"] else [(0, 128)]
+        for (lo, hi), bz, bo in zip(cuts, (4, 2), (1, 3)):
+            m, us = hi - lo, range(8 + lo // 8, 8 + hi // 8)
+            z = ps[bz][lo:hi, 0:128]
+
+            def add(terms, start, stop):
+                mms(bo, [(m, ps[bo][:, 0:m], T.tz[lo:hi, c0(j):c0(j) + 128], x[lo:hi, lo:hi], start and i == 0, stop and i == len(terms) - 1)
+                         for i, (j, x, xn, tj) in enumerate(terms)], [y for t in terms for y in t[2:]])
+
+            mms(bz, [(128, z, T.wp[0:16, 16:16 + m], s0(0), True, False)]
+                + [(64, ps[bz][lo:hi, q - q0:128:2], T.sh[0:16, 128 * q + lo:128 * q + hi], T.cm[0:16, 128:192], False, False) for q in qs],
+                ["cm", "wp"] + shn)
+            add([(0, T.ident, "ident", tn(0)), (1, T.ig0, "idg0", tn(1))], True, False)
+            add([(2, T.ig1, "idg1", tn(2)), (2, T.ident, "ident", tn(2))], False, False)
+            gather(3, us[0], us[-1] + 1)
+            mms(bz, [(8, ps[bz][lo:hi, k:128:16], gb(3, 1, 16 * lo + k, 16 * hi, 16), T.sb2[:, 3:25:3], False, k == 15) for k in range(16)],
+                ["sb2"] + [("g", 3, u) for u in us])
+            for j, cmp in ((1, A.is_lt), (2, A.is_gt)):
+                tt(128, T.tz[lo:hi, c0(2 + j):c0(2 + j) + 128], z, T.ct[lo:hi, 128 * j:128 * j + 128], cmp, ["ct"], [("ne", lo, j)], bz)
+                add([(2 + j, T.ig2, "idg2", ("ne", lo, j))], False, j == 2)
+            ts(m, T.off[:, 832 + lo:832 + hi], ps[bo][:, 0:m], BASE, LAST, A.add, A.min, (), [("off", 4, u) for u in us], bo)
         for h in (hfar, 1 - hfar):
-            b, a = bank_of(h), 0 if h == hfar else 192
+            a = 0 if h == hfar else 192
             gather(4, 8 + 8 * h, 16 + 8 * h)
             for k in range(4):
-                mms(b, [heights(h, k, 1 + j, 1024 + 1024 * h + 256 * k + j) for j in range(2)],
+                mms(bank_of(h, k), [heights(h, k, 1 + j, 1024 + 1024 * h + 256 * k + j) for j in range(2)],
                     ["d16b", ("g", 4, 8 + 8 * h + 2 * k), ("g", 4, 9 + 8 * h + 2 * k)])
+            if h == hfar and CFG["stagger"]:
+                for i in range(2):
+                    b = bank_of(h, 2 * i)
+                    ts(96, T.fs[:, 96 * i:96 * i + 96], ps[b][:, 96 * i:96 * i + 96], 1.0, None, A.mult, None, (), [("fs", i)], b)
+                    send([([hl[i]], in_e + out_e, "s", T.fs[:, 96 * i:96 * i + 96], T.rl[:, :])], [("fs", i)], [("fsent", i)])
+                op(None, None, 0, [("fsent", 1)], ["fb"], late=CFG["latf"] - 300, arrive=("fb", len(far) * (len(out_e) // 2)))
+                continue
+            b = bank_of(h, 0)
             ts(192, T.fs[:, a:a + 192], ps[b][:, 0:192], 1.0, None, A.mult, None, (), [("fs", a)], b)
             if h == hfar:
                 send([([hl[i]], es, "s", T.fs[:, 96 * i:96 * i + 96], T.rl[:, :]) for i, es in enumerate((in_e, out_e))], [("fs", a)], ["fsent"])
@@ -637,9 +714,9 @@ def rank_program(g, core, T, topo):
                 op(None, None, 0, ["nsent"], ["fa"], late=CFG["latn"], arrive=("fa", sum(len(share(d, core)) for d in near)))
 
     a = 192 + 48 * half[1 - hfar].index(rank)
-    for ds, res in (([core], ("fs", 192)), (far, "fb"), (near, "fa")):
+    for ds, res in (([core], ("fs", 192)), (near, "fa"), (far, "fb")):
         mms(7, [(128, ps[7][0:48, 0:128], T.fs[:, a:a + 48] if d == core else part(T.x2, range(NQ), T.rank_of(d)), T.ident[:, :],
-                 d == core, d == near[-1]) for d in ds], ["ident", res])
+                 d == core, d == far[-1]) for d in ds], ["ident", res])
     lin(128, T.yo[0:48, :], ps[7][0:48, 0:128], (), ["yo"], bank=7)
     dma(24576 + ROWS * 3 // 8, T.y[:, :], T.yo[0:48, :], "dy", ["yo"], ["y"])
     op("Y", None, 0, ["y"], ())

import math
import numpy as np
from concourse.bass import DstId, RemoteDMATransfer
from concourse.mybir import AluOpType as A, ActivationFunctionType as F

CFG = {"piece": 2, "merge": {"V": 4, "A": 6}, "delta": 300.0, "early": 3, "lat0": 3600.0, "lat": 3100.0, "gap": 1000.0, "latn": 2600.0,
       "latf": 3600.0, "gat": 1.62, "pe": 0.7, "bw": 350.0, "tries": 60000, "heat": 120.0, "seed": 1, "dma": 1100.0, "call": 350.0,
       "call0": 1650.0, "mean": 0.1, "when": 2, "d2": 60.0, "rep": 4, "p1a": [[0], [1], [2]], "p1": [[0], [1], [2]], "split": 1, "stagger": 1, "pq": "A", "hi": "V"}
G1 = [[0], [1, 2]]
ROWS = 98000
CASES = ((0.7, 1.0, 1.0, 1.0, 1.0, 0.83), (0.57, 0.8, 0.85, 0.85, 0.85, 0.8), (1.2, 1.4, 1.4, 1.3, 1.5, 1.1))
WEIGHTS = (0.5, 0.3, 0.2)
WAKE, FIX = 100.0, 42.0
FOUND = {}
NQ = 3
B, H, W32, I32 = "bfloat16", "float16", "float32", "int32"
SCRATCH = {n: ("sbuf", [128, c], d) for n, c, d in (
    ("img", 8320, B), ("win", 4112, B), ("posei", 8, I32), ("p8", 8, W32), ("pa", 8, W32), ("kc", 16, W32), ("hs", 4, W32),
    ("lc", 256, I32), ("v0", 256, I32), ("tab", 768, B), ("dj", 32, I32), ("wp", 144, B),
    ("ones", 128, W32), ("rep", 128, W32), ("onesb", 128, B), ("ident", 128, B), ("ig0", 128, B), ("ig1", 128, B), ("ig2", 128, B),
    ("sel", 192, B), ("lt", 48, B), ("lm", 256, B), ("cm", 192, B), ("s0", 384, B), ("ru", 384, B), ("wd", 144, B),
    ("sb1", 16, B), ("sb2", 32, B), ("sb3", 16, B), ("cr", 448, W32), ("ct", 384, W32), ("xi", 384, I32),
    ("off", 960, "uint16"), ("gb", 15360, B), ("tf", 576, W32), ("tb", 768, B), ("tz", 1440, B), ("mt", 384, B), ("x1", 384, B),
    ("raw", 4096, B), ("r16", 128, B), ("xc", 48, B), ("sh", 384, H), ("fs", 384, H), ("x2", 384, H), ("rl", 96, H), ("yo", 128, W32))}
for _b in range(8):
    SCRATCH["ps%d" % _b] = ("psum", [128, 512], "float32")
SEMAPHORES = ["cV", "cA", "cP", "cG", "dpose", "dlens", "dimg", "dtab", "draw", "dy", "loc", "s", "fa", "fb"] + \
    [n + str(q) for n in ("xa", "xb", "r") for q in range(NQ)]

LAST = 8319.0
ROUND = 191.5 + 1.0 / 8192
BASE = 64.0 * 65 - 160
CYC = 1.04


def mask_of(engs):
    m = 0
    for e in engs:
        m |= 1 << e
    return m


def helpers(core, T, topo):
    far = [d for d in T.cores if d != core and not topo.may_write(core, d)]
    can = [c for c in topo.cores_of(core) if T.rank_of(c) is None and all(topo.may_write(c, d) for d in far)]
    first = [c for c in can if topo.die(c) == topo.die(core)][0]
    second = [c for c in can if topo.die(c) != topo.die(core)][0]
    return far, [first, second]


def dst_id(topo, d, s):
    rid, pid = topo.addr(d, s)
    return DstId(rid=rid, pnc=pid)


def part(buf, qs, r):
    return buf[:, 16 * (NQ * r + qs[0]):16 * (NQ * r + qs[-1] + 1)]


def group(groups, q):
    return [x for x in groups if q in x][0]


def helper_program(g, core, owner, far, i, T, topo):
    r = T.rank_of(owner)
    engs = topo.engines(core, far[0])
    half = len(engs) // 2
    n_in = len(topo.engines(owner, core)) // 2
    steps = [("r%d" % qs[-1], "xb%d" % qs[-1], [part(T.x1, qs, r)] * 2, part(T.x1, qs, r)) for qs in G1]
    steps.append(("s", "fb", [T.rl[:, 0:48], T.rl[:, 48:96]], part(T.x2, range(NQ), r)))
    for came, sem, src, dst in steps:
        g.wait_ge(T.sem[came], 2 * n_in if came == "s" and CFG["stagger"] else n_in)
        g.remote_dma_fused([RemoteDMATransfer(dst_ids=[dst_id(topo, d, core)], dma_engine_mask=mask_of(engs[j * half:(j + 1) * half]),
                                              remote_sem=T.sem[sem], src=src[j], dst=dst)
                            for j, d in enumerate(far[2 * i:2 * i + 2])], local_sem=T.sem.loc)
    g.wait_ge(T.sem.loc, len(steps) * len(engs))


def lengths(ops, case):
    cost = [(o["cost"] - 60) * case[0] + FIX if o["gat"] else o["cost"] * case[1] if o["eng"] == "P" else
            (o["cost"] - 60) * case[5] + FIX if o["eng"] in ("V", "A", "VA") else o["cost"] for o in ops]
    late = [o["late"] * case[4 if o["bytes"] < 0 else 2] if o["eng"] is None else o["late"] for o in ops]
    return cost, late, [max(0, o["bytes"]) * case[3] / CFG["bw"] for o in ops]


def plan(ops, pre, succ, prio, size):
    cost, late, load = size
    n = len(ops)
    left = [0] * n
    for s in succ:
        for j, _ in s:
            left[j] += 1
    free, at, eng, order, line = {}, [0.0] * n, [o["eng"] for o in ops], [], 0.0
    ready = [i for i in range(n) if left[i] == 0]
    while ready:
        cand = []
        for i in ready:
            for e in (("A", "V") if eng[i] == "VA" else (eng[i],)):
                cand.append((max(at[i], free.get(e, 0.0)) if e else at[i], -prio[i], e, i))
        t0, _, e0, i0 = min(cand, key=lambda c: c[:2])
        if e0 is not None:
            d = CFG["delta"] if cost[i0] > 300 else CFG["d2"]
            t0, _, e0, i0 = min([c for c in cand if c[2] == e0 and c[0] <= t0 + d], key=lambda c: (c[1], c[0]))
        eng[i0] = e0
        t1 = free[e0] = t0 + cost[i0]
        if load[i0]:
            line = max(line, t1 + late[i0] * 0.6) + load[i0]
        fin = line + late[i0] * 0.4 if load[i0] else t1 + late[i0]
        order.append(i0)
        ready.remove(i0)
        for j, kind in succ[i0]:
            at[j] = max(at[j], t1 if kind else fin + 60)
            left[j] -= 1
            if left[j] == 0:
                ready.append(j)
    return order, eng


def quick(order, eng, succ, size, gat):
    cost, late, load = size
    n = len(eng)
    free, last, at, line, end = {"V": 0.0, "A": 0.0, "P": 0.0, "G": 0.0, "Y": 0.0}, {"V": None, "A": None}, [0.0] * n, 0.0, 0.0
    for i in order:
        e, t1 = eng[i], at[i]
        if e:
            f, c = free[e], cost[i]
            if e == "V" or e == "A":
                a, b = last[e], gat[i]
                if b and a and a[0] == b[0] and a[2] == b[1] and t1 < f - c:
                    f -= FIX
                last[e] = b
                if e == "A":
                    c += 15.0
            t1 = free[e] = (f if f > t1 else t1) + c
        if load[i]:
            line = max(line, t1 + late[i] * 0.6) + load[i]
            fin = line + late[i] * 0.4
        else:
            fin = t1 + late[i]
        if fin > end:
            end = fin
        fin += WAKE
        for j, kind in succ[i]:
            t = t1 if kind else fin
            if t > at[j]:
                at[j] = t
    return end + CFG["mean"] * sum(at) / n


def replay(order, eng, succ, size, gat, trace=None):
    cost, late, load = size
    n = len(eng)
    free, last, at, line, end = {e: 0.0 for e in "VAPGY"}, {"V": None, "A": None}, [0.0] * n, 0.0, 0.0
    why, before, start, final, lineby = [None] * n, {}, [0.0] * n, None, None
    for i in order:
        e, t1 = eng[i], at[i]
        if e:
            f = free[e]
            if e in last:
                a, b = last[e], gat[i]
                if a and b and a[0] == b[0] and a[2] == b[1] and t1 < f - cost[i]:
                    f -= FIX
                last[e] = b
            if f > t1:
                t1 = f
                if trace is not None:
                    why[i] = (before[e], True)
            if trace is not None:
                before[e], start[i] = i, max(t1, free[e])
            t1 += cost[i] + 15.0 if e == "A" else cost[i]
            free[e] = t1
        elif trace is not None:
            start[i] = t1
        if load[i]:
            if trace is not None:
                if line > t1 + late[i] * 0.6:
                    why[i] = (lineby, False)
                lineby = i
            line = max(line, t1 + late[i] * 0.6) + load[i]
            fin = line + late[i] * 0.4
        else:
            fin = t1 + late[i]
        if fin > end:
            end, final = fin, i
        fin += WAKE
        for j, kind in succ[i]:
            t = t1 if kind else fin
            if t > at[j]:
                at[j] = t
                if trace is not None:
                    why[j] = (i, False)
    if trace is not None:
        trace["start"], trace["held"] = start, []
        while why[final]:
            if why[final][1]:
                trace["held"].append((why[final][0], final))
            final = why[final][0]
    return end + CFG["mean"] * sum(at) / n


def schedule(ops):
    n = len(ops)
    succ = [[] for _ in range(n)]
    pre = []
    for i, o in enumerate(ops):
        pre.append(set(o["deps"]) | set(o["after"]))
        for j in pre[i]:
            succ[j].append((i, j not in o["deps"] or (o["eng"] == "P" and ops[j]["eng"] == "P")))
    below = [set() for _ in range(n)]
    for i in range(n - 1, -1, -1):
        for j, _ in succ[i]:
            below[i] |= below[j] | {j}
        far = set().union(*[below[j] for j, _ in succ[i]])
        succ[i] = [(j, kind) for j, kind in succ[i] if j not in far or ops[i]["late"]]
    sizes = [lengths(ops, c) for c in CASES]
    base = [0.0] * n
    for i in range(n - 1, -1, -1):
        base[i] = sizes[0][0][i] + sizes[0][1][i] + sizes[0][2][i] + 60 + max([base[j] for j, _ in succ[i]] + [0.0])

    if n not in FOUND:
        order, eng = plan(ops, pre, succ, base, sizes[0])
        gat = [o["gat"] for o in ops]
        value = lambda order, eng: sum(w * quick(order, eng, succ, s, gat) for w, s in zip(WEIGHTS, sizes))
        free = [i for i, o in enumerate(ops) if o["eng"] in ("V", "A", "VA", "P", "G")]
        now = value(order, eng)
        best = (now, order, eng)
        rng = np.random.RandomState(CFG["seed"])
        rand = rng.rand(CFG["tries"], 8).tolist()
        held = None
        for k, r in enumerate(rand):
            if held is None:
                trace = {}
                replay(order, eng, succ, sizes[0 if r[7] < 0.6 else 1 if r[7] < 0.8 else 2], gat, trace)
                order = sorted(order, key=lambda i: trace["start"][i])
                held = [(j, i) for j, i in trace["held"] if ops[i]["eng"] != "Y"]
            other, e2 = list(order), list(eng)
            if held and r[0] < 0.5:
                j, i = held[int(r[1] * len(held))]
                a = (i, j)[r[2] < 0.5]
                if order.index(j) > order.index(i):
                    continue
                if ops[a]["eng"] == "VA" and r[3] < 0.5:
                    e2[a] = "V" if eng[a] == "A" else "A"
                elif a == i:
                    pj, pi = other.index(j), other.index(i)
                    need = {i}
                    for x in other[pi - 1:pj - 1 if pj else None:-1]:
                        if any(y in need for y, _ in succ[x]):
                            need.add(x)
                    if j in need:
                        continue
                    mid = other[pj:pi + 1]
                    other[pj:pi + 1] = [x for x in mid if x in need] + [x for x in mid if x not in need]
                else:
                    pj, pi = other.index(j), min(n - 1, other.index(i) + int(r[4] * r[4] * 12))
                    need = {j}
                    for x in other[pj + 1:pi + 1]:
                        if pre[x] & need:
                            need.add(x)
                    mid = other[pj:pi + 1]
                    other[pj:pi + 1] = [x for x in mid if x not in need] + [x for x in mid if x in need]
            else:
                i = free[int(r[1] * len(free))]
                if ops[i]["eng"] == "VA" and r[2] < 0.4:
                    e2[i] = "V" if eng[i] == "A" else "A"
                p = other.index(i)
                lo, hi, reach = p, p, 1 + int(r[3] * 30)
                while lo > max(0, p - reach) and other[lo - 1] not in pre[i]:
                    lo -= 1
                while hi < min(n - 1, p + reach) and i not in pre[other[hi + 1]]:
                    hi += 1
                other.pop(p)
                other.insert(lo if r[4] < 0.2 else hi if r[4] > 0.8 else lo + int(r[5] * (hi + 1 - lo)), i)
            got = value(other, e2)
            if got <= now - CFG["heat"] * (1 - k / CFG["tries"]) * math.log(r[6] + 1e-12):
                now, order, eng = got, other, e2
                if r[5] < 0.25:
                    held = None
                if got < best[0]:
                    best = (got, other, e2)
        FOUND[n] = best
    for o, e in zip(ops, FOUND[n][2]):
        o["eng"] = e
    return list(FOUND[n][1])


def rank_program(g, core, T, topo):
    rank = T.rank_of(core)
    if rank is None:
        for owner in T.cores:
            if core in topo.cores_of(owner):
                far, hl = helpers(owner, T, topo)
                if core in hl:
                    helper_program(g, core, owner, far, hl.index(core), T, topo)
        return
    far, hl = helpers(core, T, topo)
    near = [d for d in T.cores if d != core and d not in far]
    out_e = topo.engines(core, near[0])
    in_e = [e for e in topo.engines(core, hl[0]) if e not in out_e]
    other = helpers(T.cores[0], T, topo)[0]
    half = [[r for r, d in enumerate(T.cores) if (d in other) == h] for h in (False, True)]
    dk, dh = half[0][1] - half[0][0], half[1][0] - half[0][0]
    assert half == [[h * dh + k * dk for k in range(4)] for h in range(2)]
    hfar = 1 if rank in half[0] else 0
    V, S, P, Y = g.vector, g.scalar, g.tensor, g.sync
    queue = {"V": V, "A": S, "P": P, "G": g, "Y": Y}
    ps = [T["ps%d" % b] for b in range(8)]

    ops, last_w, readers, last_q = [], {}, {}, {}

    def op(eng, fn, cost, r=(), w=(), bank=None, dma=None, arrive=None, late=0.0, nbytes=0, gat=None):
        i = len(ops)
        r, w = list(r), list(w)
        if bank is not None:
            (r if eng == "V" else w).append(("bank", bank))
        deps = set()
        for x in r:
            if x in last_w:
                deps.add(last_w[x])
        for x in w:
            if x in last_w:
                deps.add(last_w[x])
            deps.update(readers.get(x, []))
        for x in r:
            readers.setdefault(x, []).append(i)
        for x in w:
            last_w[x] = i
            readers[x] = []
        after = []
        if eng == "Y" or dma == "remote":
            if eng in last_q:
                after.append(last_q[eng])
            last_q[eng] = i
        ops.append({"eng": eng, "fn": fn, "deps": deps, "dma": dma, "arrive": arrive, "cost": cost, "late": late, "bytes": nbytes,
                    "after": after, "gat": gat})

    def vc(n):
        return 60 + max(64, n) * CYC

    def ts(n, out, in0, s1, s2, o0, o1, r, w, bank=None):
        if o1 is None:
            op("V", lambda e: V.tensor_scalar(out, in0, s1, None, o0), vc(n), r, w, bank)
        else:
            op("V", lambda e: V.tensor_scalar(out, in0, s1, s2, o0, o1), vc(n), r, w, bank)

    def tt(n, out, a, b, o, r, w, bank=None):
        op("V", lambda e: V.tensor_tensor(out, a, b, o), vc(n if bank is not None else 2 * n), r, w, bank)

    def ms(n, ap, c, r, w):
        op("V", lambda e: V.memset(ap, c), vc(n // 2), r, w)

    def lin(n, out, a, r, w, scale=1.0, bias=0.0, bank=None, eng="VA"):
        op(eng, lambda e: S.activation(out, a, F.Identity, bias=bias, scale=scale) if e == "A" else
           V.tensor_scalar(out, a, scale, bias, A.mult, A.add), vc(n), r, w, bank)

    def mms(b, calls, r, four=False, least=64):
        op("P", lambda e: [P.matmul(*c[1:]) for c in calls][-1], sum(max(least, c[0]) for c in calls) * CFG["pe"] * (4 if four else 1),
           r, (), b)

    def iota(n, out, pat, base, cm, w, fl=True):
        if fl:
            op("G", lambda e: g.iota(out, pat, base, cm, allow_small_or_imprecise_dtypes=True), 130 + 2 * n * 0.87, (), w)
        else:
            op("G", lambda e: g.iota(out, pat, base, cm), 130 + 2 * n * 0.87, (), w)

    def sel(n, out, a, pat, cm, r, w, base=0, cmp=A.is_equal):
        op("G", lambda e: g.affine_select(out, a, pat, cmp, 0.0, base, cm), 170 + 2 * n * 0.87, r, w)

    def dma(nbytes, out, a, sem, r, w, eng="Y"):
        op(eng, lambda e: queue[e].dma_start(out, a), 60, r, w, None, sem, late=CFG["dma"], nbytes=nbytes)

    loc = [0]

    def send(trs, r, w):
        cost = CFG["call"] if loc[0] else CFG["call0"]
        loc[0] += sum(len(t[1]) for t in trs)
        calls = [RemoteDMATransfer(dst_ids=[dst_id(topo, d, core) for d in ds], dma_engine_mask=mask_of(es), remote_sem=T.sem[sm],
                                   srcs=[src], dsts=[dst] * len(ds)) for ds, es, sm, src, dst in trs]
        op("G", lambda e: g.remote_dma_fused(calls, local_sem=T.sem.loc), cost, r, w, None, "remote")

    nt = {"tf": 0, "tb": 0}

    def tmp(buf, w):
        nt[buf] += w
        return T[buf][:, nt[buf] - w:nt[buf]], buf + str(nt[buf])

    IMG = ["img%d" % k for k in range(8)] + ["imgz0", "imgz1"] + [("imgr", j) for j in range(CFG["rep"])]
    WIN = ["win0", "win1", "win2"]

    def pieces(u0, u1):
        return [range(a, min(u1, a + CFG["piece"])) for a in range(u0, u1, CFG["piece"])]

    def offs(st, q):
        return T.off[:, 192 * st + 64 * q:192 * st + 64 * q + 64], [("off", st, u) for u in range(8 * q, 8 * q + 8)]

    def gb(st, q, c0, c1, step=1):
        a = 3072 * st + 1024 * q
        return T.gb[:, a + c0:a + c1:step] if step > 1 else T.gb[:, a + c0:a + c1]

    def got(st, q):
        return [("g", st, u) for u in range(8 * q, 8 * q + 8)]

    def gather_call(eng, st, u0, u1):
        w = T.win[:, 0:4112] if st in (0, 2) else T.img[:, 0:8320]
        src = w.indirect(T.off[:, 192 * st + 8 * u0:192 * st + 8 * u1])
        out = gb(st, 0, 128 * u0, 128 * u1)
        return V.tensor_copy(out, src) if eng == "V" else S.activation(out, src, F.Identity)

    def gather(st, u0, u1):
        for us in pieces(u0, u1):
            op("VA", None, 60 + 128 * len(us) * CFG["gat"], (WIN if st in (0, 2) else IMG) + [("off", st, u) for u in us],
               [("g", st, u) for u in us], gat=[st, us[0], us[-1] + 1])

    NP = 8192 - 512 * CFG["rep"]

    def img_load(k):
        dma(32 * NP, T.img[16 * k:16 * k + 16, 64:64 + NP], T.cam[:, 0:NP], "dimg", (), ["img%d" % k])

    kc = lambda j: T.kc[:, j:j + 1]
    pa = lambda j: T.pa[:, j:j + 1]
    s0 = lambda q, e=None: T.s0[0:16, 128 * q:128 * q + 128] if e is None else T.s0[0:16, 128 * q + e:128 * q + 128:2]
    sh = lambda q, e=None: T.sh[0:16, 128 * q:128 * q + 128] if e is None else T.sh[0:16, 128 * q + e:128 * q + 128:2]
    lm = lambda e: T.lm[0:16, 128 * e:128 * e + 128]
    zero = T.wp[0:16, 16:144]

    dma(192, T.posei[0:8, 0:6], T.pose[:, :], "dpose", (), ["posei"], CFG["pq"])
    dma(131072 + ROWS, T.lc[:, :], T.lens[:, :], "dlens", (), ["lc"])
    if CFG["rep"]:
        dma(32 * (8192 - NP), T.raw[0:16, 0:8192 - NP], T.cam[:, NP:8192], "draw", (), ["raw"])
    for k in range(CFG["early"]):
        img_load(k)
    iota(16, T.dj[:, 0:16], [[1, 16]], 128, -1, ["dj"], False)
    iota(128, T.ones[:, :], [[0, 128]], 1, 0, ["ones"])
    sel(128, T.rep[0:8, :], T.ones[0:8, :], [[1, 8], [0, 16]], -1, ["ones"], ["rep"])
    iota(128, T.onesb[:, :], [[0, 128]], 1, 0, ["onesb"])
    sel(128, T.ident[:, :], T.onesb[:, :], [[-1, 128]], 1, ["onesb"], ["ident"])
    s0n = lambda q: "s0a" if q == 0 else "s0b"
    for qs in ([0], [1, 2]):
        for q in qs:
            for h in range(2):
                iota(64, T.s0[0:16, 128 * q + 64 * h:128 * q + 64 * h + 64], [[48 * dk, 4], [8, 2], [0, 8]], 16 * q + 48 * dh * h, 0, [("s0y", q, h)])
        iota(128 * len(qs), T.s0[0:8, 128 * qs[0]:128 * (qs[-1] + 1)], [[0, 16 * len(qs)], [64, 8]], 0, 8,
             [s0n(qs[0])] + [("s0y", q, h) for q in qs for h in range(2)])
        if qs[0] == 0:
            if CFG["rep"]:
                sel(128, T.r16[0:16, :], T.onesb[0:16, :], [[0, 8], [1, 16]], -1, ["onesb"], ["r16"])
            sel(64, T.sel[:, 0:64], T.onesb[:, 0:64], [[-1, 8], [-16, 8]], 1, ["onesb"], ["sel1"])
    sel(8, T.sb1[:, 0:16:2], T.onesb[:, 0:8], [[-16, 8]], 1, ["onesb"], [("sb1", 0)], cmp=A.is_ge)
    iota(8, T.sb1[:, 1:16:2], [[0, 8]], 64, 0, [("sb1", 1)])
    sel(8, T.sb1[:, 0:16:2], T.sb1[:, 0:16:2], [[16, 8]], -1, (), [("sb1", 0)], base=1, cmp=A.is_ge)
    sel(8, T.sb1[:, 1:16:2], T.sb1[:, 1:16:2], [[-16, 8]], 1, (), [("sb1", 1)], base=-2)
    iota(27, T.sb2[:, 0:27], [[0, 27]], 1, 0, ["sb2"])
    iota(128, zero, [[0, 128]], 0, 0, ["wp"])
    iota(9, T.sb2[:, 0:27:3], [[0, 9]], -16, 0, ["sb2"])
    sel(27, T.sb2[:, 0:27], T.sb2[:, 0:27], [[-16, 9], [-1, 3]], 1, (), ["sb2"], base=1)
    iota(64, T.img[:, 0:64], [[0, 64]], 0, 0, ["imgz0"])
    iota(64, T.img[:, 8256:8320], [[0, 64]], 0, 0, ["imgz1"])
    for q in range(NQ):
        for e in range(2):
            iota(64, T.ru[0:16, 128 * q + 64 * e:128 * q + 64 * e + 64], [[0, 8], [48 * dh, 2], [48 * dk, 4]], 16 * q + 8 * e, 0, [("ruy", q, e)])
        iota(128, T.ru[0:8, 128 * q:128 * q + 128], [[0, 2], [8, 8], [0, 8]], 0, 64, [("ru", q), ("ruy", q, 0), ("ruy", q, 1)])
    sel(128, T.sel[:, 64:192], T.onesb[:, :], [[-16, 8], [-1, 8], [0, 2]], 1, ["onesb"], ["sel2"])
    iota(16, T.wd[:, 128:144], [[0, 16]], 0, 0, ["wd0"])

    ms(1040, T.win[:, 0:1040], 64.0, (), ["wina"])
    ms(1008, T.win[:, 1040:2048], 64.0, (), ["winb"])
    ms(1024, T.win[:, 2048:3072], 64.0, (), ["winc"])
    lin(1040, T.win[:, 3072:4112], T.win[:, 0:1040], ["wina"], ["wind"], eng="A")
    ts(6, T.p8[0:8, 0:6], T.posei[0:8, 0:6], 1.0 / 32, None, A.mult, None, ["posei"], ["p8"])
    mms(7, [(6, ps[7][:, 0:6], T.rep[0:8, :], T.p8[0:8, 0:6], True, True)], ["rep", "p8"], True)
    lin(6, T.pa[:, 0:6], ps[7][:, 0:6], (), ["pa"], bank=7)
    lin(1, T.hs[:, 0:1], pa(4), ["pa"], ["hs"], scale=1.0 / 128)
    lin(256, T.tab[:, 0:256], T.lc[:, :], ["lc"], ["tab0"], eng=CFG["hi"])
    tt(256, T.tab[:, 256:512], T.lc[:, :], T.tab[:, 0:256], A.subtract, ["lc", "tab0"], ["tab1"])
    ts(256, T.v0[:, :], T.lc[:, :], T.hs[:, 0:1], -0.5 + 1.0 / 8192, A.mult, A.add, ["lc", "hs"], ["v0"])
    ts(256, T.tab[:, 512:768], T.v0[:, :], -65.0, 64.0, A.max, A.min, ["v0"], ["tab2"])
    for t in ((0, 1, 2) if CFG["hi"] == "V" else (0, 2, 1)):
        dma(65536 + ROWS, T.win[t:128:16, 1:4097], T.tab[:, 256 * t:256 * t + 256], "dtab",
            ["tab%d" % t, "wina", "winb", "winc", "wind"], ["win%d" % t])
    for k in range(CFG["early"], 8):
        img_load(k)

    ts(16, T.dj[:, 16:32], T.dj[:, 0:16], 15, None, A.bitwise_and, None, ["dj"], ["dj2"])
    ts(16, T.wp[:, 0:16], T.dj[:, 16:32], 0.0, None, A.is_equal, None, ["dj2"], ["d16b"])
    for ch in range(2):
        lin(1, kc(ch), pa(1 - ch), ["pa"], ["k%d" % ch], scale=8.0 * ch - 4.0)
    for e in range(2):
        for ch in range(2):
            a = 16 * e + 8 * ch
            lin(8, T.lt[:, a:a + 8], T.wp[:, 8 * e:8 * e + 8], ["d16b", "k%d" % ch], [("lt", e, ch)], scale=kc(ch))
    mms(6, [(128, ps[6][0:16, 128 * e:128 * e + 128], T.lt[:, 16 * e:16 * e + 16], T.ident[:, :], True, True) for e in range(2)],
        ["ident"] + [("lt", e, ch) for e in range(2) for ch in range(2)])
    lin(256, T.lm[0:16, :], ps[6][0:16, 0:256], (), ["lm"], bank=6)
    lin(1, kc(3), pa(3), ["pa"], ["k3"], scale=4.0, bias=1.0 - 3.5 / 8)
    for b, qs in ((3, [0]), (6, [1, 2])):
        mms(b, [(64, ps[b][:, 256 + 64 * q:320 + 64 * q], lm(e), s0(q, e), e == 0, e == 1) for q in qs for e in range(2)],
            ["lm", s0n(qs[0])])
        a, n = 64 * qs[0], 64 * len(qs)
        ts(n, T.off[:, a:a + n], ps[b][:, 256 + a:256 + a + n], kc(3), 4097.0, A.add, A.min, ["k3"],
           [x for q in qs for x in offs(0, q)[1]], b)

    for j in range(CFG["rep"]):
        mms(j % 2, [(512, ps[j % 2][:, :], T.r16[0:16, :], T.raw[0:16, 512 * j:512 * j + 512], True, True)], ["r16", "raw"])
        lin(512, T.img[:, 64 + NP + 512 * j:576 + NP + 512 * j], ps[j % 2][:, :], (), [("imgr", j)], bank=j % 2)
    for ch in range(2):
        lin(8, T.lt[:, 32 + 8 * ch:40 + 8 * ch], T.wp[:, 0:8], ["d16b", "pa"], [("lx", ch)], scale=pa(ch))
    mms(4, [(64, ps[4][0:16, 0:64], T.lt[:, 32:48], T.sel[:, 0:64], True, True)], ["sel1", ("lx", 0), ("lx", 1)])
    lin(64, T.cm[0:16, 0:64], ps[4][0:16, 0:64], (), ["cm1"], bank=4)
    lin(64, T.cr[:, 0:64], T.sel[:, 0:64], ["sel1", "pa"], ["cr0"], scale=pa(2))
    mms(5, [c for q in range(NQ) for c in ((256, ps[5][:, 64 * q:64 * q + 64], T.ones[:, :], T.cr[:, 0:64], True, False),
                                           (64, ps[5][:, 64 * q:64 * q + 64], s0(q), T.cm[0:16, 0:64], False, True))],
        ["ones", "cr0", "cm1", "s0a", "s0b"])
    ts(192, T.xi[:, 0:192], ps[5][:, 0:192], -15.5 / 32, None, A.add, None, (), ["xi"], 5)
    lin(128, T.ig0[:, :], T.ident[:, :], ["ident"], ["idg0"], scale=16384.0)
    lin(128, T.ig1[:, :], T.ident[:, :], ["ident"], ["idg1"], scale=-16384.0)
    lin(1, kc(4), pa(3), ["pa"], ["k4"], scale=-4.0)
    lin(1, kc(5), pa(3), ["pa"], ["k5"], scale=-4.0, bias=0.875)
    lin(1, kc(6), pa(5), ["pa", "k4"], ["k6"], scale=-32.0, bias=kc(4))
    lin(1, kc(7), pa(5), ["pa", "k5"], ["k7"], scale=32.0, bias=kc(5))

    def second_constants(when):
        mms(6, [(64, ps[6][0:16, 64 * j:64 * j + 64], T.lt[:, 32 - 32 * j:48 - 32 * j], T.sel[:, 64:192:2], True, True) for j in range(2)],
            ["sel2", ("lx", 0), ("lx", 1), ("lt", 0, 0), ("lt", 0, 1)])
        lin(128, T.cm[0:16, 64:192], ps[6][0:16, 0:128], [when], ["cm"], bank=6)
        lin(1, kc(2), pa(2), ["pa", when], ["k2"], bias=-15.5 / 32)
        ts(1, kc(10), T.dj[:, 31:32], 0.0, -16.0, A.is_equal, A.mult, ["dj2", when], ["k10"])
        for j, k in enumerate((2, 6, 7)):
            lin(128, T.cr[:, 64 + 128 * j:192 + 128 * j], T.sel[:, 64:192], ["sel2", "k%d" % k, when], [("cr", j)], scale=kc(k))
        mms(7, [(384, ps[7][:, 0:384], T.ones[:, :], T.cr[:, 64:448], True, True)], ["ones"] + [("cr", j) for j in range(3)], True)
        lin(384, T.ct[:, :], ps[7][:, 0:384], (), ["ct"], bank=7)
        for t in range(2):
            lin(8, T.sb3[:, 8 * t:8 * t + 8], T.sb1[:, t:16:2], [("sb1", t), when], [("sb3", t)])
        lin(128, T.wd[:, 0:128], T.ident[:, :], ["ident", "k10", when], ["wd"], scale=kc(10))
        lin(128, T.ig2[:, :], T.ident[:, :], ["ident", when], ["idg2"], scale=2.0 ** 27)
        ms(720, T.tz[:, 0:720], 0.0, [when], ["tz"])

    for qs in CFG["p1a"]:
        n, q0, q = len(qs), qs[0], qs[-1]
        w, bm, bu = 64 * n, q0, 3 + q0
        (p, pn), (v, vn), (u, un), (c, cn) = [tmp(b, w) for b in ("tf", "tb", "tb", "tb")]
        for x in qs:
            gather(0, 8 * x, 8 * x + 8)
            a = 128 * (x - q0)
            mms(bm, [(16, ps[bm][:, a + 16 * r:a + 16 * r + 16], gb(0, x, r, 1024, 8), T.sb1[:, :], True, True) for r in range(8)],
                got(0, x) + [("sb1", 0), ("sb1", 1)])
        tt(w, p, ps[bm][:, 0:2 * w:2], T.xi[:, 64 * q0:64 * q0 + w], A.mult, ["xi"], [pn], bm)
        lin(w, v, ps[bm][:, 1:2 * w:2], [pn], [vn], bank=bm)
        ts(w, u, p, 1.0 / 4096, ROUND, A.mult, A.add, [pn], [un])
        ts(w // 2, c, u, 160.0, 223.0, A.max, A.min, [un], [cn])
        s = ps[bu][:, 0:w]
        mms(bu, [(w, s, T.ident[:, :], v, True, False)], ["ident", vn])
        mms(bu, [(w, s, T.ig0[:, :], u, False, False)], ["idg0", un])
        mms(bu, [(w, s, T.ig1[:, :], c, False, False), (w, s, T.ident[:, :], c, False, True)], ["idg1", "ident", cn])
        ts(w, T.off[:, 192 + 64 * q0:192 + 64 * q0 + w], s, BASE, LAST, A.add, A.min, (), [y for x in qs for y in offs(1, x)[1]], bu)
    for qs in CFG["p1"]:
        n, q0, q = len(qs), qs[0], qs[-1]
        w, bu = 64 * n, 3 + q0
        (d, dn), (m, mn) = tmp("tf", w), tmp("tb", w)
        z = ps[bu][:, 2:3 * w:3]
        mms(bu, [(3 * w, ps[bu][:, 0:3 * w], zero, T.s0[0:16, 0:3 * w], True, False)]
            + [(64, ps[bu][:, 192 * (x - q0) + 2:192 * (x - q0 + 1):3], lm(e), T.ru[0:16, 128 * x + 64 * e:128 * x + 64 * e + 64], False, False)
               for x in qs for e in range(2)], ["wp", "lm", "s0a", "s0b"] + [("ru", x) for x in qs])
        gather(1, 8 * q0, 8 * q + 8)
        for us in pieces(0, 8 * n):
            mms(bu, [(24, ps[bu][:, 24 * r:24 * r + 24], gb(1, q0, 128 * r, 128 * r + 128), T.sb2[:, 1:25], False, r == 8 * n - 1) for r in us],
                [("g", 1, 8 * q0 + r) for r in us] + ["sb2"])
        ts(w, d, z, kc(6), kc(7), A.max, A.min, ["k6", "k7"], [dn], bu)
        tt(w, m, z, d, A.is_equal, [dn], [mn], bu)
        for x in qs:
            a = nt["tb"] - w + 64 * (x - q0)
            for ch in range(2):
                tt(64, T.mt[:, 128 * x + 64 * ch:128 * x + 64 * ch + 64], ps[bu][:, 192 * (x - q0) + ch:192 * (x - q0 + 1):3], T.tb[:, a:a + 64],
                   A.mult, [mn], [("mt", x, ch)], bu)
        mms(bu, [(16, ps[bu][:, 384 + 16 * (x - q0):400 + 16 * (x - q0)], T.mt[:, 128 * x:128 * x + 128], T.wp[:, 0:16], True, True) for x in qs],
            ["d16b"] + [("mt", x, ch) for x in qs for ch in range(2)])
        lin(16 * n, part(T.x1, qs, rank), ps[bu][:, 384:384 + 16 * n], (), [("x1own", x) for x in qs], bank=bu)
        if CFG["when"] in qs:
            second_constants(("x1own", q))
        qs = group(G1, q)
        if q != qs[-1]:
            continue
        piece, own = part(T.x1, qs, rank), [("x1own", x) for x in qs]
        direct = (near, out_e, "xa%d" % q, piece, piece)
        if qs[0] == 0:
            send([([hl[0]], in_e, "r%d" % q, piece, piece), ([hl[1]], out_e, "r%d" % q, piece, piece)], own, [("sent", q)])
            send([direct], own, [("sentn", q)])
        else:
            send([(hl, in_e, "r%d" % q, piece, piece), direct], own, [("sent", q), ("sentn", q)])
        op(None, None, 0, [("sent", q)], [("way", q)], late=CFG["lat0"] if qs[0] == 0 else CFG["lat"], nbytes=-1 if qs[0] == 0 else 0)
        op(None, None, 0, [("way", q), ("x1in", qs[0] - 1)], [("x1in", q)], late=CFG["gap"], arrive=("xb%d" % q, len(far) * (len(out_e) // 2)))
        op(None, None, 0, [("sentn", q)], [("x1near", q)], late=CFG["latn"], arrive=("xa%d" % q, len(near) * len(out_e)))

    def share(src, dst):
        ds = [d for d in T.cores if d != src and topo.may_write(src, d)]
        n = len(out_e) // 2
        return [out_e, out_e[:n], out_e[n:]][ds.index(dst)]

    bank_of = lambda h, k: 6 if h != hfar else 0 if k > 1 and CFG["stagger"] else 5

    def heights(h, k, q, a):
        b = bank_of(h, k)
        return (16, ps[b][:, 48 * k + q:48 * k + 48:3], gb(4, 0, a, a - a % 2 + 256, 2), T.wp[:, 0:16], True, True)

    for qs, bb, bs, bz in (([0], 7, 0, 0), ([1, 2], 1, 3, 4)):
        n, q0 = len(qs), qs[0]
        w, ba = 64 * n, 3 * q0
        for ds, res in (([core] + near, [("x1near", qs[-1])] + [("x1own", x) for x in qs]), (far, [("x1in", qs[-1])])):
            mms(ba, [(16 * n, ps[ba][:, 128:128 + 16 * n], T.ident[:, :], part(T.x1, qs, T.rank_of(d)), d == core, d == far[-1]) for d in ds],
                ["ident"] + res)
        ts(16 * n, T.xc[:, 16 * q0:16 * (q0 + n)], ps[ba][:, 128:128 + 16 * n], -31.0, 31.0, A.max, A.min, (), [("xc", q0)], ba)
        for q in qs:
            b = ba + q - q0
            mms(b, [(16, ps[b][0:16, 16 * c:16 * c + 16], T.ident[:, c:128:8], T.xc[:, 16 * q:16 * q + 16], True, True) for c in range(8)],
                ["ident", ("xc", q0)], least=20)
            tt(128, sh(q), ps[b][0:16, 0:128], s0(q), A.add, [s0n(q)], [("sh", q)], b)
            mms(b, [(64, ps[b][:, 256:320], lm(e), sh(q, e), e == 0, e == 1) for e in range(2)], ["lm", ("sh", q)])
            o, on = offs(2, q)
            ts(64, o, ps[b][:, 256:320], kc(3), 4097.0, A.add, A.min, ["k3"], on, b)
            gather(2, 8 * q, 8 * q + 8)
        shn = [("sh", q) for q in qs]
        ct = lambda j: T.ct[:, 128 * j:128 * j + 128:2 // n]
        mms(bb, [(64, ps[bb][:, 256 + q - q0:256 + w:n], sh(q), T.cm[0:16, 64:128], True, True) for q in qs], ["cm"] + shn)
        x = T.xi[:, 192 + 64 * q0:192 + 64 * q0 + w]
        tt(w, x, ps[bb][:, 256:256 + w], ct(0), A.add, ["ct"], [("x", q0)], bb)
        for q in qs:
            mms(bb, [(16, ps[bb][:, n * r + q - q0:2 * w:8 * n], gb(2, q, r, 1024, 8), T.sb3[:, :], True, True) for r in range(8)],
                got(2, q) + [("sb3", 0), ("sb3", 1)])
        c0 = lambda j: 144 * j + 720 * q0
        tile = lambda j: T.tz[:, c0(j) + 2 - n:c0(j) + 130 - n:2 // n]
        tn = lambda j: ("tz", q0, j)
        p, pn = T.tf[:, 384 + 64 * q0:384 + 64 * q0 + w], ("p", q0)
        tt(w, p, ps[bb][:, 0:w], x, A.mult, [("x", q0)], [pn], bb)
        lin(w, tile(0), ps[bb][:, w:2 * w], [pn, "tz"], [tn(0)], bank=bb)
        ts(w, tile(1), p, 1.0 / 4096, ROUND, A.mult, A.add, [pn, "tz"], [tn(1)])
        ts(w // 2, tile(2), tile(1), 160.0, 223.0, A.max, A.min, [tn(1), "tz"], [tn(2)])

        def turned(b, terms, start, stop):
            calls = []
            for j, m, mn in terms:
                for e in range(2 // n):
                    calls.append((w, ps[b][:, 0:w], T.tz[:, c0(j) + 2 - n - e:c0(j) + 130 - n - e], m[:, w * e:w * e + w],
                                  start and not calls, False))
            calls[-1] = calls[-1][:5] + (stop,)
            mms(b, calls, [x for j, m, mn in terms for x in (tn(j), mn)])

        if n == 1:
            mms(bs, [(w, ps[bs][:, 0:w], T.ident[:, :], tile(j), j == 0, j == 1) for j in range(2)], ["ident", tn(0), tn(1)])
        else:
            turned(bs, [(0, T.ident, "ident")], True, False)
            turned(bs, [(1, T.ident, "ident")], False, True)
        on = lambda st: [x for q in qs for x in offs(st, q)[1]]
        ts(w, T.off[:, 576 + 64 * q0:576 + 64 * q0 + w], ps[bs][:, 0:w], BASE, LAST, A.add, A.min, (), on(3), bs)
        if n == 1:
            z = ps[bz][:, 0:w]
            mms(bz, [(64, z, sh(0), T.cm[0:16, 128:192], True, False)], ["cm"] + shn)
            turned(bb, [(0, T.ident, "ident")], True, False)
            turned(bb, [(1, T.ig0, "idg0")], False, False)
            turned(bb, [(2, T.ig1, "idg1"), (2, T.ident, "ident")], False, False)
            gather(3, 0, 8)
            mms(bz, [(64, z, T.wd[:, 15 - k:143 - k], gb(3, 0, k, 1024, 16), False, k == 15) for k in range(16)], ["wd", "wd0"] + got(3, 0))
            for j, cmp in ((1, A.is_lt), (2, A.is_gt)):
                tt(w, tile(2 + j), z, ct(j), cmp, ["ct", "tz"], [tn(2 + j)], bz)
                turned(bb, [(2 + j, T.ig2, "idg2")], False, j == 2)
            ts(w, T.off[:, 768:832], ps[bb][:, 0:w], BASE, LAST, A.add, A.min, (), on(4), bb)
            gather(4, 0, 8)
            for k in range(4):
                for h in (hfar, 1 - hfar):
                    mms(bank_of(h, k), [heights(h, k, 0, 256 * k + h)], ["d16b", ("g", 4, 2 * k), ("g", 4, 2 * k + 1)])
            continue
        cuts = [(64 * h, 64 * h + 64) for h in (hfar, 1 - hfar)] if CFG["split"] else [(0, 128)]
        for (lo, hi), bz, bo in zip(cuts, (4, 2), (1, 3)):
            m, us = hi - lo, range(8 + lo // 8, 8 + hi // 8)
            z = ps[bz][lo:hi, 0:128]

            def add(terms, start, stop):
                mms(bo, [(m, ps[bo][:, 0:m], T.tz[lo:hi, c0(j):c0(j) + 128], x[lo:hi, lo:hi], start and i == 0, stop and i == len(terms) - 1)
                         for i, (j, x, xn, tj) in enumerate(terms)], [y for t in terms for y in t[2:]])

            mms(bz, [(128, z, T.wp[0:16, 16:16 + m], s0(0), True, False)]
                + [(64, ps[bz][lo:hi, q - q0:128:2], T.sh[0:16, 128 * q + lo:128 * q + hi], T.cm[0:16, 128:192], False, False) for q in qs],
                ["cm", "wp"] + shn)
            add([(0, T.ident, "ident", tn(0)), (1, T.ig0, "idg0", tn(1))], True, False)
            add([(2, T.ig1, "idg1", tn(2)), (2, T.ident, "ident", tn(2))], False, False)
            gather(3, us[0], us[-1] + 1)
            mms(bz, [(8, ps[bz][lo:hi, k:128:16], gb(3, 1, 16 * lo + k, 16 * hi, 16), T.sb2[:, 3:25:3], False, k == 15) for k in range(16)],
                ["sb2"] + [("g", 3, u) for u in us])
            for j, cmp in ((1, A.is_lt), (2, A.is_gt)):
                tt(128, T.tz[lo:hi, c0(2 + j):c0(2 + j) + 128], z, T.ct[lo:hi, 128 * j:128 * j + 128], cmp, ["ct"], [("ne", lo, j)], bz)
                add([(2 + j, T.ig2, "idg2", ("ne", lo, j))], False, j == 2)
            ts(m, T.off[:, 832 + lo:832 + hi], ps[bo][:, 0:m], BASE, LAST, A.add, A.min, (), [("off", 4, u) for u in us], bo)
        for h in (hfar, 1 - hfar):
            a = 0 if h == hfar else 192
            gather(4, 8 + 8 * h, 16 + 8 * h)
            for k in range(4):
                mms(bank_of(h, k), [heights(h, k, 1 + j, 1024 + 1024 * h + 256 * k + j) for j in range(2)],
                    ["d16b", ("g", 4, 8 + 8 * h + 2 * k), ("g", 4, 9 + 8 * h + 2 * k)])
            if h == hfar and CFG["stagger"]:
                for i in range(2):
                    b = bank_of(h, 2 * i)
                    ts(96, T.fs[:, 96 * i:96 * i + 96], ps[b][:, 96 * i:96 * i + 96], 1.0, None, A.mult, None, (), [("fs", i)], b)
                    send([([hl[i]], in_e + out_e, "s", T.fs[:, 96 * i:96 * i + 96], T.rl[:, :])], [("fs", i)], [("fsent", i)])
                op(None, None, 0, [("fsent", 1)], ["fb"], late=CFG["latf"] - 300, arrive=("fb", len(far) * (len(out_e) // 2)))
                continue
            b = bank_of(h, 0)
            ts(192, T.fs[:, a:a + 192], ps[b][:, 0:192], 1.0, None, A.mult, None, (), [("fs", a)], b)
            if h == hfar:
                send([([hl[i]], es, "s", T.fs[:, 96 * i:96 * i + 96], T.rl[:, :]) for i, es in enumerate((in_e, out_e))], [("fs", a)], ["fsent"])
                op(None, None, 0, ["fsent"], ["fb"], late=CFG["latf"], arrive=("fb", len(far) * (len(out_e) // 2)))
            else:
                trs = [([T.cores[r]], share(core, T.cores[r]), "fa", T.fs[:, a + 48 * k:a + 48 * k + 48], part(T.x2, range(NQ), rank))
                       for k, r in enumerate(half[h]) if r != rank]
                send(trs[:1], [("fs", a)], ["nsent1"])
                send(trs[1:], [("fs", a)], ["nsent"])
                op(None, None, 0, ["nsent"], ["fa"], late=CFG["latn"], arrive=("fa", sum(len(share(d, core)) for d in near)))

    a = 192 + 48 * half[1 - hfar].index(rank)
    for ds, res in (([core], ("fs", 192)), (near, "fa"), (far, "fb")):
        mms(7, [(128, ps[7][0:48, 0:128], T.fs[:, a:a + 48] if d == core else part(T.x2, range(NQ), T.rank_of(d)), T.ident[:, :],
                 d == core, d == far[-1]) for d in ds], ["ident", res])
    lin(128, T.yo[0:48, :], ps[7][0:48, 0:128], (), ["yo"], bank=7)
    dma(24576 + ROWS * 3 // 8, T.y[:, :], T.yo[0:48, :], "dy", ["yo"], ["y"])
    op("Y", None, 0, ["y"], ())

    order = schedule(ops)
    first = {i: k for k, i in enumerate(order)}
    into, prev = {}, {}
    for i in order:
        o, j = ops[i], prev.get(ops[i]["eng"])
        a = ops[j]["gat"] if j is not None else None
        b = o["gat"]
        if a and b and a[0] == b[0] and a[2] == b[1] and b[2] - a[1] <= CFG["merge"][o["eng"]] and \
                all(first[d] < first[j] for d in o["deps"]):
            a[2] = b[2]
            ops[j]["deps"] = ops[j]["deps"] | o["deps"]
            into[i] = j
        else:
            prev[o["eng"]] = i
    order = [i for i in order if i not in into]
    pos = {i: k for k, i in enumerate(order)}

    def live(o):
        ds = set(into.get(j, j) for j in o["deps"])
        return [j for j in ds if not (o["eng"] == "P" and ops[j]["eng"] == "P") and ops[j]["dma"] != "remote"]

    needed = set()
    for i in order:
        best = {}
        for j in (live(ops[i]) if ops[i]["eng"] else []):
            e = ops[j]["eng"]
            if ops[j]["dma"] is None and ops[j]["arrive"] is None and (e not in best or pos[j] > pos[best[e]]):
                best[e] = j
        needed.update(best.values())
    total, token, count = {}, {}, {}
    for o in ops:
        if o["dma"] not in (None, "remote"):
            total[o["dma"]] = total.get(o["dma"], 0) + 16
    for i in order:
        o = ops[i]
        if o["arrive"] is not None:
            token[i] = o["arrive"]
        elif o["dma"] is not None:
            token[i] = (o["dma"], total.get(o["dma"], 0))
        elif i in needed:
            count[o["eng"]] = count.get(o["eng"], 0) + 1
            token[i] = ("c" + o["eng"], count[o["eng"]])
    waited = {}
    for i in order:
        o = ops[i]
        if o["eng"] is None:
            continue
        want = {}
        for j in live(o):
            if j in token:
                sm, v = token[j]
                want[sm] = max(want.get(sm, 0), v)
        for sm, v in sorted(want.items()):
            if waited.get((o["eng"], sm), 0) < v:
                queue[o["eng"]].wait_ge(T.sem[sm], v)
                waited[(o["eng"], sm)] = v
        if o["gat"]:
            ins = gather_call(o["eng"], o["gat"][0], o["gat"][1], o["gat"][2])
        elif o["fn"] is None:
            continue
        else:
            ins = o["fn"](o["eng"])
        if o["dma"] not in (None, "remote"):
            ins.then_inc(T.sem[o["dma"]], 16)
        elif i in needed:
            ins.then_inc(T.sem["c" + o["eng"]], 1)
    g.wait_ge(T.sem.loc, loc[0])
